import numpy as np
import ml_dtypes


def mxq(x, axis, fmt="e4m3"):
    dtype, down = {"e4m3": (ml_dtypes.float8_e4m3fn, 7), "e5m2": (ml_dtypes.float8_e5m2, 14)}[fmt]
    v = np.moveaxis(np.asarray(x, np.float32).astype(ml_dtypes.bfloat16).astype(np.float64), axis, -1)
    blocks = v.reshape(v.shape[:-1] + (-1, 32))
    amax = np.abs(blocks).max(-1, keepdims=True)
    byte = np.maximum(np.where(amax > 0, np.frexp(amax)[1] - 1 + 127, 0) - down, 1)
    scale = np.exp2(byte - 127.0)
    codes = (blocks / scale).astype(np.float32).astype(dtype).astype(np.float64)
    return np.moveaxis((codes * scale).reshape(v.shape), -1, axis)


WIDE = False


def mx_kscale(k):
    if not WIDE:
        return np.ones(k)
    levels = np.array([10, -10, 5, -5, 0])
    if k % 512:
        return np.exp2(np.random.permutation(np.resize(levels, k // 32))).repeat(32)
    a = np.empty((k // 512, 16))
    for p in range(k // 512):
        a[p, :8] = np.random.permutation(np.resize(levels, 8))
        for g in range(8):
            far = levels[np.abs(levels - a[p, g]) >= 10]
            a[p, g + 8] = far[np.random.randint(len(far))]
    return np.exp2(a.ravel()).repeat(32)


def f64(x):
    return np.asarray(x).astype(np.float64)


def striped(idx):
    return np.tile(idx.reshape(-1, 16).T, (8, 1)).astype(np.uint16)


def unstriped(offs):
    return offs[:16].T.reshape(-1).astype(np.int64)


E2M1 = np.array([0.0, 0.5, 1.0, 1.5, 2.0, 3.0, 4.0, 6.0, -0.0, -0.5, -1.0, -1.5, -2.0, -3.0, -4.0, -6.0])


def pack_weight(w, fmt):
    k, n = w.shape
    w = f64(np.asarray(w, np.float32).astype(ml_dtypes.bfloat16)).reshape(k // 32, 32, n)
    amax = np.abs(w).max(1)
    if fmt == "e4m3":
        byte = np.frexp(amax)[1] - 1 + 127 - 7
    else:
        mant, ex = np.frexp(amax / 6.0)
        byte = np.where(mant > 0.5, ex, ex - 1) + 127
    byte = np.clip(np.where(amax > 0, byte, 1), 1, 254)
    scaled = (w * np.exp2(127.0 - byte)[:, None, :]).reshape(k, n).astype(np.float32)
    by_word = np.ascontiguousarray(scaled.reshape(k // 512, 128, 4, n).transpose(0, 1, 3, 2))
    if fmt == "e4m3":
        words = by_word.astype(ml_dtypes.float8_e4m3fn).view(np.uint8)
    else:
        c = by_word.astype(ml_dtypes.float4_e2m1fn).view(np.uint8) & 0xF
        words = (c[..., 0::2] | (c[..., 1::2] << 4)).reshape(k // 512, 128, 2 * n)
    return np.ascontiguousarray(words), np.ascontiguousarray(byte.astype(np.uint8).reshape(k // 512, 16, n))


def unpack_weight(words, scales, fmt):
    g, _, n = scales.shape
    words = np.ascontiguousarray(words).reshape(g, 128, n, -1)
    if fmt == "e4m3":
        vals = words.view(ml_dtypes.float8_e4m3fn).astype(np.float64)
    else:
        nib = np.empty((g, 128, n, 4), np.uint8)
        nib[..., 0::2] = words & 0xF
        nib[..., 1::2] = words >> 4
        vals = E2M1[nib]
    vals = vals * np.repeat(np.exp2(scales.astype(np.float64) - 127.0), 8, axis=1)[..., None]
    return vals.transpose(0, 1, 3, 2).reshape(g * 512, n)


def gelu(v):
    return 0.5 * v * (1.0 + np.tanh(np.sqrt(2.0 / np.pi) * (v + 0.044715 * v**3)))


K, T, E, C, N = 1536, 640, 20, 128, 256
TOP = 4


def by_expert(wq, xq):
    return np.concatenate([wq[e].T @ xq[:, e * C:(e + 1) * C] for e in range(E)], axis=1)


def setup_inputs():
    n = np.random.standard_normal
    s = mx_kscale(K)[:, None]
    deal = np.repeat(np.arange(E), C).reshape(TOP, T)[:, np.random.permutation(T)]
    deal = np.take_along_axis(deal, np.argsort(np.random.rand(TOP, T), axis=0), axis=0)
    for _ in range(8):
        s_, t_ = np.random.permutation(T).reshape(2, -1); r = np.random.randint(TOP, size=T // 2); x, y = deal[r, s_].copy(), deal[r, t_].copy()
        ok = ~((deal[:, s_] == y).any(0) | (deal[:, t_] == x).any(0)); deal[r[ok], s_[ok]] = y[ok]; deal[r[ok], t_[ok]] = x[ok]
    order = np.lexsort((np.random.rand(TOP * T), deal.reshape(-1)))
    slot_token = order % T; pos = np.empty(TOP * T, np.int64); pos[order] = np.arange(TOP * T); pos = pos.reshape(TOP, T)
    g = np.random.uniform(0.5, 1.5, (TOP, T)); g = g / g.sum(0)
    x = pack_weight(n((K, T)) * s, "e4m3")
    return {
        "x_words": x[0],
        "x_scales": x[1],
        "w": (n((E, K, N)) / np.sqrt(K) / s[None]).astype(np.float32),
        "b": (0.3 * n((N, E))).astype(np.float32),
        "gate": np.stack([np.tile(r, (N, 1)) for r in g]).astype(np.float32),
        "offs": striped(slot_token),
        "pos1": striped(pos[0]),
        "pos2": striped(pos[1]),
        "pos3": striped(pos[2]),
        "pos4": striped(pos[3]),
    }


def reference(x_words, x_scales, w, b, gate, offs, pos1, pos2, pos3, pos4):
    idx = unstriped(offs)
    xq = unpack_weight(x_words, x_scales, "e4m3")[:, idx]
    y = by_expert(mxq(f64(w), 1, "e4m3"), xq)
    y = gelu(y + np.repeat(f64(b), C, axis=1))
    return sum(f64(gate[r]) * y[:, unstriped(p)] for r, p in enumerate((pos1, pos2, pos3, pos4)))

@@ -1,0 +1,191 @@
+from contextlib import ExitStack
+
+import concourse.mybir as mybir
+
+K, T, E, C, N = 1536, 640, 20, 128, 256
+TOP = 4
+FLOPS = 2 * E * C * K * N
+
+F32 = mybir.dt.float32
+BF16 = mybir.dt.bfloat16
+I32 = mybir.dt.int32
+U32 = mybir.dt.uint32
+U16 = mybir.dt.uint16
+U8 = mybir.dt.uint8
+FP8X4 = mybir.dt.float8_e4m3fn_x4
+GELU = mybir.ActivationFunctionType.Gelu_apprx_tanh
+MULT = mybir.AluOpType.mult
+ADD = mybir.AluOpType.add
+
+P = 128
+PACK = 4
+K_PASS = P * PACK
+PASSES = K // K_PASS
+HALVES = N // P
+GROUP = 2
+RAW_BUFS = 6
+RING = 12
+
+
+def tile_moe_pkd_lin_gelu_kernel(
+    tc, x_words, x_scales, w, b, gate, offs, pos1, pos2, pos3, pos4, out
+):
+    nc = tc.nc
+    with ExitStack() as ctx:
+        keep = ctx.enter_context(tc.tile_pool(name="keep", bufs=1))
+        stream = ctx.enter_context(tc.tile_pool(name="stream", bufs=RAW_BUFS))
+        work = ctx.enter_context(tc.tile_pool(name="work", bufs=3))
+        ring = ctx.enter_context(tc.tile_pool(name="ring", bufs=1))
+        psum = ctx.enter_context(tc.psum_pool(name="psum", bufs=6))
+
+        token_scales = keep.tile([P, T], U8, name="token_scales")
+        nc.gpsimd.memset(token_scales[:].bitcast(I32), 0)
+        for q in range(4):
+            nc.scalar.dma_start(
+                token_scales[32 * q : 32 * q + 4 * PASSES, :].bitcast(I32),
+                x_scales[:, 4 * q : 4 * q + 4, :].bitcast(I32),
+            )
+        bias = keep.tile([P, HALVES, 24], F32, name="bias")
+        nc.scalar.dma_start(bias[:, :, 0:E], b.rearrange("(h p) e -> p h e", p=P))
+
+        slot_list = keep.tile([P, E * C // 16], U16, name="slot_list")
+        token_words = [keep.tile([P, T], I32, name="token_words%d" % o) for o in range(PASSES)]
+
+        def load_token_words(o):
+            nc.sync.dma_start(token_words[o][:], x_words[o].rearrange("p t r -> p (t r)").bitcast(I32))
+
+        w_rows = w.rearrange("e k n -> (e k) n")
+        raw = {}
+
+        def load_w(first, count, one_dma):
+            chunk = stream.tile([P, count, PACK, N], F32, name="chunk", tag="stream")
+            src = w_rows[first * K_PASS : (first + count) * K_PASS, :].rearrange("(o p j) n -> p o (j n)", p=P, j=PACK)
+            dst = chunk[:].rearrange("p o j n -> p o (j n)")
+            if one_dma:
+                nc.sync.dma_start(dst, src)
+            else:
+                for i in range(count):
+                    nc.sync.dma_start(dst[:, i, :], src[:, i, :])
+            for i in range(count):
+                raw[divmod(first + i, PASSES)] = chunk[:, i, :, :]
+
+        slot_words = {}
+        slot_scales = {}
+
+        def gather(g, sort, pool, tag):
+            cols = slot_list[:, g * GROUP * C // 16 : (g + 1) * GROUP * C // 16]
+            if sort == PASSES:
+                slot_scales[g] = pool.tile([P, GROUP * C], U8, name="slot_scales", tag=tag, align_bytes=64)
+                nc.vector.tensor_copy(slot_scales[g][:], token_scales[:].indirect(cols))
+            else:
+                slot_words[g, sort] = pool.tile([P, GROUP * C], U32, name="slot_words", tag=tag, align_bytes=64)
+                nc.vector.tensor_copy(slot_words[g, sort][:], token_words[sort][:].bitcast(U32).indirect(cols))
+
+        def interleave(copy, dst, src):
+            copy(
+                dst.rearrange("p (c i) t -> p c t i", i=4),
+                src.rearrange("p t (c i) -> p c t i", i=4),
+            )
+
+        y = [keep.tile([P, E * C], F32, name="y%d" % h) for h in range(HALVES)]
+        w_codes = {}
+        w_scales = {}
+        acc = {}
+
+        def quantize(e, passes, cols, side):
+            nc.vector.quantize_mx(
+                out=w_codes[e][:, passes, cols].rearrange("p o n -> p (o n)").bitcast(FP8X4),
+                scales=w_scales[e][:, passes, cols].rearrange("p o n -> p (o n)"),
+                in_=side.rearrange("p o n t -> p (o n t)"),
+            )
+
+        def multiply(e, h, o):
+            g, j = divmod(e, GROUP)
+            mine = slice(j * C, (j + 1) * C)
+            cols = slice(h * P, (h + 1) * P)
+            nc.tensor.matmul_mx(
+                out=acc[e, h][:],
+                lhsT=w_codes[e][:, o, cols].bitcast(FP8X4),
+                lhsT_scale=w_scales[e][:, o, cols],
+                rhs=slot_words[g, o][:, mine].bitcast(FP8X4),
+                rhs_scale=slot_scales[g][4 * o : P, mine],
+                start=(o == 0),
+                stop=(o == PASSES - 1),
+            )
+
+        def activate(e, h):
+            nc.scalar.activation(y[h][:, e * C : (e + 1) * C], acc[e, h][:], GELU, bias=bias[:, h, e : e + 1])
+
+        def begin_expert(e):
+            w_codes[e] = work.tile([P, PASSES, N], U32, name="w_codes", align_bytes=64)
+            w_scales[e] = work.tile([P, PASSES, N], U8, name="w_scales", align_bytes=64)
+            side = work.tile([P, 2, N, PACK], BF16, name="side_s", align_bytes=64)
+            if e < E - 1:
+                for o in range(2):
+                    interleave(nc.scalar.copy, side[:, o, :, :], raw[e, o])
+                quantize(e, slice(0, 2), slice(0, N), side[:])
+            else:
+                interleave(nc.scalar.copy, side[:, 0, :, :], raw[e, 0])
+                quantize(e, slice(0, 1), slice(0, N), side[:, 0:1, :, :])
+                interleave(nc.vector.tensor_copy, side[:, 1, :, :], raw[e, 1])
+                quantize(e, slice(1, 2), slice(0, N), side[:, 1:2, :, :])
+            for h in range(HALVES):
+                acc[e, h] = psum.tile([P, C], F32, name="acc")
+                for o in range(2):
+                    multiply(e, h, o)
+
+        def end_expert(e):
+            last = slice(PASSES - 1, PASSES)
+            tags = ["ring%d" % ((HALVES * e + h) % RING) for h in range(HALVES)]
+            sides = []
+            for h in range(HALVES):
+                copy = nc.scalar.copy if (e == E - 1 and h == 1) else nc.vector.tensor_copy
+                sides.append(ring.tile([P, 1, P, PACK], BF16, name="side_v", tag=tags[h], align_bytes=64))
+                interleave(copy, sides[h][:, 0, :, :], raw[e, 2][:, :, h * P : (h + 1) * P])
+            for h in range(HALVES):
+                quantize(e, last, slice(h * P, (h + 1) * P), sides[h][:])
+                multiply(e, h, 2)
+                activate(e, h)
+            g = e // GROUP + 1
+            if g < E // GROUP:
+                for h in range(HALVES):
+                    gather(g, ((PASSES, 0), (1, 2))[e % GROUP][h], ring, tags[h])
+
+        nc.sync.dma_start(slot_list[:], offs)
+        load_token_words(0)
+        load_w(0, 2, False)
+        load_token_words(1)
+        load_token_words(2)
+        for sort in (0, PASSES, 1, 2):
+            gather(0, sort, keep, "first%d" % sort)
+        begin_expert(0)
+        for e in range(1, E):
+            load_w(PASSES * e - 1, PASSES, e < E - 1)
+            end_expert(e - 1)
+            begin_expert(e)
+        load_w(PASSES * E - 1, 1, True)
+        end_expert(E - 1)
+
+        back = []
+        for r, pos in enumerate((pos1, pos2, pos3, pos4)):
+            back.append(keep.tile([P, T // 16], U16, name="back%d" % r))
+            nc.sync.dma_start(back[r][:], pos)
+
+        for h in range(HALVES):
+            rows = slice(h * P, (h + 1) * P)
+            gates = stream.tile([P, TOP, T], F32, name="gates", tag="stream")
+            for r in range(TOP):
+                nc.sync.dma_start(gates[:, r, :], gate[r, rows, :])
+            part = []
+            for r in range(TOP):
+                part.append(keep.tile([P, T], F32, name="part%d_%d" % (h, r)))
+                nc.vector.tensor_tensor(part[r][:], y[h][:].indirect(back[r][:]), gates[:, r, :], MULT)
+            s01 = keep.tile([P, T], F32, name="s01_%d" % h)
+            s23 = keep.tile([P, T], F32, name="s23_%d" % h)
+            total = keep.tile([P, T], F32, name="total%d" % h)
+            nc.vector.tensor_tensor(s01[:], part[0][:], part[1][:], ADD)
+            nc.vector.tensor_tensor(s23[:], s01[:], part[2][:], ADD)
+            for c0 in range(0, T, T // 2):
+                cols = slice(c0, c0 + T // 2)
+                nc.vector.tensor_tensor(total[:, cols], s23[:, cols], part[3][:, cols], ADD)
+                nc.sync.dma_start(out[rows, cols], total[:, cols])

@@ -1,6 +1,7 @@
 from contextlib import ExitStack
 
 import concourse.mybir as mybir
+from concourse.masks import make_identity
 
 K, T, E, C, N = 1536, 640, 20, 128, 256
 TOP = 4
@@ -36,7 +37,7 @@ def tile_moe_pkd_lin_gelu_kernel(
         stream = ctx.enter_context(tc.tile_pool(name="stream", bufs=RAW_BUFS))
         work = ctx.enter_context(tc.tile_pool(name="work", bufs=3))
         ring = ctx.enter_context(tc.tile_pool(name="ring", bufs=1))
-        psum = ctx.enter_context(tc.psum_pool(name="psum", bufs=6))
+        psum = ctx.enter_context(tc.psum_pool(name="psum", bufs=8))
 
         token_scales = keep.tile([P, T], U8, name="token_scales")
         nc.gpsimd.memset(token_scales[:].bitcast(I32), 0)
@@ -67,7 +68,11 @@ def tile_moe_pkd_lin_gelu_kernel(
                 for i in range(count):
                     nc.sync.dma_start(dst[:, i, :], src[:, i, :])
             for i in range(count):
-                raw[divmod(first + i, PASSES)] = chunk[:, i, :, :]
+                raw[divmod(first + i, PASSES)] = (chunk, i)
+
+        def raw_passes(e, o, count, cols):
+            chunk, i = raw[e, o]
+            return chunk[:, i : i + count, :, cols]
 
         slot_words = {}
         slot_scales = {}
@@ -83,8 +88,8 @@ def tile_moe_pkd_lin_gelu_kernel(
 
         def interleave(copy, dst, src):
             copy(
-                dst.rearrange("p (c i) t -> p c t i", i=4),
-                src.rearrange("p t (c i) -> p c t i", i=4),
+                dst.rearrange("p o (c i) t -> p o c t i", i=2),
+                src.rearrange("p o t (c i) -> p o c t i", i=2),
             )
 
         y = [keep.tile([P, E * C], F32, name="y%d" % h) for h in range(HALVES)]
@@ -120,17 +125,17 @@ def tile_moe_pkd_lin_gelu_kernel(
             w_codes[e] = work.tile([P, PASSES, N], U32, name="w_codes", align_bytes=64)
             w_scales[e] = work.tile([P, PASSES, N], U8, name="w_scales", align_bytes=64)
             side = work.tile([P, 2, N, PACK], BF16, name="side_s", align_bytes=64)
+            every = slice(0, N)
             if e < E - 1:
-                for o in range(2):
-                    interleave(nc.scalar.copy, side[:, o, :, :], raw[e, o])
-                quantize(e, slice(0, 2), slice(0, N), side[:])
+                interleave(nc.scalar.copy, side[:], raw_passes(e, 0, 2, every))
+                quantize(e, slice(0, 2), every, side[:])
             else:
-                interleave(nc.scalar.copy, side[:, 0, :, :], raw[e, 0])
-                quantize(e, slice(0, 1), slice(0, N), side[:, 0:1, :, :])
-                interleave(nc.vector.tensor_copy, side[:, 1, :, :], raw[e, 1])
+                interleave(nc.scalar.copy, side[:, 0:1, :, :], raw_passes(e, 0, 1, every))
+                quantize(e, slice(0, 1), every, side[:, 0:1, :, :])
+                interleave(nc.vector.tensor_copy, side[:, 1:2, :, :], raw_passes(e, 1, 1, every))
                 quantize(e, slice(1, 2), slice(0, N), side[:, 1:2, :, :])
             for h in range(HALVES):
-                acc[e, h] = psum.tile([P, C], F32, name="acc")
+                acc[e, h] = psum.tile([P, C], F32, name="acc", tag="bank")
                 for o in range(2):
                     multiply(e, h, o)
 
@@ -141,7 +146,7 @@ def tile_moe_pkd_lin_gelu_kernel(
             for h in range(HALVES):
                 copy = nc.scalar.copy if (e == E - 1 and h == 1) else nc.vector.tensor_copy
                 sides.append(ring.tile([P, 1, P, PACK], BF16, name="side_v", tag=tags[h], align_bytes=64))
-                interleave(copy, sides[h][:, 0, :, :], raw[e, 2][:, :, h * P : (h + 1) * P])
+                interleave(copy, sides[h][:], raw_passes(e, 2, 1, slice(h * P, (h + 1) * P)))
             for h in range(HALVES):
                 quantize(e, last, slice(h * P, (h + 1) * P), sides[h][:])
                 multiply(e, h, 2)
@@ -171,21 +176,47 @@ def tile_moe_pkd_lin_gelu_kernel(
             back.append(keep.tile([P, T // 16], U16, name="back%d" % r))
             nc.sync.dma_start(back[r][:], pos)
 
+        identity = keep.tile([P, P], F32, name="identity")
+        make_identity(nc, identity[:])
+        blocks = T // P
+        pieces = (slice(0, 3 * P), slice(3 * P, T))
         for h in range(HALVES):
             rows = slice(h * P, (h + 1) * P)
             gates = stream.tile([P, TOP, T], F32, name="gates", tag="stream")
             for r in range(TOP):
                 nc.sync.dma_start(gates[:, r, :], gate[r, rows, :])
-            part = []
-            for r in range(TOP):
-                part.append(keep.tile([P, T], F32, name="part%d_%d" % (h, r)))
-                nc.vector.tensor_tensor(part[r][:], y[h][:].indirect(back[r][:]), gates[:, r, :], MULT)
-            s01 = keep.tile([P, T], F32, name="s01_%d" % h)
-            s23 = keep.tile([P, T], F32, name="s23_%d" % h)
+            summed = TOP if h < HALVES - 1 else TOP - 1
+            turned = [psum.tile([P, P], F32, name="turned", tag="bank") for c in range(blocks)]
+            for r in range(summed):
+                part = keep.tile([P, T], F32, name="part%d_%d" % (h, r))
+                nc.vector.tensor_tensor(part[:], y[h][:].indirect(back[r][:]), gates[:, r, :], MULT)
+                for c in range(blocks):
+                    nc.tensor.matmul(
+                        turned[c][:],
+                        lhsT=part[:, c * P : (c + 1) * P],
+                        rhs=identity[:],
+                        start=(r == 0),
+                        stop=(r == summed - 1),
+                        is_transpose=True,
+                    )
+            by_token = keep.tile([P, blocks, P], F32, name="by_token%d" % h)
             total = keep.tile([P, T], F32, name="total%d" % h)
-            nc.vector.tensor_tensor(s01[:], part[0][:], part[1][:], ADD)
-            nc.vector.tensor_tensor(s23[:], s01[:], part[2][:], ADD)
-            for c0 in range(0, T, T // 2):
-                cols = slice(c0, c0 + T // 2)
-                nc.vector.tensor_tensor(total[:, cols], s23[:, cols], part[3][:, cols], ADD)
-                nc.sync.dma_start(out[rows, cols], total[:, cols])
+            sums = []
+            for cols in pieces:
+                sums.append(psum.tile([P, cols.stop - cols.start], F32, name="sums", tag="bank"))
+                for c in range(cols.start // P, cols.stop // P):
+                    nc.scalar.copy(by_token[:, c, :], turned[c][:])
+                    at = c * P - cols.start
+                    nc.tensor.transpose(sums[-1][:, at : at + P], by_token[:, c, :], identity[:])
+            if summed == TOP:
+                for cols, bank in zip(pieces, sums):
+                    nc.scalar.copy(total[:, cols], bank[:])
+                nc.sync.dma_start(out[rows, :], total[:])
+            else:
+                part = keep.tile([P, T], F32, name="part_last")
+                for cols in pieces:
+                    picks = back[TOP - 1][:, cols.start // 16 : cols.stop // 16]
+                    nc.vector.tensor_tensor(part[:, cols], y[h][:].indirect(picks), gates[:, TOP - 1, cols], MULT)
+                for cols, bank in zip(pieces, sums):
+                    nc.vector.tensor_tensor(total[:, cols], bank[:], part[:, cols], ADD)
+                    nc.sync.dma_start(out[rows, cols], total[:, cols])

@@ -26,6 +26,7 @@ HALVES = N // P
 GROUP = 2
 RAW_BUFS = 6
 RING = 12
+SHARE = 64
 
 
 def tile_moe_pkd_lin_gelu_kernel(
@@ -144,9 +145,12 @@ def tile_moe_pkd_lin_gelu_kernel(
             tags = ["ring%d" % ((HALVES * e + h) % RING) for h in range(HALVES)]
             sides = []
             for h in range(HALVES):
-                copy = nc.scalar.copy if (e == E - 1 and h == 1) else nc.vector.tensor_copy
                 sides.append(ring.tile([P, 1, P, PACK], BF16, name="side_v", tag=tags[h], align_bytes=64))
-                interleave(copy, sides[h][:], raw_passes(e, 2, 1, slice(h * P, (h + 1) * P)))
+            cut = SHARE if e < E - 1 else 0
+            interleave(nc.vector.tensor_copy, sides[0][:], raw_passes(e, 2, 1, slice(0, P)))
+            if cut > 0:
+                interleave(nc.vector.tensor_copy, sides[1][:, :, 0:cut, :], raw_passes(e, 2, 1, slice(P, P + cut)))
+            interleave(nc.scalar.copy, sides[1][:, :, cut:P, :], raw_passes(e, 2, 1, slice(P + cut, N)))
             for h in range(HALVES):
                 quantize(e, last, slice(h * P, (h + 1) * P), sides[h][:])
                 multiply(e, h, 2)
@@ -189,16 +193,18 @@ def tile_moe_pkd_lin_gelu_kernel(
             turned = [psum.tile([P, P], F32, name="turned", tag="bank") for c in range(blocks)]
             for r in range(summed):
                 part = keep.tile([P, T], F32, name="part%d_%d" % (h, r))
-                nc.vector.tensor_tensor(part[:], y[h][:].indirect(back[r][:]), gates[:, r, :], MULT)
-                for c in range(blocks):
-                    nc.tensor.matmul(
-                        turned[c][:],
-                        lhsT=part[:, c * P : (c + 1) * P],
-                        rhs=identity[:],
-                        start=(r == 0),
-                        stop=(r == summed - 1),
-                        is_transpose=True,
-                    )
+                for cols in pieces if (h, r) == (HALVES - 1, summed - 1) else (slice(0, T),):
+                    picks = back[r][:, cols.start // 16 : cols.stop // 16]
+                    nc.vector.tensor_tensor(part[:, cols], y[h][:].indirect(picks), gates[:, r, cols], MULT)
+                    for c in range(cols.start // P, cols.stop // P):
+                        nc.tensor.matmul(
+                            turned[c][:],
+                            lhsT=part[:, c * P : (c + 1) * P],
+                            rhs=identity[:],
+                            start=(r == 0),
+                            stop=(r == summed - 1),
+                            is_transpose=True,
+                        )
             by_token = keep.tile([P, blocks, P], F32, name="by_token%d" % h)
             total = keep.tile([P, T], F32, name="total%d" % h)
             sums = []

@@ -23,9 +23,9 @@ PACK = 4
 K_PASS = P * PACK
 PASSES = K // K_PASS
 HALVES = N // P
-GROUP = 2
+GROUP = 4
+CUT = 256
 RAW_BUFS = 6
-RING = 12
 SHARE = 64
 
 
@@ -79,13 +79,24 @@ def tile_moe_pkd_lin_gelu_kernel(
         slot_scales = {}
 
         def gather(g, sort, pool, tag):
-            cols = slot_list[:, g * GROUP * C // 16 : (g + 1) * GROUP * C // 16]
             if sort == PASSES:
-                slot_scales[g] = pool.tile([P, GROUP * C], U8, name="slot_scales", tag=tag, align_bytes=64)
-                nc.vector.tensor_copy(slot_scales[g][:], token_scales[:].indirect(cols))
+                dst = pool.tile([P, GROUP * C], U8, name="slot_scales", tag=tag, align_bytes=64)
+                slot_scales[g] = dst
+                window = token_scales[:]
             else:
-                slot_words[g, sort] = pool.tile([P, GROUP * C], U32, name="slot_words", tag=tag, align_bytes=64)
-                nc.vector.tensor_copy(slot_words[g, sort][:], token_words[sort][:].bitcast(U32).indirect(cols))
+                dst = pool.tile([P, GROUP * C], U32, name="slot_words", tag=tag, align_bytes=64)
+                slot_words[g, sort] = dst
+                window = token_words[sort][:].bitcast(U32)
+            for at in range(0, GROUP * C, CUT):
+                first = g * GROUP * C + at
+                cols = slot_list[:, first // 16 : (first + CUT) // 16]
+                nc.vector.tensor_copy(dst[:, at : at + CUT], window.indirect(cols))
+
+        order = (0, PASSES, 1, 2)
+        later = [(g, sort) for g in range(1, E // GROUP) for sort in order]
+        places = [(e, h) for e in range(E) for h in range(HALVES) if h == 0 or e % 2 == 0]
+        paced = dict(zip(places, later))
+        busy = max(e for e, h in paced)
 
         def interleave(copy, dst, src):
             copy(
@@ -142,30 +153,32 @@ def tile_moe_pkd_lin_gelu_kernel(
 
         def end_expert(e):
             last = slice(PASSES - 1, PASSES)
-            tags = ["ring%d" % ((HALVES * e + h) % RING) for h in range(HALVES)]
             sides = []
             for h in range(HALVES):
-                sides.append(ring.tile([P, 1, P, PACK], BF16, name="side_v", tag=tags[h], align_bytes=64))
-            cut = SHARE if e < E - 1 else 0
+                if (e, h) in paced:
+                    sides.append(ring.tile([P, 1, P, PACK], BF16, name="side_p", tag="pace%d_%d" % (e, h), align_bytes=64))
+                else:
+                    sides.append(work.tile([P, 1, P, PACK], BF16, name="side_v", tag="side_v%d" % h, align_bytes=64))
+            cut = SHARE if e <= busy else P if e < E - 1 else 0
             interleave(nc.vector.tensor_copy, sides[0][:], raw_passes(e, 2, 1, slice(0, P)))
             if cut > 0:
                 interleave(nc.vector.tensor_copy, sides[1][:, :, 0:cut, :], raw_passes(e, 2, 1, slice(P, P + cut)))
-            interleave(nc.scalar.copy, sides[1][:, :, cut:P, :], raw_passes(e, 2, 1, slice(P + cut, N)))
+            if cut < P:
+                interleave(nc.scalar.copy, sides[1][:, :, cut:P, :], raw_passes(e, 2, 1, slice(P + cut, N)))
             for h in range(HALVES):
                 quantize(e, last, slice(h * P, (h + 1) * P), sides[h][:])
                 multiply(e, h, 2)
                 activate(e, h)
-            g = e // GROUP + 1
-            if g < E // GROUP:
-                for h in range(HALVES):
-                    gather(g, ((PASSES, 0), (1, 2))[e % GROUP][h], ring, tags[h])
+            for h in range(HALVES):
+                if (e, h) in paced:
+                    gather(paced[e, h][0], paced[e, h][1], ring, "pace%d_%d" % (e, h))
 
         nc.sync.dma_start(slot_list[:], offs)
         load_token_words(0)
         load_w(0, 2, False)
         load_token_words(1)
         load_token_words(2)
-        for sort in (0, PASSES, 1, 2):
+        for sort in order:
             gather(0, sort, keep, "first%d" % sort)
         begin_expert(0)
         for e in range(1, E):

@@ -23,10 +23,15 @@ PACK = 4
 K_PASS = P * PACK
 PASSES = K // K_PASS
 HALVES = N // P
+BANK = 512
 GROUP = 4
-CUT = 256
+WINDOW = 704
 RAW_BUFS = 6
-SHARE = 64
+SHARE = 128
+SPLIT = 4
+WHOLE = E - SPLIT
+SHIFT = 1
+AHEAD = 6
 
 
 def tile_moe_pkd_lin_gelu_kernel(
@@ -40,26 +45,35 @@ def tile_moe_pkd_lin_gelu_kernel(
         ring = ctx.enter_context(tc.tile_pool(name="ring", bufs=1))
         psum = ctx.enter_context(tc.psum_pool(name="psum", bufs=8))
 
-        token_scales = keep.tile([P, T], U8, name="token_scales")
-        nc.gpsimd.memset(token_scales[:].bitcast(I32), 0)
+        token_scales = keep.tile([P, WINDOW], U8, name="token_scales")
+        blocks = T // P
+        gate_rows = keep.tile([P, P], F32, name="gate_rows")
+        nc.vector.memset(gate_rows[:], 0.0)
+        nc.vector.memset(token_scales[:].bitcast(I32), 0)
+        spaced = gate.rearrange("r n t -> (r n t)").rearrange("(q s) -> q s", q=TOP * blocks)
+        nc.scalar.dma_start(gate_rows[0 : TOP * blocks, :], spaced[:, 0:P])
         for q in range(4):
             nc.scalar.dma_start(
-                token_scales[32 * q : 32 * q + 4 * PASSES, :].bitcast(I32),
+                token_scales[32 * q : 32 * q + 4 * PASSES, 0:T].bitcast(I32),
                 x_scales[:, 4 * q : 4 * q + 4, :].bitcast(I32),
             )
         bias = keep.tile([P, HALVES, 24], F32, name="bias")
         nc.scalar.dma_start(bias[:, :, 0:E], b.rearrange("(h p) e -> p h e", p=P))
+        identity = keep.tile([P, P], F32, name="identity")
+        make_identity(nc, identity[:])
 
         slot_list = keep.tile([P, E * C // 16], U16, name="slot_list")
-        token_words = [keep.tile([P, T], I32, name="token_words%d" % o) for o in range(PASSES)]
+        token_words = [keep.tile([P, WINDOW], I32, name="token_words%d" % o) for o in range(PASSES)]
+        for o in range(PASSES):
+            nc.vector.memset(token_words[o][:, T:WINDOW], 0)
 
         def load_token_words(o):
-            nc.sync.dma_start(token_words[o][:], x_words[o].rearrange("p t r -> p (t r)").bitcast(I32))
+            nc.sync.dma_start(token_words[o][:, 0:T], x_words[o].rearrange("p t r -> p (t r)").bitcast(I32))
 
         w_rows = w.rearrange("e k n -> (e k) n")
         raw = {}
 
-        def load_w(first, count, one_dma):
+        def load_whole(first, count, one_dma):
             chunk = stream.tile([P, count, PACK, N], F32, name="chunk", tag="stream")
             src = w_rows[first * K_PASS : (first + count) * K_PASS, :].rearrange("(o p j) n -> p o (j n)", p=P, j=PACK)
             dst = chunk[:].rearrange("p o j n -> p o (j n)")
@@ -71,8 +85,18 @@ def tile_moe_pkd_lin_gelu_kernel(
             for i in range(count):
                 raw[divmod(first + i, PASSES)] = (chunk, i)
 
-        def raw_passes(e, o, count, cols):
-            chunk, i = raw[e, o]
+        def load_halves(h, which):
+            for e, o in which:
+                i = ((e - WHOLE) * PASSES + o + SHIFT * h) % (HALVES * PASSES)
+                if (e, o, h) not in raw:
+                    chunk = stream.tile([P, HALVES * PASSES, PACK, P], F32, name="chunk", tag="stream")
+                    for q in range(e * PASSES + o, min(e * PASSES + o + HALVES * PASSES - i, E * PASSES)):
+                        raw[divmod(q, PASSES) + (h,)] = (chunk, i + q - e * PASSES - o)
+                rows = w[e, o * K_PASS : (o + 1) * K_PASS, h * P : (h + 1) * P]
+                nc.sync.dma_start(raw[e, o, h][0][:, i, :, :], rows.rearrange("(p j) n -> p j n", j=PACK))
+
+        def raw_passes(key, count, cols):
+            chunk, i = raw[key]
             return chunk[:, i : i + count, :, cols]
 
         slot_words = {}
@@ -87,14 +111,12 @@ def tile_moe_pkd_lin_gelu_kernel(
                 dst = pool.tile([P, GROUP * C], U32, name="slot_words", tag=tag, align_bytes=64)
                 slot_words[g, sort] = dst
                 window = token_words[sort][:].bitcast(U32)
-            for at in range(0, GROUP * C, CUT):
-                first = g * GROUP * C + at
-                cols = slot_list[:, first // 16 : (first + CUT) // 16]
-                nc.vector.tensor_copy(dst[:, at : at + CUT], window.indirect(cols))
+            cols = slot_list[:, g * GROUP * C // 16 : (g + 1) * GROUP * C // 16]
+            nc.vector.tensor_copy(dst[:], window.indirect(cols))
 
-        order = (0, PASSES, 1, 2)
-        later = [(g, sort) for g in range(1, E // GROUP) for sort in order]
-        places = [(e, h) for e in range(E) for h in range(HALVES) if h == 0 or e % 2 == 0]
+        every_gather = [(g, sort) for g in range(E // GROUP) for sort in range(PASSES + 1)]
+        later = every_gather[AHEAD:]
+        places = [(e, h) for e in range(E) for h in range(HALVES) if h == 0 or e == 10]
         paced = dict(zip(places, later))
         busy = max(e for e, h in paced)
 
@@ -105,87 +127,127 @@ def tile_moe_pkd_lin_gelu_kernel(
             )
 
         y = [keep.tile([P, E * C], F32, name="y%d" % h) for h in range(HALVES)]
-        w_codes = {}
-        w_scales = {}
         acc = {}
 
-        def quantize(e, passes, cols, side):
+        def quantize(codes, scales, side):
             nc.vector.quantize_mx(
-                out=w_codes[e][:, passes, cols].rearrange("p o n -> p (o n)").bitcast(FP8X4),
-                scales=w_scales[e][:, passes, cols].rearrange("p o n -> p (o n)"),
+                out=codes.rearrange("p o n -> p (o n)").bitcast(FP8X4),
+                scales=scales.rearrange("p o n -> p (o n)"),
                 in_=side.rearrange("p o n t -> p (o n t)"),
             )
 
-        def multiply(e, h, o):
+        def multiply(bank, codes, scales, e, o, start, stop):
             g, j = divmod(e, GROUP)
             mine = slice(j * C, (j + 1) * C)
-            cols = slice(h * P, (h + 1) * P)
             nc.tensor.matmul_mx(
-                out=acc[e, h][:],
-                lhsT=w_codes[e][:, o, cols].bitcast(FP8X4),
-                lhsT_scale=w_scales[e][:, o, cols],
+                out=bank,
+                lhsT=codes.bitcast(FP8X4),
+                lhsT_scale=scales,
                 rhs=slot_words[g, o][:, mine].bitcast(FP8X4),
                 rhs_scale=slot_scales[g][4 * o : P, mine],
-                start=(o == 0),
-                stop=(o == PASSES - 1),
+                start=start,
+                stop=stop,
             )
 
-        def activate(e, h):
-            nc.scalar.activation(y[h][:, e * C : (e + 1) * C], acc[e, h][:], GELU, bias=bias[:, h, e : e + 1])
+        def activate(e, h, bank):
+            nc.scalar.activation(y[h][:, e * C : (e + 1) * C], bank, GELU, bias=bias[:, h, e : e + 1])
+
+        w_codes = {}
+        w_scales = {}
+        last = slice(PASSES - 1, PASSES)
 
         def begin_expert(e):
-            w_codes[e] = work.tile([P, PASSES, N], U32, name="w_codes", align_bytes=64)
-            w_scales[e] = work.tile([P, PASSES, N], U8, name="w_scales", align_bytes=64)
-            side = work.tile([P, 2, N, PACK], BF16, name="side_s", align_bytes=64)
-            every = slice(0, N)
-            if e < E - 1:
-                interleave(nc.scalar.copy, side[:], raw_passes(e, 0, 2, every))
-                quantize(e, slice(0, 2), every, side[:])
+            width = N if e < WHOLE else P
+            every = slice(0, width)
+            key = (e, 0) if e < WHOLE else (e, 0, 0)
+            w_codes[e] = work.tile([P, PASSES, width], U32, name="w_codes", align_bytes=64)
+            w_scales[e] = work.tile([P, PASSES, width], U8, name="w_scales", align_bytes=64)
+            side = work.tile([P, 2, width, PACK], BF16, name="side_s", align_bytes=64)
+            if e == E - 1:
+                for o in range(2):
+                    interleave(nc.scalar.copy, side[:, o : o + 1, :, :], raw_passes((e, o, 0), 1, every))
+                    quantize(w_codes[e][:, o : o + 1, :], w_scales[e][:, o : o + 1, :], side[:, o : o + 1, :, :])
             else:
-                interleave(nc.scalar.copy, side[:, 0:1, :, :], raw_passes(e, 0, 1, every))
-                quantize(e, slice(0, 1), every, side[:, 0:1, :, :])
-                interleave(nc.vector.tensor_copy, side[:, 1:2, :, :], raw_passes(e, 1, 1, every))
-                quantize(e, slice(1, 2), slice(0, N), side[:, 1:2, :, :])
-            for h in range(HALVES):
+                cut = width * 3 // 4 if busy + 1 < e < WHOLE else width
+                interleave(nc.scalar.copy, side[:, :, 0:cut, :], raw_passes(key, 2, slice(0, cut)))
+                if cut < width:
+                    interleave(nc.vector.tensor_copy, side[:, :, cut:width, :], raw_passes(key, 2, slice(cut, width)))
+                quantize(w_codes[e][:, 0:2, :], w_scales[e][:, 0:2, :], side[:])
+            for h in range(width // P):
+                cols = slice(h * P, (h + 1) * P)
                 acc[e, h] = psum.tile([P, C], F32, name="acc", tag="bank")
                 for o in range(2):
-                    multiply(e, h, o)
+                    multiply(acc[e, h][:], w_codes[e][:, o, cols], w_scales[e][:, o, cols], e, o, o == 0, False)
+
+        def close(e, h):
+            cols = slice(h * P, (h + 1) * P)
+            multiply(acc[e, h][:], w_codes[e][:, 2, cols], w_scales[e][:, 2, cols], e, 2, False, True)
+            activate(e, h, acc[e, h][:])
 
         def end_expert(e):
-            last = slice(PASSES - 1, PASSES)
+            if e > busy:
+                width = N if e < WHOLE else P
+                side = work.tile([P, 1, width, PACK], BF16, name="side_w", align_bytes=64)
+                key = (e, 2) if e < WHOLE else (e, 2, 0)
+                interleave(nc.vector.tensor_copy, side[:], raw_passes(key, 1, slice(0, width)))
+                quantize(w_codes[e][:, last, :], w_scales[e][:, last, :], side[:])
+                for h in range(width // P):
+                    close(e, h)
+                return
             sides = []
             for h in range(HALVES):
                 if (e, h) in paced:
                     sides.append(ring.tile([P, 1, P, PACK], BF16, name="side_p", tag="pace%d_%d" % (e, h), align_bytes=64))
                 else:
-                    sides.append(work.tile([P, 1, P, PACK], BF16, name="side_v", tag="side_v%d" % h, align_bytes=64))
-            cut = SHARE if e <= busy else P if e < E - 1 else 0
-            interleave(nc.vector.tensor_copy, sides[0][:], raw_passes(e, 2, 1, slice(0, P)))
-            if cut > 0:
-                interleave(nc.vector.tensor_copy, sides[1][:, :, 0:cut, :], raw_passes(e, 2, 1, slice(P, P + cut)))
-            if cut < P:
-                interleave(nc.scalar.copy, sides[1][:, :, cut:P, :], raw_passes(e, 2, 1, slice(P + cut, N)))
+                    sides.append(work.tile([P, 1, P, PACK], BF16, name="side_v", align_bytes=64))
+            interleave(nc.vector.tensor_copy, sides[0][:], raw_passes((e, 2), 1, slice(0, P)))
+            interleave(nc.vector.tensor_copy, sides[1][:, :, 0:SHARE, :], raw_passes((e, 2), 1, slice(P, P + SHARE)))
+            if SHARE < P:
+                interleave(nc.scalar.copy, sides[1][:, :, SHARE:P, :], raw_passes((e, 2), 1, slice(P + SHARE, N)))
             for h in range(HALVES):
-                quantize(e, last, slice(h * P, (h + 1) * P), sides[h][:])
-                multiply(e, h, 2)
-                activate(e, h)
+                cols = slice(h * P, (h + 1) * P)
+                quantize(w_codes[e][:, last, cols], w_scales[e][:, last, cols], sides[h][:])
+                close(e, h)
             for h in range(HALVES):
                 if (e, h) in paced:
                     gather(paced[e, h][0], paced[e, h][1], ring, "pace%d_%d" % (e, h))
 
         nc.sync.dma_start(slot_list[:], offs)
-        load_token_words(0)
-        load_w(0, 2, False)
-        load_token_words(1)
-        load_token_words(2)
-        for sort in order:
-            gather(0, sort, keep, "first%d" % sort)
+        for o in range(PASSES):
+            load_token_words(o)
+        load_whole(0, 2, False)
+        for g, sort in every_gather[:AHEAD]:
+            gather(g, sort, keep, "first%d_%d" % (g, sort))
+
+        by_row = psum.tile([P, P], F32, name="by_row", tag="bank")
+        nc.tensor.transpose(by_row[:], gate_rows[:], identity[:])
+        gate_cols = keep.tile([P, TOP * blocks], F32, name="gate_cols")
+        nc.scalar.copy(gate_cols[:], by_row[:, 0 : TOP * blocks])
+        planes = keep.tile([P, TOP * T], F32, name="planes")
+        for at in range(0, TOP * T, BANK):
+            spread = psum.tile([P, BANK], F32, name="spread", tag="bank")
+            for j in range(0, BANK, P):
+                q = (at + j) // P
+                nc.tensor.transpose(spread[:, j : j + P], gate_cols[:, q : q + 1].to_broadcast([P, P]), identity[:])
+            nc.scalar.copy(planes[:, at : at + BANK], spread[:])
+
         begin_expert(0)
-        for e in range(1, E):
-            load_w(PASSES * e - 1, PASSES, e < E - 1)
+        for e in range(1, WHOLE):
+            load_whole(PASSES * e - 1, PASSES, True)
             end_expert(e - 1)
             begin_expert(e)
-        load_w(PASSES * E - 1, 1, True)
+        load_halves(0, [(WHOLE, 0)])
+        load_whole(PASSES * WHOLE - 1, 1, True)
+        load_halves(0, [(WHOLE, 1)])
+        end_expert(WHOLE - 1)
+        begin_expert(WHOLE)
+        for e in range(WHOLE + 1, E - 1):
+            load_halves(0, [(e, 0), (e, 1), (e - 1, 2)])
+            end_expert(e - 1)
+            begin_expert(e)
+        load_halves(0, [(E - 2, 2), (E - 1, 0), (E - 1, 1), (E - 1, 2)])
+        end_expert(E - 2)
+        begin_expert(E - 1)
         end_expert(E - 1)
 
         back = []
@@ -193,22 +255,42 @@ def tile_moe_pkd_lin_gelu_kernel(
             back.append(keep.tile([P, T // 16], U16, name="back%d" % r))
             nc.sync.dma_start(back[r][:], pos)
 
-        identity = keep.tile([P, P], F32, name="identity")
-        make_identity(nc, identity[:])
-        blocks = T // P
+        todo = [(e, o) for e in range(WHOLE, E) for o in range(PASSES)]
+        steps = [todo[0:1]] + [todo[i : i + 2] for i in range(1, len(todo) - 1, 2)] + [todo[-1:]]
+        if len(todo) % 2:
+            steps = [todo[0:1]] + [todo[i : i + 2] for i in range(1, len(todo) - 2, 2)] + [todo[-2:-1], todo[-1:]]
+        held = {1: "part1", 3: "part2", len(steps) - 1: "part3"}
+        rest = psum.tile([P, SPLIT * C], F32, name="rest", tag="bank")
+        for s, step in enumerate(steps):
+            load_halves(1, step)
+            count = len(step)
+            tag = held.get(s, "pace%d_%d" % places[s])
+            side = ring.tile([P, count, P, PACK], BF16, name="side_r", tag=tag, align_bytes=64)
+            codes = keep.tile([P, count, P], U32, name="rest_codes%d" % s, align_bytes=64)
+            scales = keep.tile([P, count, P], U8, name="rest_scales%d" % s, align_bytes=64)
+            if s < 3:
+                interleave(nc.scalar.copy, side[:], raw_passes(step[0] + (1,), count, slice(0, P)))
+            else:
+                for i in range(count):
+                    interleave(nc.scalar.copy, side[:, i : i + 1, :, :], raw_passes(step[i] + (1,), 1, slice(0, P)))
+            quantize(codes[:], scales[:], side[:])
+            for i, (e, o) in enumerate(step):
+                cols = slice((e - WHOLE) * C, (e - WHOLE + 1) * C)
+                multiply(rest[:, cols], codes[:, i, :], scales[:, i, :], e, o, (e, o) == todo[0], (e, o) == todo[-1])
+        for e in range(WHOLE, E):
+            activate(e, 1, rest[:, (e - WHOLE) * C : (e - WHOLE + 1) * C])
+
         pieces = (slice(0, 3 * P), slice(3 * P, T))
         for h in range(HALVES):
             rows = slice(h * P, (h + 1) * P)
-            gates = stream.tile([P, TOP, T], F32, name="gates", tag="stream")
-            for r in range(TOP):
-                nc.sync.dma_start(gates[:, r, :], gate[r, rows, :])
             summed = TOP if h < HALVES - 1 else TOP - 1
             turned = [psum.tile([P, P], F32, name="turned", tag="bank") for c in range(blocks)]
             for r in range(summed):
-                part = keep.tile([P, T], F32, name="part%d_%d" % (h, r))
+                part = ring.tile([P, T], F32, name="part", tag="part%d" % r, align_bytes=64)
                 for cols in pieces if (h, r) == (HALVES - 1, summed - 1) else (slice(0, T),):
                     picks = back[r][:, cols.start // 16 : cols.stop // 16]
-                    nc.vector.tensor_tensor(part[:, cols], y[h][:].indirect(picks), gates[:, r, cols], MULT)
+                    factor = planes[:, r * T + cols.start : r * T + cols.stop]
+                    nc.vector.tensor_tensor(part[:, cols], y[h][:].indirect(picks), factor, MULT)
                     for c in range(cols.start // P, cols.stop // P):
                         nc.tensor.matmul(
                             turned[c][:],
@@ -235,7 +317,8 @@ def tile_moe_pkd_lin_gelu_kernel(
                 part = keep.tile([P, T], F32, name="part_last")
                 for cols in pieces:
                     picks = back[TOP - 1][:, cols.start // 16 : cols.stop // 16]
-                    nc.vector.tensor_tensor(part[:, cols], y[h][:].indirect(picks), gates[:, TOP - 1, cols], MULT)
+                    factor = planes[:, (TOP - 1) * T + cols.start : (TOP - 1) * T + cols.stop]
+                    nc.vector.tensor_tensor(part[:, cols], y[h][:].indirect(picks), factor, MULT)
                 for cols, bank in zip(pieces, sums):
                     nc.vector.tensor_tensor(total[:, cols], bank[:], part[:, cols], ADD)
                     nc.sync.dma_start(out[rows, cols], total[:, cols])

@@ -23,15 +23,14 @@ PACK = 4
 K_PASS = P * PACK
 PASSES = K // K_PASS
 HALVES = N // P
-BANK = 512
 GROUP = 4
-WINDOW = 704
+CUT = 256
 RAW_BUFS = 6
-SHARE = 128
-SPLIT = 4
+SHARE = 64
+LATE = 192
+SPLIT = 3
 WHOLE = E - SPLIT
-SHIFT = 1
-AHEAD = 6
+ROOM = PASSES * PACK * N
 
 
 def tile_moe_pkd_lin_gelu_kernel(
@@ -45,30 +44,24 @@ def tile_moe_pkd_lin_gelu_kernel(
         ring = ctx.enter_context(tc.tile_pool(name="ring", bufs=1))
         psum = ctx.enter_context(tc.psum_pool(name="psum", bufs=8))
 
-        token_scales = keep.tile([P, WINDOW], U8, name="token_scales")
-        blocks = T // P
-        gate_rows = keep.tile([P, P], F32, name="gate_rows")
-        nc.vector.memset(gate_rows[:], 0.0)
-        nc.vector.memset(token_scales[:].bitcast(I32), 0)
-        spaced = gate.rearrange("r n t -> (r n t)").rearrange("(q s) -> q s", q=TOP * blocks)
-        nc.scalar.dma_start(gate_rows[0 : TOP * blocks, :], spaced[:, 0:P])
+        token_scales = keep.tile([P, T], U8, name="token_scales")
+        nc.gpsimd.memset(token_scales[:].bitcast(I32), 0)
         for q in range(4):
             nc.scalar.dma_start(
-                token_scales[32 * q : 32 * q + 4 * PASSES, 0:T].bitcast(I32),
+                token_scales[32 * q : 32 * q + 4 * PASSES, :].bitcast(I32),
                 x_scales[:, 4 * q : 4 * q + 4, :].bitcast(I32),
             )
+        blocks = T // P
         bias = keep.tile([P, HALVES, 24], F32, name="bias")
         nc.scalar.dma_start(bias[:, :, 0:E], b.rearrange("(h p) e -> p h e", p=P))
         identity = keep.tile([P, P], F32, name="identity")
         make_identity(nc, identity[:])
 
         slot_list = keep.tile([P, E * C // 16], U16, name="slot_list")
-        token_words = [keep.tile([P, WINDOW], I32, name="token_words%d" % o) for o in range(PASSES)]
-        for o in range(PASSES):
-            nc.vector.memset(token_words[o][:, T:WINDOW], 0)
+        token_words = [keep.tile([P, T], I32, name="token_words%d" % o) for o in range(PASSES)]
 
         def load_token_words(o):
-            nc.sync.dma_start(token_words[o][:, 0:T], x_words[o].rearrange("p t r -> p (t r)").bitcast(I32))
+            nc.sync.dma_start(token_words[o][:], x_words[o].rearrange("p t r -> p (t r)").bitcast(I32))
 
         w_rows = w.rearrange("e k n -> (e k) n")
         raw = {}
@@ -85,15 +78,34 @@ def tile_moe_pkd_lin_gelu_kernel(
             for i in range(count):
                 raw[divmod(first + i, PASSES)] = (chunk, i)
 
+        room = [None, ROOM]
+
+        def take(columns):
+            if room[1] + columns > ROOM:
+                room[0:2] = [stream.tile([P, ROOM], F32, name="small", tag="stream"), 0]
+            room[1:2] = [room[1] + columns]
+            return room[0][:, room[1] - columns : room[1]]
+
+        def place_halves(h, which):
+            place = take(len(which) * K_PASS).rearrange("p (o j n) -> p o j n", j=PACK, n=P)
+            for i, (e, o) in enumerate(which):
+                raw[e, o, h] = (place, i)
+
+        def load_half(e, o, h):
+            rows = w[e, o * K_PASS : (o + 1) * K_PASS, h * P : (h + 1) * P]
+            place, i = raw[e, o, h]
+            nc.sync.dma_start(place[:, i, :, :], rows.rearrange("(p j) n -> p j n", j=PACK))
+
         def load_halves(h, which):
+            place_halves(h, which)
             for e, o in which:
-                i = ((e - WHOLE) * PASSES + o + SHIFT * h) % (HALVES * PASSES)
-                if (e, o, h) not in raw:
-                    chunk = stream.tile([P, HALVES * PASSES, PACK, P], F32, name="chunk", tag="stream")
-                    for q in range(e * PASSES + o, min(e * PASSES + o + HALVES * PASSES - i, E * PASSES)):
-                        raw[divmod(q, PASSES) + (h,)] = (chunk, i + q - e * PASSES - o)
-                rows = w[e, o * K_PASS : (o + 1) * K_PASS, h * P : (h + 1) * P]
-                nc.sync.dma_start(raw[e, o, h][0][:, i, :, :], rows.rearrange("(p j) n -> p j n", j=PACK))
+                load_half(e, o, h)
+
+        planes = []
+
+        def load_plane():
+            planes.append(take(T))
+            nc.sync.dma_start(planes[-1], gate[len(planes) - 1, 0:P, :])
 
         def raw_passes(key, count, cols):
             chunk, i = raw[key]
@@ -111,12 +123,14 @@ def tile_moe_pkd_lin_gelu_kernel(
                 dst = pool.tile([P, GROUP * C], U32, name="slot_words", tag=tag, align_bytes=64)
                 slot_words[g, sort] = dst
                 window = token_words[sort][:].bitcast(U32)
-            cols = slot_list[:, g * GROUP * C // 16 : (g + 1) * GROUP * C // 16]
-            nc.vector.tensor_copy(dst[:], window.indirect(cols))
+            for at in range(0, GROUP * C, CUT):
+                first = g * GROUP * C + at
+                cols = slot_list[:, first // 16 : (first + CUT) // 16]
+                nc.vector.tensor_copy(dst[:, at : at + CUT], window.indirect(cols))
 
-        every_gather = [(g, sort) for g in range(E // GROUP) for sort in range(PASSES + 1)]
-        later = every_gather[AHEAD:]
-        places = [(e, h) for e in range(E) for h in range(HALVES) if h == 0 or e == 10]
+        order = (0, PASSES, 1, 2)
+        later = [(g, sort) for g in range(1, E // GROUP) for sort in order]
+        places = [(e, h) for e in range(E) for h in range(HALVES) if h == 0 or e % 2 == 0]
         paced = dict(zip(places, later))
         busy = max(e for e, h in paced)
 
@@ -168,7 +182,7 @@ def tile_moe_pkd_lin_gelu_kernel(
                     interleave(nc.scalar.copy, side[:, o : o + 1, :, :], raw_passes((e, o, 0), 1, every))
                     quantize(w_codes[e][:, o : o + 1, :], w_scales[e][:, o : o + 1, :], side[:, o : o + 1, :, :])
             else:
-                cut = width * 3 // 4 if busy + 1 < e < WHOLE else width
+                cut = LATE if busy + 1 < e < WHOLE else width
                 interleave(nc.scalar.copy, side[:, :, 0:cut, :], raw_passes(key, 2, slice(0, cut)))
                 if cut < width:
                     interleave(nc.vector.tensor_copy, side[:, :, cut:width, :], raw_passes(key, 2, slice(cut, width)))
@@ -202,8 +216,7 @@ def tile_moe_pkd_lin_gelu_kernel(
                     sides.append(work.tile([P, 1, P, PACK], BF16, name="side_v", align_bytes=64))
             interleave(nc.vector.tensor_copy, sides[0][:], raw_passes((e, 2), 1, slice(0, P)))
             interleave(nc.vector.tensor_copy, sides[1][:, :, 0:SHARE, :], raw_passes((e, 2), 1, slice(P, P + SHARE)))
-            if SHARE < P:
-                interleave(nc.scalar.copy, sides[1][:, :, SHARE:P, :], raw_passes((e, 2), 1, slice(P + SHARE, N)))
+            interleave(nc.scalar.copy, sides[1][:, :, SHARE:P, :], raw_passes((e, 2), 1, slice(P + SHARE, N)))
             for h in range(HALVES):
                 cols = slice(h * P, (h + 1) * P)
                 quantize(w_codes[e][:, last, cols], w_scales[e][:, last, cols], sides[h][:])
@@ -213,32 +226,24 @@ def tile_moe_pkd_lin_gelu_kernel(
                     gather(paced[e, h][0], paced[e, h][1], ring, "pace%d_%d" % (e, h))
 
         nc.sync.dma_start(slot_list[:], offs)
-        for o in range(PASSES):
-            load_token_words(o)
+        load_token_words(0)
         load_whole(0, 2, False)
-        for g, sort in every_gather[:AHEAD]:
-            gather(g, sort, keep, "first%d_%d" % (g, sort))
-
-        by_row = psum.tile([P, P], F32, name="by_row", tag="bank")
-        nc.tensor.transpose(by_row[:], gate_rows[:], identity[:])
-        gate_cols = keep.tile([P, TOP * blocks], F32, name="gate_cols")
-        nc.scalar.copy(gate_cols[:], by_row[:, 0 : TOP * blocks])
-        planes = keep.tile([P, TOP * T], F32, name="planes")
-        for at in range(0, TOP * T, BANK):
-            spread = psum.tile([P, BANK], F32, name="spread", tag="bank")
-            for j in range(0, BANK, P):
-                q = (at + j) // P
-                nc.tensor.transpose(spread[:, j : j + P], gate_cols[:, q : q + 1].to_broadcast([P, P]), identity[:])
-            nc.scalar.copy(planes[:, at : at + BANK], spread[:])
+        load_token_words(1)
+        load_token_words(2)
+        for sort in order:
+            gather(0, sort, keep, "first%d" % sort)
 
         begin_expert(0)
         for e in range(1, WHOLE):
             load_whole(PASSES * e - 1, PASSES, True)
             end_expert(e - 1)
             begin_expert(e)
-        load_halves(0, [(WHOLE, 0)])
-        load_whole(PASSES * WHOLE - 1, 1, True)
-        load_halves(0, [(WHOLE, 1)])
+        place_halves(0, [(WHOLE, 0), (WHOLE, 1)])
+        load_half(WHOLE, 0, 0)
+        place = take(PACK * N).rearrange("p (o j n) -> p o j n", j=PACK, n=N)
+        raw[WHOLE - 1, 2] = (place, 0)
+        nc.sync.dma_start(place[:, 0, :, :], w[WHOLE - 1, 2 * K_PASS : K, :].rearrange("(p j) n -> p j n", j=PACK))
+        load_half(WHOLE, 1, 0)
         end_expert(WHOLE - 1)
         begin_expert(WHOLE)
         for e in range(WHOLE + 1, E - 1):
@@ -262,21 +267,25 @@ def tile_moe_pkd_lin_gelu_kernel(
         held = {1: "part1", 3: "part2", len(steps) - 1: "part3"}
         rest = psum.tile([P, SPLIT * C], F32, name="rest", tag="bank")
         for s, step in enumerate(steps):
+            if s in (0, 2, 4):
+                load_plane()
             load_halves(1, step)
             count = len(step)
             tag = held.get(s, "pace%d_%d" % places[s])
             side = ring.tile([P, count, P, PACK], BF16, name="side_r", tag=tag, align_bytes=64)
             codes = keep.tile([P, count, P], U32, name="rest_codes%d" % s, align_bytes=64)
             scales = keep.tile([P, count, P], U8, name="rest_scales%d" % s, align_bytes=64)
+            chunk = raw[step[0] + (1,)][0]
             if s < 3:
-                interleave(nc.scalar.copy, side[:], raw_passes(step[0] + (1,), count, slice(0, P)))
+                interleave(nc.scalar.copy, side[:], chunk)
             else:
                 for i in range(count):
-                    interleave(nc.scalar.copy, side[:, i : i + 1, :, :], raw_passes(step[i] + (1,), 1, slice(0, P)))
+                    interleave(nc.scalar.copy, side[:, i : i + 1, :, :], chunk[:, i : i + 1, :, :])
             quantize(codes[:], scales[:], side[:])
             for i, (e, o) in enumerate(step):
                 cols = slice((e - WHOLE) * C, (e - WHOLE + 1) * C)
                 multiply(rest[:, cols], codes[:, i, :], scales[:, i, :], e, o, (e, o) == todo[0], (e, o) == todo[-1])
+        load_plane()
         for e in range(WHOLE, E):
             activate(e, 1, rest[:, (e - WHOLE) * C : (e - WHOLE + 1) * C])
 
@@ -289,7 +298,7 @@ def tile_moe_pkd_lin_gelu_kernel(
                 part = ring.tile([P, T], F32, name="part", tag="part%d" % r, align_bytes=64)
                 for cols in pieces if (h, r) == (HALVES - 1, summed - 1) else (slice(0, T),):
                     picks = back[r][:, cols.start // 16 : cols.stop // 16]
-                    factor = planes[:, r * T + cols.start : r * T + cols.stop]
+                    factor = planes[r][:, cols]
                     nc.vector.tensor_tensor(part[:, cols], y[h][:].indirect(picks), factor, MULT)
                     for c in range(cols.start // P, cols.stop // P):
                         nc.tensor.matmul(
@@ -317,7 +326,7 @@ def tile_moe_pkd_lin_gelu_kernel(
                 part = keep.tile([P, T], F32, name="part_last")
                 for cols in pieces:
                     picks = back[TOP - 1][:, cols.start // 16 : cols.stop // 16]
-                    factor = planes[:, (TOP - 1) * T + cols.start : (TOP - 1) * T + cols.stop]
+                    factor = planes[TOP - 1][:, cols]
                     nc.vector.tensor_tensor(part[:, cols], y[h][:].indirect(picks), factor, MULT)
                 for cols, bank in zip(pieces, sums):
                     nc.vector.tensor_tensor(total[:, cols], bank[:], part[:, cols], ADD)

@@ -24,10 +24,12 @@ K_PASS = P * PACK
 PASSES = K // K_PASS
 HALVES = N // P
 GROUP = 4
-CUT = 256
+WINDOW = 704
+AHEAD = 6
+RELIEF = 2
+LATE = 192
 RAW_BUFS = 6
 SHARE = 64
-LATE = 192
 SPLIT = 3
 WHOLE = E - SPLIT
 ROOM = PASSES * PACK * N
@@ -44,11 +46,11 @@ def tile_moe_pkd_lin_gelu_kernel(
         ring = ctx.enter_context(tc.tile_pool(name="ring", bufs=1))
         psum = ctx.enter_context(tc.psum_pool(name="psum", bufs=8))
 
-        token_scales = keep.tile([P, T], U8, name="token_scales")
+        token_scales = keep.tile([P, WINDOW], U8, name="token_scales")
         nc.gpsimd.memset(token_scales[:].bitcast(I32), 0)
         for q in range(4):
             nc.scalar.dma_start(
-                token_scales[32 * q : 32 * q + 4 * PASSES, :].bitcast(I32),
+                token_scales[32 * q : 32 * q + 4 * PASSES, 0:T].bitcast(I32),
                 x_scales[:, 4 * q : 4 * q + 4, :].bitcast(I32),
             )
         blocks = T // P
@@ -58,10 +60,12 @@ def tile_moe_pkd_lin_gelu_kernel(
         make_identity(nc, identity[:])
 
         slot_list = keep.tile([P, E * C // 16], U16, name="slot_list")
-        token_words = [keep.tile([P, T], I32, name="token_words%d" % o) for o in range(PASSES)]
+        token_words = [keep.tile([P, WINDOW], I32, name="token_words%d" % o) for o in range(PASSES)]
+        for o in range(PASSES):
+            nc.vector.memset(token_words[o][:, T:WINDOW], 0)
 
         def load_token_words(o):
-            nc.sync.dma_start(token_words[o][:], x_words[o].rearrange("p t r -> p (t r)").bitcast(I32))
+            nc.sync.dma_start(token_words[o][:, 0:T], x_words[o].rearrange("p t r -> p (t r)").bitcast(I32))
 
         w_rows = w.rearrange("e k n -> (e k) n")
         raw = {}
@@ -123,14 +127,12 @@ def tile_moe_pkd_lin_gelu_kernel(
                 dst = pool.tile([P, GROUP * C], U32, name="slot_words", tag=tag, align_bytes=64)
                 slot_words[g, sort] = dst
                 window = token_words[sort][:].bitcast(U32)
-            for at in range(0, GROUP * C, CUT):
-                first = g * GROUP * C + at
-                cols = slot_list[:, first // 16 : (first + CUT) // 16]
-                nc.vector.tensor_copy(dst[:, at : at + CUT], window.indirect(cols))
+            cols = slot_list[:, g * GROUP * C // 16 : (g + 1) * GROUP * C // 16]
+            nc.vector.tensor_copy(dst[:], window.indirect(cols))
 
-        order = (0, PASSES, 1, 2)
-        later = [(g, sort) for g in range(1, E // GROUP) for sort in order]
-        places = [(e, h) for e in range(E) for h in range(HALVES) if h == 0 or e % 2 == 0]
+        every_gather = [(g, sort) for g in range(E // GROUP) for sort in range(PASSES + 1)]
+        later = every_gather[AHEAD:]
+        places = [(e, 0) for e in range(E)]
         paced = dict(zip(places, later))
         busy = max(e for e, h in paced)
 
@@ -182,10 +184,14 @@ def tile_moe_pkd_lin_gelu_kernel(
                     interleave(nc.scalar.copy, side[:, o : o + 1, :, :], raw_passes((e, o, 0), 1, every))
                     quantize(w_codes[e][:, o : o + 1, :], w_scales[e][:, o : o + 1, :], side[:, o : o + 1, :, :])
             else:
-                cut = LATE if busy + 1 < e < WHOLE else width
-                interleave(nc.scalar.copy, side[:, :, 0:cut, :], raw_passes(key, 2, slice(0, cut)))
-                if cut < width:
-                    interleave(nc.vector.tensor_copy, side[:, :, cut:width, :], raw_passes(key, 2, slice(cut, width)))
+                if e == 0:
+                    for o in range(2):
+                        interleave(nc.scalar.copy, side[:, o : o + 1, :, :], raw_passes((e, o), 1, every))
+                elif WHOLE - RELIEF <= e < WHOLE:
+                    interleave(nc.scalar.copy, side[:, :, 0:LATE, :], raw_passes(key, 2, slice(0, LATE)))
+                    interleave(nc.vector.tensor_copy, side[:, :, LATE:N, :], raw_passes(key, 2, slice(LATE, N)))
+                else:
+                    interleave(nc.scalar.copy, side[:], raw_passes(key, 2, every))
                 quantize(w_codes[e][:, 0:2, :], w_scales[e][:, 0:2, :], side[:])
             for h in range(width // P):
                 cols = slice(h * P, (h + 1) * P)
@@ -227,11 +233,11 @@ def tile_moe_pkd_lin_gelu_kernel(
 
         nc.sync.dma_start(slot_list[:], offs)
         load_token_words(0)
-        load_whole(0, 2, False)
         load_token_words(1)
+        load_whole(0, 2, False)
         load_token_words(2)
-        for sort in order:
-            gather(0, sort, keep, "first%d" % sort)
+        for g, sort in every_gather[:AHEAD]:
+            gather(g, sort, keep, "first%d_%d" % (g, sort))
 
         begin_expert(0)
         for e in range(1, WHOLE):
@@ -264,10 +270,10 @@ def tile_moe_pkd_lin_gelu_kernel(
         steps = [todo[0:1]] + [todo[i : i + 2] for i in range(1, len(todo) - 1, 2)] + [todo[-1:]]
         if len(todo) % 2:
             steps = [todo[0:1]] + [todo[i : i + 2] for i in range(1, len(todo) - 2, 2)] + [todo[-2:-1], todo[-1:]]
-        held = {1: "part1", 3: "part2", len(steps) - 1: "part3"}
+        held = {1: "part1", 2: "part2", len(steps) - 1: "part3"}
         rest = psum.tile([P, SPLIT * C], F32, name="rest", tag="bank")
         for s, step in enumerate(steps):
-            if s in (0, 2, 4):
+            if s in (0, 2, 3):
                 load_plane()
             load_halves(1, step)
             count = len(step)

@@ -26,6 +26,7 @@ HALVES = N // P
 GROUP = 4
 WINDOW = 704
 AHEAD = 6
+ALIGN = 256
 RELIEF = 2
 LATE = 192
 RAW_BUFS = 6
@@ -60,7 +61,7 @@ def tile_moe_pkd_lin_gelu_kernel(
         make_identity(nc, identity[:])
 
         slot_list = keep.tile([P, E * C // 16], U16, name="slot_list")
-        token_words = [keep.tile([P, WINDOW], I32, name="token_words%d" % o) for o in range(PASSES)]
+        token_words = [keep.tile([P, WINDOW], I32, name="token_words%d" % o, align_bytes=ALIGN) for o in range(PASSES)]
         for o in range(PASSES):
             nc.vector.memset(token_words[o][:, T:WINDOW], 0)
 
@@ -71,7 +72,7 @@ def tile_moe_pkd_lin_gelu_kernel(
         raw = {}
 
         def load_whole(first, count, one_dma):
-            chunk = stream.tile([P, count, PACK, N], F32, name="chunk", tag="stream")
+            chunk = stream.tile([P, count, PACK, N], F32, name="chunk", tag="stream", align_bytes=ALIGN)
             src = w_rows[first * K_PASS : (first + count) * K_PASS, :].rearrange("(o p j) n -> p o (j n)", p=P, j=PACK)
             dst = chunk[:].rearrange("p o j n -> p o (j n)")
             if one_dma:
@@ -86,7 +87,7 @@ def tile_moe_pkd_lin_gelu_kernel(
 
         def take(columns):
             if room[1] + columns > ROOM:
-                room[0:2] = [stream.tile([P, ROOM], F32, name="small", tag="stream"), 0]
+                room[0:2] = [stream.tile([P, ROOM], F32, name="small", tag="stream", align_bytes=ALIGN), 0]
             room[1:2] = [room[1] + columns]
             return room[0][:, room[1] - columns : room[1]]
 
@@ -316,7 +317,7 @@ def tile_moe_pkd_lin_gelu_kernel(
                             is_transpose=True,
                         )
             by_token = keep.tile([P, blocks, P], F32, name="by_token%d" % h)
-            total = keep.tile([P, T], F32, name="total%d" % h)
+            total = keep.tile([P, T], F32, name="total%d" % h, align_bytes=ALIGN)
             sums = []
             for cols in pieces:
                 sums.append(psum.tile([P, cols.stop - cols.start], F32, name="sums", tag="bank"))

@@ -26,12 +26,13 @@ HALVES = N // P
 GROUP = 4
 WINDOW = 704
 AHEAD = 6
+BANK = 512
 ALIGN = 256
 RELIEF = 2
 LATE = 192
 RAW_BUFS = 6
-SHARE = 64
-SPLIT = 3
+SHARE = 128
+SPLIT = 4
 WHOLE = E - SPLIT
 ROOM = PASSES * PACK * N
 
@@ -49,14 +50,10 @@ def tile_moe_pkd_lin_gelu_kernel(
 
         token_scales = keep.tile([P, WINDOW], U8, name="token_scales")
         nc.gpsimd.memset(token_scales[:].bitcast(I32), 0)
-        for q in range(4):
-            nc.scalar.dma_start(
-                token_scales[32 * q : 32 * q + 4 * PASSES, 0:T].bitcast(I32),
-                x_scales[:, 4 * q : 4 * q + 4, :].bitcast(I32),
-            )
         blocks = T // P
+        gate_rows = keep.tile([P, P], F32, name="gate_rows")
+        nc.gpsimd.memset(gate_rows[:], 0.0)
         bias = keep.tile([P, HALVES, 24], F32, name="bias")
-        nc.scalar.dma_start(bias[:, :, 0:E], b.rearrange("(h p) e -> p h e", p=P))
         identity = keep.tile([P, P], F32, name="identity")
         make_identity(nc, identity[:])
 
@@ -105,12 +102,6 @@ def tile_moe_pkd_lin_gelu_kernel(
             place_halves(h, which)
             for e, o in which:
                 load_half(e, o, h)
-
-        planes = []
-
-        def load_plane():
-            planes.append(take(T))
-            nc.sync.dma_start(planes[-1], gate[len(planes) - 1, 0:P, :])
 
         def raw_passes(key, count, cols):
             chunk, i = raw[key]
@@ -180,20 +171,15 @@ def tile_moe_pkd_lin_gelu_kernel(
             w_codes[e] = work.tile([P, PASSES, width], U32, name="w_codes", align_bytes=64)
             w_scales[e] = work.tile([P, PASSES, width], U8, name="w_scales", align_bytes=64)
             side = work.tile([P, 2, width, PACK], BF16, name="side_s", align_bytes=64)
-            if e == E - 1:
+            if e == 0:
                 for o in range(2):
-                    interleave(nc.scalar.copy, side[:, o : o + 1, :, :], raw_passes((e, o, 0), 1, every))
-                    quantize(w_codes[e][:, o : o + 1, :], w_scales[e][:, o : o + 1, :], side[:, o : o + 1, :, :])
+                    interleave(nc.scalar.copy, side[:, o : o + 1, :, :], raw_passes((e, o), 1, every))
+            elif WHOLE - RELIEF <= e < WHOLE:
+                interleave(nc.scalar.copy, side[:, :, 0:LATE, :], raw_passes(key, 2, slice(0, LATE)))
+                interleave(nc.vector.tensor_copy, side[:, :, LATE:N, :], raw_passes(key, 2, slice(LATE, N)))
             else:
-                if e == 0:
-                    for o in range(2):
-                        interleave(nc.scalar.copy, side[:, o : o + 1, :, :], raw_passes((e, o), 1, every))
-                elif WHOLE - RELIEF <= e < WHOLE:
-                    interleave(nc.scalar.copy, side[:, :, 0:LATE, :], raw_passes(key, 2, slice(0, LATE)))
-                    interleave(nc.vector.tensor_copy, side[:, :, LATE:N, :], raw_passes(key, 2, slice(LATE, N)))
-                else:
-                    interleave(nc.scalar.copy, side[:], raw_passes(key, 2, every))
-                quantize(w_codes[e][:, 0:2, :], w_scales[e][:, 0:2, :], side[:])
+                interleave(nc.scalar.copy, side[:], raw_passes(key, 2, every))
+            quantize(w_codes[e][:, 0:2, :], w_scales[e][:, 0:2, :], side[:])
             for h in range(width // P):
                 cols = slice(h * P, (h + 1) * P)
                 acc[e, h] = psum.tile([P, C], F32, name="acc", tag="bank")
@@ -223,7 +209,6 @@ def tile_moe_pkd_lin_gelu_kernel(
                     sides.append(work.tile([P, 1, P, PACK], BF16, name="side_v", align_bytes=64))
             interleave(nc.vector.tensor_copy, sides[0][:], raw_passes((e, 2), 1, slice(0, P)))
             interleave(nc.vector.tensor_copy, sides[1][:, :, 0:SHARE, :], raw_passes((e, 2), 1, slice(P, P + SHARE)))
-            interleave(nc.scalar.copy, sides[1][:, :, SHARE:P, :], raw_passes((e, 2), 1, slice(P + SHARE, N)))
             for h in range(HALVES):
                 cols = slice(h * P, (h + 1) * P)
                 quantize(w_codes[e][:, last, cols], w_scales[e][:, last, cols], sides[h][:])
@@ -237,8 +222,28 @@ def tile_moe_pkd_lin_gelu_kernel(
         load_token_words(1)
         load_whole(0, 2, False)
         load_token_words(2)
+        for q in range(4):
+            nc.sync.dma_start(
+                token_scales[32 * q : 32 * q + 4 * PASSES, 0:T].bitcast(I32),
+                x_scales[:, 4 * q : 4 * q + 4, :].bitcast(I32),
+            )
+        spaced = gate.rearrange("r n t -> (r n t)").rearrange("(q s) -> q s", q=TOP * blocks)
+        nc.sync.dma_start(gate_rows[0 : TOP * blocks, :], spaced[:, 0:P])
+        nc.sync.dma_start(bias[:, :, 0:E], b.rearrange("(h p) e -> p h e", p=P))
         for g, sort in every_gather[:AHEAD]:
             gather(g, sort, keep, "first%d_%d" % (g, sort))
+
+        by_row = psum.tile([P, P], F32, name="by_row", tag="bank")
+        nc.tensor.transpose(by_row[:], gate_rows[:], identity[:])
+        gate_cols = keep.tile([P, TOP * blocks], F32, name="gate_cols")
+        nc.scalar.copy(gate_cols[:], by_row[:, 0 : TOP * blocks])
+        planes = keep.tile([P, TOP * T], F32, name="planes", align_bytes=ALIGN)
+        for at in range(0, TOP * T, BANK):
+            spread = psum.tile([P, BANK], F32, name="spread", tag="bank")
+            for j in range(0, BANK, P):
+                q = (at + j) // P
+                nc.tensor.transpose(spread[:, j : j + P], gate_cols[:, q : q + 1].to_broadcast([P, P]), identity[:])
+            nc.scalar.copy(planes[:, at : at + BANK], spread[:])
 
         begin_expert(0)
         for e in range(1, WHOLE):
@@ -253,13 +258,11 @@ def tile_moe_pkd_lin_gelu_kernel(
         load_half(WHOLE, 1, 0)
         end_expert(WHOLE - 1)
         begin_expert(WHOLE)
-        for e in range(WHOLE + 1, E - 1):
+        for e in range(WHOLE + 1, E):
             load_halves(0, [(e, 0), (e, 1), (e - 1, 2)])
             end_expert(e - 1)
             begin_expert(e)
-        load_halves(0, [(E - 2, 2), (E - 1, 0), (E - 1, 1), (E - 1, 2)])
-        end_expert(E - 2)
-        begin_expert(E - 1)
+        load_halves(0, [(E - 1, 2)])
         end_expert(E - 1)
 
         back = []
@@ -271,11 +274,9 @@ def tile_moe_pkd_lin_gelu_kernel(
         steps = [todo[0:1]] + [todo[i : i + 2] for i in range(1, len(todo) - 1, 2)] + [todo[-1:]]
         if len(todo) % 2:
             steps = [todo[0:1]] + [todo[i : i + 2] for i in range(1, len(todo) - 2, 2)] + [todo[-2:-1], todo[-1:]]
-        held = {1: "part1", 2: "part2", len(steps) - 1: "part3"}
+        held = {1: "part1", 3: "part2", len(steps) - 1: "part3"}
         rest = psum.tile([P, SPLIT * C], F32, name="rest", tag="bank")
         for s, step in enumerate(steps):
-            if s in (0, 2, 3):
-                load_plane()
             load_halves(1, step)
             count = len(step)
             tag = held.get(s, "pace%d_%d" % places[s])
@@ -292,7 +293,6 @@ def tile_moe_pkd_lin_gelu_kernel(
             for i, (e, o) in enumerate(step):
                 cols = slice((e - WHOLE) * C, (e - WHOLE + 1) * C)
                 multiply(rest[:, cols], codes[:, i, :], scales[:, i, :], e, o, (e, o) == todo[0], (e, o) == todo[-1])
-        load_plane()
         for e in range(WHOLE, E):
             activate(e, 1, rest[:, (e - WHOLE) * C : (e - WHOLE + 1) * C])
 
@@ -305,7 +305,7 @@ def tile_moe_pkd_lin_gelu_kernel(
                 part = ring.tile([P, T], F32, name="part", tag="part%d" % r, align_bytes=64)
                 for cols in pieces if (h, r) == (HALVES - 1, summed - 1) else (slice(0, T),):
                     picks = back[r][:, cols.start // 16 : cols.stop // 16]
-                    factor = planes[r][:, cols]
+                    factor = planes[:, r * T + cols.start : r * T + cols.stop]
                     nc.vector.tensor_tensor(part[:, cols], y[h][:].indirect(picks), factor, MULT)
                     for c in range(cols.start // P, cols.stop // P):
                         nc.tensor.matmul(
@@ -333,7 +333,7 @@ def tile_moe_pkd_lin_gelu_kernel(
                 part = keep.tile([P, T], F32, name="part_last")
                 for cols in pieces:
                     picks = back[TOP - 1][:, cols.start // 16 : cols.stop // 16]
-                    factor = planes[TOP - 1][:, cols]
+                    factor = planes[:, (TOP - 1) * T + cols.start : (TOP - 1) * T + cols.stop]
                     nc.vector.tensor_tensor(part[:, cols], y[h][:].indirect(picks), factor, MULT)
                 for cols, bank in zip(pieces, sums):
                     nc.vector.tensor_tensor(total[:, cols], bank[:], part[:, cols], ADD)

@@ -25,16 +25,17 @@ PASSES = K // K_PASS
 HALVES = N // P
 GROUP = 4
 WINDOW = 704
-AHEAD = 6
+AHEAD = 8
+PAIRED = 11
 BANK = 512
 ALIGN = 256
 RELIEF = 2
 LATE = 192
-RAW_BUFS = 6
+RAW_BUFS = 3
 SHARE = 128
 SPLIT = 4
 WHOLE = E - SPLIT
-ROOM = PASSES * PACK * N
+ROOM = 2 * PASSES * PACK * N
 
 
 def tile_moe_pkd_lin_gelu_kernel(
@@ -58,25 +59,18 @@ def tile_moe_pkd_lin_gelu_kernel(
         make_identity(nc, identity[:])
 
         slot_list = keep.tile([P, E * C // 16], U16, name="slot_list")
-        token_words = [keep.tile([P, WINDOW], I32, name="token_words%d" % o, align_bytes=ALIGN) for o in range(PASSES)]
-        for o in range(PASSES):
-            nc.vector.memset(token_words[o][:, T:WINDOW], 0)
-
-        def load_token_words(o):
-            nc.sync.dma_start(token_words[o][:, 0:T], x_words[o].rearrange("p t r -> p (t r)").bitcast(I32))
+        token_words = keep.tile([P, (PASSES - 1) * T + WINDOW], I32, name="token_words", align_bytes=ALIGN)
+        nc.vector.memset(token_words[:, PASSES * T :], 0)
 
         w_rows = w.rearrange("e k n -> (e k) n")
         raw = {}
 
-        def load_whole(first, count, one_dma):
+        def load_whole(first, count, step):
             chunk = stream.tile([P, count, PACK, N], F32, name="chunk", tag="stream", align_bytes=ALIGN)
             src = w_rows[first * K_PASS : (first + count) * K_PASS, :].rearrange("(o p j) n -> p o (j n)", p=P, j=PACK)
             dst = chunk[:].rearrange("p o j n -> p o (j n)")
-            if one_dma:
-                nc.sync.dma_start(dst, src)
-            else:
-                for i in range(count):
-                    nc.sync.dma_start(dst[:, i, :], src[:, i, :])
+            for i in range(0, count, step):
+                nc.sync.dma_start(dst[:, i : i + step, :], src[:, i : i + step, :])
             for i in range(count):
                 raw[divmod(first + i, PASSES)] = (chunk, i)
 
@@ -118,7 +112,7 @@ def tile_moe_pkd_lin_gelu_kernel(
             else:
                 dst = pool.tile([P, GROUP * C], U32, name="slot_words", tag=tag, align_bytes=64)
                 slot_words[g, sort] = dst
-                window = token_words[sort][:].bitcast(U32)
+                window = token_words[:, sort * T : sort * T + WINDOW].bitcast(U32)
             cols = slot_list[:, g * GROUP * C // 16 : (g + 1) * GROUP * C // 16]
             nc.vector.tensor_copy(dst[:], window.indirect(cols))
 
@@ -136,6 +130,7 @@ def tile_moe_pkd_lin_gelu_kernel(
 
         y = [keep.tile([P, E * C], F32, name="y%d" % h) for h in range(HALVES)]
         acc = {}
+        shared = []
 
         def quantize(codes, scales, side):
             nc.vector.quantize_mx(
@@ -171,10 +166,7 @@ def tile_moe_pkd_lin_gelu_kernel(
             w_codes[e] = work.tile([P, PASSES, width], U32, name="w_codes", align_bytes=64)
             w_scales[e] = work.tile([P, PASSES, width], U8, name="w_scales", align_bytes=64)
             side = work.tile([P, 2, width, PACK], BF16, name="side_s", align_bytes=64)
-            if e == 0:
-                for o in range(2):
-                    interleave(nc.scalar.copy, side[:, o : o + 1, :, :], raw_passes((e, o), 1, every))
-            elif WHOLE - RELIEF <= e < WHOLE:
+            if WHOLE - RELIEF <= e < WHOLE:
                 interleave(nc.scalar.copy, side[:, :, 0:LATE, :], raw_passes(key, 2, slice(0, LATE)))
                 interleave(nc.vector.tensor_copy, side[:, :, LATE:N, :], raw_passes(key, 2, slice(LATE, N)))
             else:
@@ -182,14 +174,25 @@ def tile_moe_pkd_lin_gelu_kernel(
             quantize(w_codes[e][:, 0:2, :], w_scales[e][:, 0:2, :], side[:])
             for h in range(width // P):
                 cols = slice(h * P, (h + 1) * P)
-                acc[e, h] = psum.tile([P, C], F32, name="acc", tag="bank")
+                if e == WHOLE:
+                    shared.append(psum.tile([P, (SPLIT - 1) * C], F32, name="shared", tag="bank"))
+                if WHOLE <= e < E - 1:
+                    acc[e, h] = shared[0][:, (e - WHOLE) * C : (e - WHOLE + 1) * C]
+                else:
+                    acc[e, h] = psum.tile([P, C], F32, name="acc", tag="bank")[:]
                 for o in range(2):
-                    multiply(acc[e, h][:], w_codes[e][:, o, cols], w_scales[e][:, o, cols], e, o, o == 0, False)
+                    opens = o == 0 and not WHOLE < e < E - 1
+                    multiply(acc[e, h], w_codes[e][:, o, cols], w_scales[e][:, o, cols], e, o, opens, False)
 
         def close(e, h):
             cols = slice(h * P, (h + 1) * P)
-            multiply(acc[e, h][:], w_codes[e][:, 2, cols], w_scales[e][:, 2, cols], e, 2, False, True)
-            activate(e, h, acc[e, h][:])
+            closes = not WHOLE <= e < E - 2
+            multiply(acc[e, h], w_codes[e][:, 2, cols], w_scales[e][:, 2, cols], e, 2, False, closes)
+            if e == E - 2:
+                for done in range(WHOLE, E - 1):
+                    activate(done, h, acc[done, h])
+            elif closes:
+                activate(e, h, acc[e, h])
 
         def end_expert(e):
             if e > busy:
@@ -218,10 +221,11 @@ def tile_moe_pkd_lin_gelu_kernel(
                     gather(paced[e, h][0], paced[e, h][1], ring, "pace%d_%d" % (e, h))
 
         nc.sync.dma_start(slot_list[:], offs)
-        load_token_words(0)
-        load_token_words(1)
-        load_whole(0, 2, False)
-        load_token_words(2)
+        nc.sync.dma_start(
+            token_words[:, 0 : PASSES * T].rearrange("p (o t) -> p o t", o=PASSES),
+            x_words.rearrange("o p t r -> p o (t r)").bitcast(I32),
+        )
+        load_whole(0, 2, 2)
         for q in range(4):
             nc.sync.dma_start(
                 token_scales[32 * q : 32 * q + 4 * PASSES, 0:T].bitcast(I32),
@@ -247,7 +251,8 @@ def tile_moe_pkd_lin_gelu_kernel(
 
         begin_expert(0)
         for e in range(1, WHOLE):
-            load_whole(PASSES * e - 1, PASSES, True)
+            if e % 2:
+                load_whole(PASSES * e - 1, PASSES * min(2, WHOLE - e), 2 * PASSES if e < PAIRED else PASSES)
             end_expert(e - 1)
             begin_expert(e)
         place_halves(0, [(WHOLE, 0), (WHOLE, 1)])
@@ -271,10 +276,8 @@ def tile_moe_pkd_lin_gelu_kernel(
             nc.sync.dma_start(back[r][:], pos)
 
         todo = [(e, o) for e in range(WHOLE, E) for o in range(PASSES)]
-        steps = [todo[0:1]] + [todo[i : i + 2] for i in range(1, len(todo) - 1, 2)] + [todo[-1:]]
-        if len(todo) % 2:
-            steps = [todo[0:1]] + [todo[i : i + 2] for i in range(1, len(todo) - 2, 2)] + [todo[-2:-1], todo[-1:]]
-        held = {1: "part1", 3: "part2", len(steps) - 1: "part3"}
+        steps = [todo[0:1], todo[1:5], todo[5:9], todo[9:11], todo[11:12]]
+        held = {1: "part2", len(steps) - 1: "part3"}
         rest = psum.tile([P, SPLIT * C], F32, name="rest", tag="bank")
         for s, step in enumerate(steps):
             load_halves(1, step)
@@ -284,11 +287,9 @@ def tile_moe_pkd_lin_gelu_kernel(
             codes = keep.tile([P, count, P], U32, name="rest_codes%d" % s, align_bytes=64)
             scales = keep.tile([P, count, P], U8, name="rest_scales%d" % s, align_bytes=64)
             chunk = raw[step[0] + (1,)][0]
-            if s < 3:
-                interleave(nc.scalar.copy, side[:], chunk)
-            else:
-                for i in range(count):
-                    interleave(nc.scalar.copy, side[:, i : i + 1, :, :], chunk[:, i : i + 1, :, :])
+            piece = 2 if s == 1 else 1
+            for i in range(0, count, piece):
+                interleave(nc.scalar.copy, side[:, i : i + piece, :, :], chunk[:, i : i + piece, :, :])
             quantize(codes[:], scales[:], side[:])
             for i, (e, o) in enumerate(step):
                 cols = slice((e - WHOLE) * C, (e - WHOLE + 1) * C)

@@ -25,11 +25,11 @@ PASSES = K // K_PASS
 HALVES = N // P
 GROUP = 4
 WINDOW = 704
-AHEAD = 8
-PAIRED = 11
+AHEAD = 9
+PAIRED = 13
 BANK = 512
 ALIGN = 256
-RELIEF = 2
+RELIEF = 5
 LATE = 192
 RAW_BUFS = 3
 SHARE = 128
@@ -302,21 +302,24 @@ def tile_moe_pkd_lin_gelu_kernel(
             rows = slice(h * P, (h + 1) * P)
             summed = TOP if h < HALVES - 1 else TOP - 1
             turned = [psum.tile([P, P], F32, name="turned", tag="bank") for c in range(blocks)]
-            for r in range(summed):
-                part = ring.tile([P, T], F32, name="part", tag="part%d" % r, align_bytes=64)
-                for cols in pieces if (h, r) == (HALVES - 1, summed - 1) else (slice(0, T),):
-                    picks = back[r][:, cols.start // 16 : cols.stop // 16]
-                    factor = planes[:, r * T + cols.start : r * T + cols.stop]
-                    nc.vector.tensor_tensor(part[:, cols], y[h][:].indirect(picks), factor, MULT)
-                    for c in range(cols.start // P, cols.stop // P):
-                        nc.tensor.matmul(
-                            turned[c][:],
-                            lhsT=part[:, c * P : (c + 1) * P],
-                            rhs=identity[:],
-                            start=(r == 0),
-                            stop=(r == summed - 1),
-                            is_transpose=True,
-                        )
+            parts = [ring.tile([P, T], F32, name="part", tag="part%d" % r, align_bytes=64) for r in range(summed)]
+            if summed == TOP:
+                turns = [(r, slice(0, T)) for r in range(TOP)]
+            else:
+                turns = [(0, slice(0, T))] + [(r, cols) for cols in pieces for r in range(1, summed)]
+            for r, cols in turns:
+                picks = back[r][:, cols.start // 16 : cols.stop // 16]
+                factor = planes[:, r * T + cols.start : r * T + cols.stop]
+                nc.vector.tensor_tensor(parts[r][:, cols], y[h][:].indirect(picks), factor, MULT)
+                for c in range(cols.start // P, cols.stop // P):
+                    nc.tensor.matmul(
+                        turned[c][:],
+                        lhsT=parts[r][:, c * P : (c + 1) * P],
+                        rhs=identity[:],
+                        start=(r == 0),
+                        stop=(r == summed - 1),
+                        is_transpose=True,
+                    )
             by_token = keep.tile([P, blocks, P], F32, name="by_token%d" % h)
             total = keep.tile([P, T], F32, name="total%d" % h, align_bytes=ALIGN)
             sums = []

@@ -232,8 +232,8 @@ def tile_moe_pkd_lin_gelu_kernel(
                 x_scales[:, 4 * q : 4 * q + 4, :].bitcast(I32),
             )
         spaced = gate.rearrange("r n t -> (r n t)").rearrange("(q s) -> q s", q=TOP * blocks)
-        nc.sync.dma_start(gate_rows[0 : TOP * blocks, :], spaced[:, 0:P])
-        nc.sync.dma_start(bias[:, :, 0:E], b.rearrange("(h p) e -> p h e", p=P))
+        nc.scalar.dma_start(gate_rows[0 : TOP * blocks, :], spaced[:, 0:P])
+        nc.scalar.dma_start(bias[:, :, 0:E], b.rearrange("(h p) e -> p h e", p=P))
         for g, sort in every_gather[:AHEAD]:
             gather(g, sort, keep, "first%d_%d" % (g, sort))
 
@@ -288,8 +288,9 @@ def tile_moe_pkd_lin_gelu_kernel(
             scales = keep.tile([P, count, P], U8, name="rest_scales%d" % s, align_bytes=64)
             chunk = raw[step[0] + (1,)][0]
             piece = 2 if s == 1 else 1
+            copy = nc.vector.tensor_copy if s == len(steps) - 1 else nc.scalar.copy
             for i in range(0, count, piece):
-                interleave(nc.scalar.copy, side[:, i : i + piece, :, :], chunk[:, i : i + piece, :, :])
+                interleave(copy, side[:, i : i + piece, :, :], chunk[:, i : i + piece, :, :])
             quantize(codes[:], scales[:], side[:])
             for i, (e, o) in enumerate(step):
                 cols = slice((e - WHOLE) * C, (e - WHOLE + 1) * C)

@@ -15,6 +15,7 @@ U16 = mybir.dt.uint16
 U8 = mybir.dt.uint8
 FP8X4 = mybir.dt.float8_e4m3fn_x4
 GELU = mybir.ActivationFunctionType.Gelu_apprx_tanh
+COPY = mybir.ActivationFunctionType.Copy
 MULT = mybir.AluOpType.mult
 ADD = mybir.AluOpType.add
 
@@ -23,19 +24,15 @@ PACK = 4
 K_PASS = P * PACK
 PASSES = K // K_PASS
 HALVES = N // P
-GROUP = 4
-WINDOW = 704
-AHEAD = 9
-PAIRED = 13
+BLOCKS = T // P
 BANK = 512
 ALIGN = 256
-RELIEF = 5
-LATE = 192
-RAW_BUFS = 3
-SHARE = 128
-SPLIT = 4
+KIB = 1024
+SLOTS = E * C // 2
+WINDOW = 1728
+SPLIT = 6
 WHOLE = E - SPLIT
-ROOM = 2 * PASSES * PACK * N
+Z0, Z1, Z2, Z3 = 0, 41 * KIB, 77 * KIB, 101 * KIB
 
 
 def tile_moe_pkd_lin_gelu_kernel(
@@ -44,203 +41,153 @@ def tile_moe_pkd_lin_gelu_kernel(
     nc = tc.nc
     with ExitStack() as ctx:
         keep = ctx.enter_context(tc.tile_pool(name="keep", bufs=1))
-        stream = ctx.enter_context(tc.tile_pool(name="stream", bufs=RAW_BUFS))
-        work = ctx.enter_context(tc.tile_pool(name="work", bufs=3))
-        ring = ctx.enter_context(tc.tile_pool(name="ring", bufs=1))
+        room = ctx.enter_context(tc.tile_pool(name="room", bufs=1))
+        sides = ctx.enter_context(tc.tile_pool(name="sides", bufs=5))
+        coded = ctx.enter_context(tc.tile_pool(name="coded", bufs=4))
         psum = ctx.enter_context(tc.psum_pool(name="psum", bufs=8))
 
+        def place(shape, name, offset):
+            return room.tile(shape, F32, name=name, offset=offset, align_bytes=ALIGN)
+
+        gate_rows = keep.tile([P, P], F32, name="gate_rows")
+        nc.vector.memset(gate_rows[:], 0.0)
         token_scales = keep.tile([P, WINDOW], U8, name="token_scales")
         nc.gpsimd.memset(token_scales[:].bitcast(I32), 0)
-        blocks = T // P
-        gate_rows = keep.tile([P, P], F32, name="gate_rows")
-        nc.gpsimd.memset(gate_rows[:], 0.0)
+        token_words = keep.tile([P, (PASSES - 1) * T + WINDOW], I32, name="token_words", align_bytes=ALIGN)
+        nc.vector.memset(token_words[:, PASSES * T :], 0)
         bias = keep.tile([P, HALVES, 24], F32, name="bias")
         identity = keep.tile([P, P], F32, name="identity")
         make_identity(nc, identity[:])
-
         slot_list = keep.tile([P, E * C // 16], U16, name="slot_list")
-        token_words = keep.tile([P, (PASSES - 1) * T + WINDOW], I32, name="token_words", align_bytes=ALIGN)
-        nc.vector.memset(token_words[:, PASSES * T :], 0)
 
         w_rows = w.rearrange("e k n -> (e k) n")
-        raw = {}
+        w_by_row = w.rearrange("e (o p j) n -> j p (e o) n", p=P, j=PACK)
 
-        def load_whole(first, count, step):
-            chunk = stream.tile([P, count, PACK, N], F32, name="chunk", tag="stream", align_bytes=ALIGN)
+        def load_whole(first, count, offset):
+            chunk = place([P, count, PACK, N], "chunk%d" % first, offset)
             src = w_rows[first * K_PASS : (first + count) * K_PASS, :].rearrange("(o p j) n -> p o (j n)", p=P, j=PACK)
-            dst = chunk[:].rearrange("p o j n -> p o (j n)")
-            for i in range(0, count, step):
-                nc.sync.dma_start(dst[:, i : i + step, :], src[:, i : i + step, :])
-            for i in range(count):
-                raw[divmod(first + i, PASSES)] = (chunk, i)
+            nc.sync.dma_start(chunk[:].rearrange("p o j n -> p o (j n)"), src)
+            return chunk
 
-        room = [None, ROOM]
+        def load_group(h, count, offset):
+            group = place([P, PACK, count, P], "group%d" % h, offset)
+            first = WHOLE * PASSES
+            for j in range(PACK):
+                nc.sync.dma_start(group[:, j, :, :], w_by_row[j][:, first : first + count, h * P : (h + 1) * P])
+            return group
 
-        def take(columns):
-            if room[1] + columns > ROOM:
-                room[0:2] = [stream.tile([P, ROOM], F32, name="small", tag="stream", align_bytes=ALIGN), 0]
-            room[1:2] = [room[1] + columns]
-            return room[0][:, room[1] - columns : room[1]]
+        def whole_keys(first, count):
+            return [divmod(g, PASSES) + (h,) for g in range(first, first + count) for h in range(HALVES)]
 
-        def place_halves(h, which):
-            place = take(len(which) * K_PASS).rearrange("p (o j n) -> p o j n", j=PACK, n=P)
-            for i, (e, o) in enumerate(which):
-                raw[e, o, h] = (place, i)
+        def half_keys(h, first, count):
+            return [divmod(WHOLE * PASSES + i, PASSES) + (h,) for i in range(first, first + count)]
 
-        def load_half(e, o, h):
-            rows = w[e, o * K_PASS : (o + 1) * K_PASS, h * P : (h + 1) * P]
-            place, i = raw[e, o, h]
-            nc.sync.dma_start(place[:, i, :, :], rows.rearrange("(p j) n -> p j n", j=PACK))
+        def by_pass(src):
+            return src.rearrange("p o t (c i) -> p o c t i", i=2)
 
-        def load_halves(h, which):
-            place_halves(h, which)
-            for e, o in which:
-                load_half(e, o, h)
+        def by_row(src):
+            return src.rearrange("p t o (c i) -> p o c t i", i=2)
 
-        def raw_passes(key, count, cols):
-            chunk, i = raw[key]
-            return chunk[:, i : i + count, :, cols]
+        def round_and_weave(copy, src, keys, offset=None):
+            if offset is None:
+                side = sides.tile([P, len(keys) * P * PACK], BF16, name="side", align_bytes=64)
+            else:
+                side = room.tile([P, len(keys) * P * PACK], BF16, name="side%d" % offset, offset=offset, align_bytes=ALIGN)
+            copy(side[:].rearrange("p (o c i t) -> p o c t i", o=src.shape[1], i=2, t=PACK), src)
+            return side, keys
 
+        y = [place([P, E * C], "y%d" % h, Z2 + h * E * C * 4) for h in range(HALVES)]
         slot_words = {}
         slot_scales = {}
+        banks = {}
 
-        def gather(g, sort, pool, tag):
-            if sort == PASSES:
-                dst = pool.tile([P, GROUP * C], U8, name="slot_scales", tag=tag, align_bytes=64)
-                slot_scales[g] = dst
-                window = token_scales[:]
-            else:
-                dst = pool.tile([P, GROUP * C], U32, name="slot_words", tag=tag, align_bytes=64)
-                slot_words[g, sort] = dst
-                window = token_words[:, sort * T : sort * T + WINDOW].bitcast(U32)
-            cols = slot_list[:, g * GROUP * C // 16 : (g + 1) * GROUP * C // 16]
-            nc.vector.tensor_copy(dst[:], window.indirect(cols))
+        def share_bank(results):
+            bank = psum.tile([P, len(results) * C], F32, name="acc", tag="bank")
+            entry = [bank, results, len(results) * PASSES]
+            for result in results:
+                banks[result] = entry
 
-        every_gather = [(g, sort) for g in range(E // GROUP) for sort in range(PASSES + 1)]
-        later = every_gather[AHEAD:]
-        places = [(e, 0) for e in range(E)]
-        paced = dict(zip(places, later))
-        busy = max(e for e, h in paced)
-
-        def interleave(copy, dst, src):
-            copy(
-                dst.rearrange("p o (c i) t -> p o c t i", i=2),
-                src.rearrange("p o t (c i) -> p o c t i", i=2),
-            )
-
-        y = [keep.tile([P, E * C], F32, name="y%d" % h) for h in range(HALVES)]
-        acc = {}
-        shared = []
-
-        def quantize(codes, scales, side):
-            nc.vector.quantize_mx(
-                out=codes.rearrange("p o n -> p (o n)").bitcast(FP8X4),
-                scales=scales.rearrange("p o n -> p (o n)"),
-                in_=side.rearrange("p o n t -> p (o n t)"),
-            )
-
-        def multiply(bank, codes, scales, e, o, start, stop):
-            g, j = divmod(e, GROUP)
-            mine = slice(j * C, (j + 1) * C)
-            nc.tensor.matmul_mx(
-                out=bank,
-                lhsT=codes.bitcast(FP8X4),
-                lhsT_scale=scales,
-                rhs=slot_words[g, o][:, mine].bitcast(FP8X4),
-                rhs_scale=slot_scales[g][4 * o : P, mine],
-                start=start,
-                stop=stop,
-            )
-
-        def activate(e, h, bank):
-            nc.scalar.activation(y[h][:, e * C : (e + 1) * C], bank, GELU, bias=bias[:, h, e : e + 1])
-
-        w_codes = {}
-        w_scales = {}
-        last = slice(PASSES - 1, PASSES)
-
-        def begin_expert(e):
-            width = N if e < WHOLE else P
-            every = slice(0, width)
-            key = (e, 0) if e < WHOLE else (e, 0, 0)
-            w_codes[e] = work.tile([P, PASSES, width], U32, name="w_codes", align_bytes=64)
-            w_scales[e] = work.tile([P, PASSES, width], U8, name="w_scales", align_bytes=64)
-            side = work.tile([P, 2, width, PACK], BF16, name="side_s", align_bytes=64)
-            if WHOLE - RELIEF <= e < WHOLE:
-                interleave(nc.scalar.copy, side[:, :, 0:LATE, :], raw_passes(key, 2, slice(0, LATE)))
-                interleave(nc.vector.tensor_copy, side[:, :, LATE:N, :], raw_passes(key, 2, slice(LATE, N)))
-            else:
-                interleave(nc.scalar.copy, side[:], raw_passes(key, 2, every))
-            quantize(w_codes[e][:, 0:2, :], w_scales[e][:, 0:2, :], side[:])
-            for h in range(width // P):
-                cols = slice(h * P, (h + 1) * P)
-                if e == WHOLE:
-                    shared.append(psum.tile([P, (SPLIT - 1) * C], F32, name="shared", tag="bank"))
-                if WHOLE <= e < E - 1:
-                    acc[e, h] = shared[0][:, (e - WHOLE) * C : (e - WHOLE + 1) * C]
-                else:
-                    acc[e, h] = psum.tile([P, C], F32, name="acc", tag="bank")[:]
-                for o in range(2):
-                    opens = o == 0 and not WHOLE < e < E - 1
-                    multiply(acc[e, h], w_codes[e][:, o, cols], w_scales[e][:, o, cols], e, o, opens, False)
-
-        def close(e, h):
-            cols = slice(h * P, (h + 1) * P)
-            closes = not WHOLE <= e < E - 2
-            multiply(acc[e, h], w_codes[e][:, 2, cols], w_scales[e][:, 2, cols], e, 2, False, closes)
-            if e == E - 2:
-                for done in range(WHOLE, E - 1):
-                    activate(done, h, acc[done, h])
-            elif closes:
-                activate(e, h, acc[e, h])
-
-        def end_expert(e):
-            if e > busy:
-                width = N if e < WHOLE else P
-                side = work.tile([P, 1, width, PACK], BF16, name="side_w", align_bytes=64)
-                key = (e, 2) if e < WHOLE else (e, 2, 0)
-                interleave(nc.vector.tensor_copy, side[:], raw_passes(key, 1, slice(0, width)))
-                quantize(w_codes[e][:, last, :], w_scales[e][:, last, :], side[:])
-                for h in range(width // P):
-                    close(e, h)
-                return
-            sides = []
-            for h in range(HALVES):
-                if (e, h) in paced:
-                    sides.append(ring.tile([P, 1, P, PACK], BF16, name="side_p", tag="pace%d_%d" % (e, h), align_bytes=64))
-                else:
-                    sides.append(work.tile([P, 1, P, PACK], BF16, name="side_v", align_bytes=64))
-            interleave(nc.vector.tensor_copy, sides[0][:], raw_passes((e, 2), 1, slice(0, P)))
-            interleave(nc.vector.tensor_copy, sides[1][:, :, 0:SHARE, :], raw_passes((e, 2), 1, slice(P, P + SHARE)))
-            for h in range(HALVES):
-                cols = slice(h * P, (h + 1) * P)
-                quantize(w_codes[e][:, last, cols], w_scales[e][:, last, cols], sides[h][:])
-                close(e, h)
-            for h in range(HALVES):
-                if (e, h) in paced:
-                    gather(paced[e, h][0], paced[e, h][1], ring, "pace%d_%d" % (e, h))
+        def multiply(unit, codes=None):
+            side, keys = unit
+            if codes is None:
+                wide = {"tag": "wide", "bufs": 2} if len(keys) > 4 else {}
+                codes = coded.tile([P, len(keys) * P], U32, name="codes", align_bytes=64, **wide)
+            scales = coded.tile([P, len(keys) * P], U8, name="scales", align_bytes=64)
+            nc.vector.quantize_mx(out=codes[:].bitcast(FP8X4), scales=scales[:], in_=side[:])
+            for i, (e, o, h) in enumerate(keys):
+                entry = banks[e, h]
+                bank, results, left = entry
+                at = results.index((e, h)) * C
+                g, j = divmod(e * C, SLOTS)
+                nc.tensor.matmul_mx(
+                    out=bank[:, at : at + C],
+                    lhsT=codes[:, i * P : (i + 1) * P].bitcast(FP8X4),
+                    lhsT_scale=scales[:, i * P : (i + 1) * P],
+                    rhs=slot_words[g, o][:, j : j + C].bitcast(FP8X4),
+                    rhs_scale=slot_scales[g][4 * o : P, j : j + C],
+                    start=left == len(results) * PASSES,
+                    stop=left == 1,
+                )
+                entry[2:3] = [left - 1]
+                if left == 1:
+                    for n, (done, half) in enumerate(results):
+                        nc.scalar.activation(
+                            y[half][:, done * C : (done + 1) * C],
+                            bank[:, n * C : (n + 1) * C],
+                            GELU,
+                            bias=columns[half][:, done : done + 1],
+                        )
 
         nc.sync.dma_start(slot_list[:], offs)
         nc.sync.dma_start(
             token_words[:, 0 : PASSES * T].rearrange("p (o t) -> p o t", o=PASSES),
             x_words.rearrange("o p t r -> p o (t r)").bitcast(I32),
         )
-        load_whole(0, 2, 2)
+        spaced = gate.rearrange("r n t -> (r n t)").rearrange("(q s) -> q s", q=TOP * BLOCKS)
+        nc.sync.dma_start(gate_rows[0 : TOP * BLOCKS, :], spaced[:, 0:P])
+        early = [load_whole(0, 2, Z0), load_whole(2, 4, Z0 + 8 * KIB), load_whole(6, 6, Z1)]
         for q in range(4):
             nc.sync.dma_start(
                 token_scales[32 * q : 32 * q + 4 * PASSES, 0:T].bitcast(I32),
                 x_scales[:, 4 * q : 4 * q + 4, :].bitcast(I32),
             )
-        spaced = gate.rearrange("r n t -> (r n t)").rearrange("(q s) -> q s", q=TOP * blocks)
-        nc.scalar.dma_start(gate_rows[0 : TOP * blocks, :], spaced[:, 0:P])
-        nc.scalar.dma_start(bias[:, :, 0:E], b.rearrange("(h p) e -> p h e", p=P))
-        for g, sort in every_gather[:AHEAD]:
-            gather(g, sort, keep, "first%d_%d" % (g, sort))
+        nc.sync.dma_start(bias[:, :, 0:E], b.rearrange("(h p) e -> p h e", p=P))
+        first_bias = place([P, E], "first_bias", Z0 + 39 * KIB)
+        nc.vector.tensor_copy(first_bias[:], bias[:, 0, 0:E])
+        columns = (first_bias[:], bias[:, 1, :])
+        early.append(load_whole(12, 6, Z2))
+        back = []
+        for r, pos in enumerate((pos1, pos2, pos3, pos4)):
+            back.append(keep.tile([P, T // 16], U16, name="back%d" % r))
+            nc.sync.dma_start(back[r][:], pos)
 
-        by_row = psum.tile([P, P], F32, name="by_row", tag="bank")
-        nc.tensor.transpose(by_row[:], gate_rows[:], identity[:])
-        gate_cols = keep.tile([P, TOP * blocks], F32, name="gate_cols")
-        nc.scalar.copy(gate_cols[:], by_row[:, 0 : TOP * blocks])
+        for sort in range(PASSES + 1):
+            for g in range(2):
+                cols = slot_list[:, g * SLOTS // 16 : (g + 1) * SLOTS // 16]
+                if sort == PASSES:
+                    dst = keep.tile([P, SLOTS], U8, name="slot_scales%d" % g, align_bytes=64)
+                    slot_scales[g] = dst
+                    window = token_scales[:]
+                else:
+                    dst = keep.tile([P, SLOTS], U32, name="slot_words%d_%d" % (g, sort), align_bytes=64)
+                    slot_words[g, sort] = dst
+                    window = token_words[:, sort * T : sort * T + WINDOW].bitcast(U32)
+                nc.vector.tensor_copy(dst[:], window.indirect(cols))
+
+        units = []
+        first = 0
+        for chunk in early:
+            count = chunk.shape[1]
+            for i in range(0, count, 4):
+                n = min(4, count - i)
+                src = by_pass(chunk[:, i : i + n, :, :])
+                units.append(round_and_weave(nc.scalar.copy, src, whole_keys(first + i, n), Z3 + (first + i) * 2 * KIB))
+            first = first + count
+
+        turned_gate = psum.tile([P, P], F32, name="turned_gate", tag="bank")
+        nc.tensor.transpose(turned_gate[:], gate_rows[:], identity[:])
+        gate_cols = keep.tile([P, TOP * BLOCKS], F32, name="gate_cols")
+        nc.scalar.copy(gate_cols[:], turned_gate[:, 0 : TOP * BLOCKS])
         planes = keep.tile([P, TOP * T], F32, name="planes", align_bytes=ALIGN)
         for at in range(0, TOP * T, BANK):
             spread = psum.tile([P, BANK], F32, name="spread", tag="bank")
@@ -249,97 +196,129 @@ def tile_moe_pkd_lin_gelu_kernel(
                 nc.tensor.transpose(spread[:, j : j + P], gate_cols[:, q : q + 1].to_broadcast([P, P]), identity[:])
             nc.scalar.copy(planes[:, at : at + BANK], spread[:])
 
-        begin_expert(0)
-        for e in range(1, WHOLE):
-            if e % 2:
-                load_whole(PASSES * e - 1, PASSES * min(2, WHOLE - e), 2 * PASSES if e < PAIRED else PASSES)
-            end_expert(e - 1)
-            begin_expert(e)
-        place_halves(0, [(WHOLE, 0), (WHOLE, 1)])
-        load_half(WHOLE, 0, 0)
-        place = take(PACK * N).rearrange("p (o j n) -> p o j n", j=PACK, n=N)
-        raw[WHOLE - 1, 2] = (place, 0)
-        nc.sync.dma_start(place[:, 0, :, :], w[WHOLE - 1, 2 * K_PASS : K, :].rearrange("(p j) n -> p j n", j=PACK))
-        load_half(WHOLE, 1, 0)
-        end_expert(WHOLE - 1)
-        begin_expert(WHOLE)
-        for e in range(WHOLE + 1, E):
-            load_halves(0, [(e, 0), (e, 1), (e - 1, 2)])
-            end_expert(e - 1)
-            begin_expert(e)
-        load_halves(0, [(E - 1, 2)])
-        end_expert(E - 1)
+        for e in range(0, first // PASSES, 2):
+            share_bank([(e + i, h) for i in range(2) for h in range(HALVES)])
+        for unit in units:
+            multiply(unit)
 
-        back = []
-        for r, pos in enumerate((pos1, pos2, pos3, pos4)):
-            back.append(keep.tile([P, T // 16], U16, name="back%d" % r))
-            nc.sync.dma_start(back[r][:], pos)
+        group = load_group(0, SPLIT * PASSES, Z0)
+        for e in range(WHOLE, E, 3):
+            share_bank([(e + i, 0) for i in range(3)])
+        units = []
+        for copy, i, n in ((nc.vector.tensor_copy, 0, 4), (nc.vector.tensor_copy, 4, 4), (nc.vector.tensor_copy, 8, 2), (nc.scalar.copy, 10, 4), (nc.scalar.copy, 14, 4)):
+            units.append(round_and_weave(copy, by_row(group[:, :, i : i + n, :]), half_keys(0, i, n)))
+        for unit in units:
+            multiply(unit)
 
-        todo = [(e, o) for e in range(WHOLE, E) for o in range(PASSES)]
-        steps = [todo[0:1], todo[1:5], todo[5:9], todo[9:11], todo[11:12]]
-        held = {1: "part2", len(steps) - 1: "part3"}
-        rest = psum.tile([P, SPLIT * C], F32, name="rest", tag="bank")
-        for s, step in enumerate(steps):
-            load_halves(1, step)
-            count = len(step)
-            tag = held.get(s, "pace%d_%d" % places[s])
-            side = ring.tile([P, count, P, PACK], BF16, name="side_r", tag=tag, align_bytes=64)
-            codes = keep.tile([P, count, P], U32, name="rest_codes%d" % s, align_bytes=64)
-            scales = keep.tile([P, count, P], U8, name="rest_scales%d" % s, align_bytes=64)
-            chunk = raw[step[0] + (1,)][0]
-            piece = 2 if s == 1 else 1
-            copy = nc.vector.tensor_copy if s == len(steps) - 1 else nc.scalar.copy
-            for i in range(0, count, piece):
-                interleave(copy, side[:, i : i + piece, :, :], chunk[:, i : i + piece, :, :])
-            quantize(codes[:], scales[:], side[:])
-            for i, (e, o) in enumerate(step):
-                cols = slice((e - WHOLE) * C, (e - WHOLE + 1) * C)
-                multiply(rest[:, cols], codes[:, i, :], scales[:, i, :], e, o, (e, o) == todo[0], (e, o) == todo[-1])
-        for e in range(WHOLE, E):
-            activate(e, 1, rest[:, (e - WHOLE) * C : (e - WHOLE + 1) * C])
+        late = (
+            (7, Z1, (2, 2), (2, 1)),
+            (5, Z3, (2, 1), (2,)),
+            (4, Z3 + 20 * KIB, (2,), (2,)),
+            (3, Z0, (2,), (1,)),
+            (3, Z0 + 12 * KIB, (2,), (1,)),
+        )
+        for count, offset, mine, theirs in late:
+            chunk = load_whole(first, count, offset)
+            units = []
+            i = 0
+            for copy, sizes in ((nc.vector.tensor_copy, mine), (nc.scalar.copy, theirs)):
+                for n in sizes:
+                    units.append(round_and_weave(copy, by_pass(chunk[:, i : i + n, :, :]), whole_keys(first + i, n)))
+                    i = i + n
+            for g in range(first, first + count):
+                e, o = divmod(g, PASSES)
+                if o == 0 and e < WHOLE - 1:
+                    share_bank([(e, h) for h in range(HALVES)])
+                elif o == 0:
+                    for h in range(HALVES):
+                        share_bank([(e, h)])
+            for unit in units:
+                multiply(unit)
+            first = first + count
+        chunk = load_whole(first, 2, Z0 + 24 * KIB)
+        units = []
+        for h, copy in enumerate((nc.vector.tensor_copy, nc.scalar.copy)):
+            keys = [key for key in whole_keys(first, 2) if key[2] == h]
+            units.append(round_and_weave(copy, by_pass(chunk[:, :, :, h * P : (h + 1) * P]), keys))
+        for unit in units:
+            multiply(unit)
 
-        pieces = (slice(0, 3 * P), slice(3 * P, T))
-        for h in range(HALVES):
-            rows = slice(h * P, (h + 1) * P)
-            summed = TOP if h < HALVES - 1 else TOP - 1
-            turned = [psum.tile([P, P], F32, name="turned", tag="bank") for c in range(blocks)]
-            parts = [ring.tile([P, T], F32, name="part", tag="part%d" % r, align_bytes=64) for r in range(summed)]
-            if summed == TOP:
-                turns = [(r, slice(0, T)) for r in range(TOP)]
-            else:
-                turns = [(0, slice(0, T))] + [(r, cols) for cols in pieces for r in range(1, summed)]
-            for r, cols in turns:
-                picks = back[r][:, cols.start // 16 : cols.stop // 16]
-                factor = planes[:, r * T + cols.start : r * T + cols.stop]
-                nc.vector.tensor_tensor(parts[r][:, cols], y[h][:].indirect(picks), factor, MULT)
-                for c in range(cols.start // P, cols.stop // P):
+        singles = place([P, SPLIT * PASSES, PACK, P], "singles", Z1)
+        rest = [(e, o, 1) for e in range(WHOLE, E) for o in range(2)] + [(e, 2, 1) for e in range(WHOLE, E)]
+        for i, (e, o, h) in enumerate(rest):
+            rows = w[e, o * K_PASS : (o + 1) * K_PASS, h * P : (h + 1) * P]
+            nc.sync.dma_start(singles[:, i, :, :], rows.rearrange("(p j) n -> p j n", j=PACK))
+
+        def factor(r, cols):
+            return planes[:, r * T + cols.start : r * T + cols.stop]
+
+        def fetch(h, r, cols, part):
+            picks = back[r][:, cols.start // 16 : cols.stop // 16]
+            nc.vector.tensor_tensor(part, y[h][:].indirect(picks), factor(r, cols), MULT)
+
+        def add_up(parts, cols):
+            turned = psum.tile([P, cols.stop - cols.start], F32, name="turned", tag="bank")
+            blocks = range(cols.start, cols.stop, P)
+            for n, part in enumerate(parts):
+                for at in blocks:
                     nc.tensor.matmul(
-                        turned[c][:],
-                        lhsT=parts[r][:, c * P : (c + 1) * P],
+                        turned[:, at - cols.start : at - cols.start + P],
+                        lhsT=part[:, at : at + P],
                         rhs=identity[:],
-                        start=(r == 0),
-                        stop=(r == summed - 1),
+                        start=(n == 0 and at == blocks[0]),
+                        stop=(n == len(parts) - 1 and at == blocks[-1]),
                         is_transpose=True,
                     )
-            by_token = keep.tile([P, blocks, P], F32, name="by_token%d" % h)
-            total = keep.tile([P, T], F32, name="total%d" % h, align_bytes=ALIGN)
-            sums = []
-            for cols in pieces:
-                sums.append(psum.tile([P, cols.stop - cols.start], F32, name="sums", tag="bank"))
-                for c in range(cols.start // P, cols.stop // P):
-                    nc.scalar.copy(by_token[:, c, :], turned[c][:])
-                    at = c * P - cols.start
-                    nc.tensor.transpose(sums[-1][:, at : at + P], by_token[:, c, :], identity[:])
-            if summed == TOP:
-                for cols, bank in zip(pieces, sums):
-                    nc.scalar.copy(total[:, cols], bank[:])
-                nc.sync.dma_start(out[rows, :], total[:])
-            else:
-                part = keep.tile([P, T], F32, name="part_last")
-                for cols in pieces:
-                    picks = back[TOP - 1][:, cols.start // 16 : cols.stop // 16]
-                    factor = planes[:, (TOP - 1) * T + cols.start : (TOP - 1) * T + cols.stop]
-                    nc.vector.tensor_tensor(part[:, cols], y[h][:].indirect(picks), factor, MULT)
-                for cols, bank in zip(pieces, sums):
-                    nc.vector.tensor_tensor(total[:, cols], bank[:], part[:, cols], ADD)
-                    nc.sync.dma_start(out[rows, cols], total[:, cols])
+            return turned
+
+        def turn_back(turned, by_token, cols):
+            nc.scalar.copy(by_token[:, cols], turned[:])
+            sums = psum.tile([P, cols.stop - cols.start], F32, name="sums", tag="bank")
+            for at in range(cols.start, cols.stop, P):
+                nc.tensor.transpose(sums[:, at - cols.start : at - cols.start + P], by_token[:, at : at + P], identity[:])
+            return sums
+
+        pieces = (slice(0, 3 * P), slice(3 * P, T))
+        parts = [place([P, T], "part0_%d" % r, Z3 + r * T * 4) for r in range(TOP)]
+        for r in range(TOP):
+            fetch(0, r, slice(0, T), parts[r][:])
+        turned = [add_up(parts, cols) for cols in pieces]
+
+        for e in range(WHOLE, E, 2):
+            share_bank([(e, 1), (e + 1, 1)])
+        last_codes = room.tile([P, 2 * P], U32, name="last_codes", offset=Z0 + 36 * KIB, align_bytes=ALIGN)
+        for i in range(0, len(rest), 2):
+            copy = nc.vector.tensor_copy if i in (0, len(rest) - 2) else nc.scalar.copy
+            offset = Z0 + 39 * KIB if i == 2 else Z3 + 12 * KIB + i * KIB
+            unit = round_and_weave(copy, by_pass(singles[:, i : i + 2, :, :]), rest[i : i + 2], offset)
+            multiply(unit, last_codes if i == len(rest) - 4 else None)
+
+        by_token = place([P, T], "by_token0", Z0 + 36 * KIB)
+        first_sums = [turn_back(bank, by_token, cols) for cols, bank in zip(pieces, turned)]
+
+        parts = {r: place([P, T], "part1_%d" % r, Z0 + r * T * 4) for r in (0, 1, 3)}
+        plain = []
+        for cols in pieces:
+            picks = back[TOP - 1][:, cols.start // 16 : cols.stop // 16]
+            at = Z0 + 15 * KIB + cols.start * 4
+            plain.append(place([P, cols.stop - cols.start], "plain%d" % cols.start, at))
+            nc.scalar.activation(plain[-1][:], y[1][:].indirect(picks), COPY)
+
+        total = place([P, T], "total0", Z0 + 20 * KIB)
+        for cols, bank in zip(pieces, first_sums):
+            nc.scalar.copy(total[:, cols], bank[:])
+        nc.sync.dma_start(out[0:P, :], total[:])
+
+        by_token = place([P, T], "by_token1", Z0 + 10 * KIB)
+        total = place([P, T], "total1", Z0 + 10 * KIB + T * 4)
+        sums = []
+        for cols, values in zip(pieces, plain):
+            for r in (0, 1):
+                fetch(1, r, cols, parts[r][:, cols])
+            nc.vector.tensor_tensor(parts[3][:, cols], values[:], factor(3, cols), MULT)
+            sums.append(turn_back(add_up([parts[r] for r in (0, 1, 3)], cols), by_token, cols))
+        for cols, bank in zip(pieces, sums):
+            closing = place([P, cols.stop - cols.start], "closing%d" % cols.start, Z0 + 15 * KIB + cols.start * 4)
+            fetch(1, 2, cols, closing[:])
+            nc.vector.tensor_tensor(total[:, cols], bank[:], closing[:], ADD)
+            nc.sync.dma_start(out[P:N, cols], total[:, cols])

@@ -32,7 +32,8 @@ SLOTS = E * C // 2
 WINDOW = 1728
 SPLIT = 6
 WHOLE = E - SPLIT
-Z0, Z1, Z2, Z3 = 0, 41 * KIB, 77 * KIB, 101 * KIB
+GROUPED = 9
+Z0, Z1, Z2, Z3 = 0, 36 * KIB, 72 * KIB, 108 * KIB
 
 
 def tile_moe_pkd_lin_gelu_kernel(
@@ -42,7 +43,7 @@ def tile_moe_pkd_lin_gelu_kernel(
     with ExitStack() as ctx:
         keep = ctx.enter_context(tc.tile_pool(name="keep", bufs=1))
         room = ctx.enter_context(tc.tile_pool(name="room", bufs=1))
-        sides = ctx.enter_context(tc.tile_pool(name="sides", bufs=5))
+        sides = ctx.enter_context(tc.tile_pool(name="sides", bufs=6))
         coded = ctx.enter_context(tc.tile_pool(name="coded", bufs=4))
         psum = ctx.enter_context(tc.psum_pool(name="psum", bufs=8))
 
@@ -107,11 +108,9 @@ def tile_moe_pkd_lin_gelu_kernel(
             for result in results:
                 banks[result] = entry
 
-        def multiply(unit, codes=None):
+        def multiply(unit):
             side, keys = unit
-            if codes is None:
-                wide = {"tag": "wide", "bufs": 2} if len(keys) > 4 else {}
-                codes = coded.tile([P, len(keys) * P], U32, name="codes", align_bytes=64, **wide)
+            codes = coded.tile([P, len(keys) * P], U32, name="codes", align_bytes=64)
             scales = coded.tile([P, len(keys) * P], U8, name="scales", align_bytes=64)
             nc.vector.quantize_mx(out=codes[:].bitcast(FP8X4), scales=scales[:], in_=side[:])
             for i, (e, o, h) in enumerate(keys):
@@ -135,8 +134,10 @@ def tile_moe_pkd_lin_gelu_kernel(
                             y[half][:, done * C : (done + 1) * C],
                             bank[:, n * C : (n + 1) * C],
                             GELU,
-                            bias=columns[half][:, done : done + 1],
+                            bias=bias[:, half, done : done + 1],
                         )
+
+        vector, scalar = nc.vector.tensor_copy, nc.scalar.copy
 
         nc.sync.dma_start(slot_list[:], offs)
         nc.sync.dma_start(
@@ -145,17 +146,16 @@ def tile_moe_pkd_lin_gelu_kernel(
         )
         spaced = gate.rearrange("r n t -> (r n t)").rearrange("(q s) -> q s", q=TOP * BLOCKS)
         nc.sync.dma_start(gate_rows[0 : TOP * BLOCKS, :], spaced[:, 0:P])
-        early = [load_whole(0, 2, Z0), load_whole(2, 4, Z0 + 8 * KIB), load_whole(6, 6, Z1)]
+        group = load_group(0, SPLIT * PASSES, Z1)
         for q in range(4):
             nc.sync.dma_start(
                 token_scales[32 * q : 32 * q + 4 * PASSES, 0:T].bitcast(I32),
                 x_scales[:, 4 * q : 4 * q + 4, :].bitcast(I32),
             )
+        first = 9
+        chunk = load_whole(0, first, Z2)
         nc.sync.dma_start(bias[:, :, 0:E], b.rearrange("(h p) e -> p h e", p=P))
-        first_bias = place([P, E], "first_bias", Z0 + 39 * KIB)
-        nc.vector.tensor_copy(first_bias[:], bias[:, 0, 0:E])
-        columns = (first_bias[:], bias[:, 1, :])
-        early.append(load_whole(12, 6, Z2))
+        second = load_whole(first, 9, Z0)
         back = []
         for r, pos in enumerate((pos1, pos2, pos3, pos4)):
             back.append(keep.tile([P, T // 16], U16, name="back%d" % r))
@@ -175,14 +175,13 @@ def tile_moe_pkd_lin_gelu_kernel(
                 nc.vector.tensor_copy(dst[:], window.indirect(cols))
 
         units = []
-        first = 0
-        for chunk in early:
-            count = chunk.shape[1]
-            for i in range(0, count, 4):
-                n = min(4, count - i)
-                src = by_pass(chunk[:, i : i + n, :, :])
-                units.append(round_and_weave(nc.scalar.copy, src, whole_keys(first + i, n), Z3 + (first + i) * 2 * KIB))
-            first = first + count
+        for i in range(0, SPLIT * PASSES, 4):
+            n = min(4, SPLIT * PASSES - i)
+            units.append(round_and_weave(scalar, by_row(group[:, :, i : i + n, :]), half_keys(0, i, n), Z3 + i * KIB))
+        for i in range(0, first, 2):
+            n = min(2, first - i)
+            at = Z3 + (SPLIT * PASSES + 2 * i) * KIB
+            units.append(round_and_weave(scalar, by_pass(chunk[:, i : i + n, :, :]), whole_keys(i, n), at))
 
         turned_gate = psum.tile([P, P], F32, name="turned_gate", tag="bank")
         nc.tensor.transpose(turned_gate[:], gate_rows[:], identity[:])
@@ -196,129 +195,131 @@ def tile_moe_pkd_lin_gelu_kernel(
                 nc.tensor.transpose(spread[:, j : j + P], gate_cols[:, q : q + 1].to_broadcast([P, P]), identity[:])
             nc.scalar.copy(planes[:, at : at + BANK], spread[:])
 
-        for e in range(0, first // PASSES, 2):
-            share_bank([(e + i, h) for i in range(2) for h in range(HALVES)])
-        for unit in units:
-            multiply(unit)
-
-        group = load_group(0, SPLIT * PASSES, Z0)
-        for e in range(WHOLE, E, 3):
-            share_bank([(e + i, 0) for i in range(3)])
-        units = []
-        for copy, i, n in ((nc.vector.tensor_copy, 0, 4), (nc.vector.tensor_copy, 4, 4), (nc.vector.tensor_copy, 8, 2), (nc.scalar.copy, 10, 4), (nc.scalar.copy, 14, 4)):
-            units.append(round_and_weave(copy, by_row(group[:, :, i : i + n, :]), half_keys(0, i, n)))
+        for e in range(first // PASSES):
+            share_bank([(e, h) for h in range(HALVES)])
+        share_bank([(e, 0) for e in range(WHOLE, E - 2)])
+        share_bank([(e, 0) for e in range(E - 2, E)])
         for unit in units:
             multiply(unit)
 
         late = (
-            (7, Z1, (2, 2), (2, 1)),
-            (5, Z3, (2, 1), (2,)),
-            (4, Z3 + 20 * KIB, (2,), (2,)),
-            (3, Z0, (2,), (1,)),
-            (3, Z0 + 12 * KIB, (2,), (1,)),
+            (9, Z0, (2, 2, 1), (2, 2)),
+            (9, Z1, (2, 2, 1), (2, 2)),
+            (6, Z3, (2, 1), (2, 1)),
+            (4, Z0, (2,), (2,)),
+            (3, Z0 + 16 * KIB, (2,), (1,)),
         )
         for count, offset, mine, theirs in late:
-            chunk = load_whole(first, count, offset)
+            chunk = second if first == 9 else load_whole(first, count, offset)
             units = []
             i = 0
-            for copy, sizes in ((nc.vector.tensor_copy, mine), (nc.scalar.copy, theirs)):
+            for copy, sizes in ((vector, mine), (scalar, theirs)):
                 for n in sizes:
                     units.append(round_and_weave(copy, by_pass(chunk[:, i : i + n, :, :]), whole_keys(first + i, n)))
                     i = i + n
             for g in range(first, first + count):
                 e, o = divmod(g, PASSES)
-                if o == 0 and e < WHOLE - 1:
-                    share_bank([(e, h) for h in range(HALVES)])
-                elif o == 0:
+                if o == 0:
                     for h in range(HALVES):
                         share_bank([(e, h)])
             for unit in units:
                 multiply(unit)
             first = first + count
-        chunk = load_whole(first, 2, Z0 + 24 * KIB)
+        chunk = load_whole(first, 2, Z1)
         units = []
-        for h, copy in enumerate((nc.vector.tensor_copy, nc.scalar.copy)):
-            keys = [key for key in whole_keys(first, 2) if key[2] == h]
-            units.append(round_and_weave(copy, by_pass(chunk[:, :, :, h * P : (h + 1) * P]), keys))
+        for i in range(2):
+            units.append(round_and_weave(vector, by_pass(chunk[:, i : i + 1, :, 0:P]), whole_keys(first + i, 1)[0:1]))
+        units.append(round_and_weave(scalar, by_pass(chunk[:, :, :, P:N]), whole_keys(first, 2)[1::2]))
         for unit in units:
             multiply(unit)
 
-        singles = place([P, SPLIT * PASSES, PACK, P], "singles", Z1)
-        rest = [(e, o, 1) for e in range(WHOLE, E) for o in range(2)] + [(e, 2, 1) for e in range(WHOLE, E)]
-        for i, (e, o, h) in enumerate(rest):
+        rest = half_keys(1, 0, SPLIT * PASSES)
+        group = load_group(1, GROUPED, Z1 + 8 * KIB)
+        singles = place([P, len(rest) - GROUPED, PACK, P], "singles", Z3)
+        for i, (e, o, h) in enumerate(rest[GROUPED:]):
             rows = w[e, o * K_PASS : (o + 1) * K_PASS, h * P : (h + 1) * P]
             nc.sync.dma_start(singles[:, i, :, :], rows.rearrange("(p j) n -> p j n", j=PACK))
+
+        def picks(r, cols):
+            return back[r][:, cols.start // 16 : cols.stop // 16]
 
         def factor(r, cols):
             return planes[:, r * T + cols.start : r * T + cols.stop]
 
-        def fetch(h, r, cols, part):
-            picks = back[r][:, cols.start // 16 : cols.stop // 16]
-            nc.vector.tensor_tensor(part, y[h][:].indirect(picks), factor(r, cols), MULT)
-
-        def add_up(parts, cols):
-            turned = psum.tile([P, cols.stop - cols.start], F32, name="turned", tag="bank")
-            blocks = range(cols.start, cols.stop, P)
-            for n, part in enumerate(parts):
-                for at in blocks:
-                    nc.tensor.matmul(
-                        turned[:, at - cols.start : at - cols.start + P],
-                        lhsT=part[:, at : at + P],
-                        rhs=identity[:],
-                        start=(n == 0 and at == blocks[0]),
-                        stop=(n == len(parts) - 1 and at == blocks[-1]),
-                        is_transpose=True,
-                    )
-            return turned
+        def add_turned(turned, part, cols, start, stop):
+            for c in range(cols.start // P, cols.stop // P):
+                nc.tensor.matmul(
+                    turned[c][:],
+                    lhsT=part[:, c * P : (c + 1) * P],
+                    rhs=identity[:],
+                    start=start,
+                    stop=stop,
+                    is_transpose=True,
+                )
 
         def turn_back(turned, by_token, cols):
-            nc.scalar.copy(by_token[:, cols], turned[:])
             sums = psum.tile([P, cols.stop - cols.start], F32, name="sums", tag="bank")
-            for at in range(cols.start, cols.stop, P):
-                nc.tensor.transpose(sums[:, at - cols.start : at - cols.start + P], by_token[:, at : at + P], identity[:])
+            for c in range(cols.start // P, cols.stop // P):
+                nc.scalar.copy(by_token[:, c, :], turned[c][:])
+                at = c * P - cols.start
+                nc.tensor.transpose(sums[:, at : at + P], by_token[:, c, :], identity[:])
             return sums
 
         pieces = (slice(0, 3 * P), slice(3 * P, T))
-        parts = [place([P, T], "part0_%d" % r, Z3 + r * T * 4) for r in range(TOP)]
-        for r in range(TOP):
-            fetch(0, r, slice(0, T), parts[r][:])
-        turned = [add_up(parts, cols) for cols in pieces]
+        tokens = slice(0, T)
+        wide = T * 4
+        turned = [psum.tile([P, P], F32, name="turned", tag="bank") for c in range(BLOCKS)]
+        plain = place([P, T], "plain0", Z0)
+        nc.scalar.activation(plain[:], y[0][:].indirect(picks(3, tokens)), COPY)
+        extra = place([P, T], "extra0", Z0 + 7 * wide)
+        nc.scalar.activation(extra[:, pieces[1]], y[0][:].indirect(picks(1, pieces[1])), COPY)
+        parts = {r: place([P, T], "part0_%d" % r, Z0 + (n + 1) * wide) for n, r in enumerate((0, 1, 3))}
+        parts[2] = parts[1]
+        for r, cols, values in ((0, tokens, None), (1, pieces[0], None), (3, tokens, plain), (2, pieces[1], None)):
+            values = y[0][:].indirect(picks(r, cols)) if values is None else values[:, cols]
+            nc.vector.tensor_tensor(parts[r][:, cols], values, factor(r, cols), MULT)
+            add_turned(turned, parts[r], cols, r == 0, False)
 
-        for e in range(WHOLE, E, 2):
-            share_bank([(e, 1), (e + 1, 1)])
-        last_codes = room.tile([P, 2 * P], U32, name="last_codes", offset=Z0 + 36 * KIB, align_bytes=ALIGN)
-        for i in range(0, len(rest), 2):
-            copy = nc.vector.tensor_copy if i in (0, len(rest) - 2) else nc.scalar.copy
-            offset = Z0 + 39 * KIB if i == 2 else Z3 + 12 * KIB + i * KIB
-            unit = round_and_weave(copy, by_pass(singles[:, i : i + 2, :, :]), rest[i : i + 2], offset)
-            multiply(unit, last_codes if i == len(rest) - 4 else None)
+        share_bank([(e, 1) for e in range(WHOLE, E - 2)])
+        for e in range(E - 2, E):
+            share_bank([(e, 1)])
+        held = Z3 + 20 * KIB
+        units = []
+        for i, n, copy in ((0, 4, scalar), (4, 4, vector), (8, 1, scalar)):
+            units.append(round_and_weave(copy, by_row(group[:, :, i : i + n, :]), rest[i : i + n]))
+        for i, n, copy, offset in ((0, 2, scalar, None), (2, 2, vector, None), (4, 2, scalar, None), (8, 1, vector, held - KIB), (6, 2, scalar, held)):
+            keys = rest[GROUPED + i : GROUPED + i + n]
+            units.append(round_and_weave(copy, by_pass(singles[:, i : i + n, :, :]), keys, offset))
+        for n in range(len(units)):
+            multiply(units[n])
 
-        by_token = place([P, T], "by_token0", Z0 + 36 * KIB)
-        first_sums = [turn_back(bank, by_token, cols) for cols, bank in zip(pieces, turned)]
+        part = place([P, T], "part0_held", held - KIB)
+        for r, cols, values in ((2, pieces[0], y[0][:].indirect(picks(2, pieces[0]))), (1, pieces[1], extra[:, pieces[1]])):
+            nc.vector.tensor_tensor(part[:, cols], values, factor(r, cols), MULT)
+            add_turned(turned, part, cols, False, True)
 
-        parts = {r: place([P, T], "part1_%d" % r, Z0 + r * T * 4) for r in (0, 1, 3)}
-        plain = []
+        plain = place([P, T], "plain1", Z0 + 4 * wide)
         for cols in pieces:
-            picks = back[TOP - 1][:, cols.start // 16 : cols.stop // 16]
-            at = Z0 + 15 * KIB + cols.start * 4
-            plain.append(place([P, cols.stop - cols.start], "plain%d" % cols.start, at))
-            nc.scalar.activation(plain[-1][:], y[1][:].indirect(picks), COPY)
+            nc.scalar.activation(plain[:, cols], y[1][:].indirect(picks(2, cols)), COPY)
 
-        total = place([P, T], "total0", Z0 + 20 * KIB)
-        for cols, bank in zip(pieces, first_sums):
+        by_token = place([P, BLOCKS, P], "by_token0", Z0 + 5 * wide)
+        total = place([P, T], "total0", Z0 + 6 * wide)
+        sums = [turn_back(turned, by_token, cols) for cols in pieces]
+        for cols, bank in zip(pieces, sums):
             nc.scalar.copy(total[:, cols], bank[:])
         nc.sync.dma_start(out[0:P, :], total[:])
 
-        by_token = place([P, T], "by_token1", Z0 + 10 * KIB)
-        total = place([P, T], "total1", Z0 + 10 * KIB + T * 4)
-        sums = []
-        for cols, values in zip(pieces, plain):
-            for r in (0, 1):
-                fetch(1, r, cols, parts[r][:, cols])
-            nc.vector.tensor_tensor(parts[3][:, cols], values[:], factor(3, cols), MULT)
-            sums.append(turn_back(add_up([parts[r] for r in (0, 1, 3)], cols), by_token, cols))
+        turned = [psum.tile([P, P], F32, name="turned", tag="bank") for c in range(BLOCKS)]
+        parts = [place([P, T], "part1_%d" % r, Z1 + r * wide) for r in range(TOP)]
+        for r, cols in [(0, tokens)] + [(r, cols) for cols in pieces for r in (1, 2)]:
+            values = plain[:, cols] if r == 2 else y[1][:].indirect(picks(r, cols))
+            nc.vector.tensor_tensor(parts[r][:, cols], values, factor(r, cols), MULT)
+            add_turned(turned, parts[r], cols, r == 0, r == 2)
+        by_token = place([P, BLOCKS, P], "by_token1", Z1 + 4 * wide)
+        total = place([P, T], "total1", Z1 + 5 * wide)
+        sums = [turn_back(turned, by_token, cols) for cols in pieces]
+        for cols in pieces:
+            nc.vector.tensor_tensor(parts[3][:, cols], y[1][:].indirect(picks(3, cols)), factor(3, cols), MULT)
         for cols, bank in zip(pieces, sums):
-            closing = place([P, cols.stop - cols.start], "closing%d" % cols.start, Z0 + 15 * KIB + cols.start * 4)
-            fetch(1, 2, cols, closing[:])
-            nc.vector.tensor_tensor(total[:, cols], bank[:], closing[:], ADD)
+            nc.vector.tensor_tensor(total[:, cols], bank[:], parts[3][:, cols], ADD)
             nc.sync.dma_start(out[P:N, cols], total[:, cols])

@@ -30,11 +30,11 @@ ALIGN = 256
 KIB = 1024
 SLOTS = E * C // 2
 WINDOW = 1728
-SPLIT = 6
+SPLIT = 12
 WHOLE = E - SPLIT
-GROUPED = 9
-Z0, Z1, Z2, Z3 = 0, 36 * KIB, 72 * KIB, 108 * KIB
-
+GROUPS = (12, 9, 7)
+LATE_BANKS = (4, 5, 6, 6, 6, 7, 7, 7, 4, 5, 6, 7)
+ZA, ZB, ZC, ZD, ZE = 0, 24 * KIB, 44 * KIB, 80 * KIB, 116 * KIB
 
 def tile_moe_pkd_lin_gelu_kernel(
     tc, x_words, x_scales, w, b, gate, offs, pos1, pos2, pos3, pos4, out
@@ -45,10 +45,13 @@ def tile_moe_pkd_lin_gelu_kernel(
         room = ctx.enter_context(tc.tile_pool(name="room", bufs=1))
         sides = ctx.enter_context(tc.tile_pool(name="sides", bufs=6))
         coded = ctx.enter_context(tc.tile_pool(name="coded", bufs=4))
-        psum = ctx.enter_context(tc.psum_pool(name="psum", bufs=8))
+        psum = ctx.enter_context(tc.psum_pool(name="psum", bufs=1))
 
         def place(shape, name, offset):
             return room.tile(shape, F32, name=name, offset=offset, align_bytes=ALIGN)
+
+        def in_bank(width, name, number):
+            return psum.tile([P, width], F32, name=name, offset=number * BANK * 4)
 
         gate_rows = keep.tile([P, P], F32, name="gate_rows")
         nc.vector.memset(gate_rows[:], 0.0)
@@ -70,11 +73,11 @@ def tile_moe_pkd_lin_gelu_kernel(
             nc.sync.dma_start(chunk[:].rearrange("p o j n -> p o (j n)"), src)
             return chunk
 
-        def load_group(h, count, offset):
-            group = place([P, PACK, count, P], "group%d" % h, offset)
-            first = WHOLE * PASSES
+        def load_group(h, first, count, offset):
+            group = place([P, PACK, count, P], "group%d_%d" % (h, first), offset)
+            at = WHOLE * PASSES + first
             for j in range(PACK):
-                nc.sync.dma_start(group[:, j, :, :], w_by_row[j][:, first : first + count, h * P : (h + 1) * P])
+                nc.sync.dma_start(group[:, j, :, :], w_by_row[j][:, at : at + count, h * P : (h + 1) * P])
             return group
 
         def whole_keys(first, count):
@@ -89,21 +92,31 @@ def tile_moe_pkd_lin_gelu_kernel(
         def by_row(src):
             return src.rearrange("p t o (c i) -> p o c t i", i=2)
 
-        def round_and_weave(copy, src, keys, offset=None):
+        woven = {}
+
+        def weave(copy, src, keys, offset=None):
             if offset is None:
                 side = sides.tile([P, len(keys) * P * PACK], BF16, name="side", align_bytes=64)
             else:
                 side = room.tile([P, len(keys) * P * PACK], BF16, name="side%d" % offset, offset=offset, align_bytes=ALIGN)
             copy(side[:].rearrange("p (o c i t) -> p o c t i", o=src.shape[1], i=2, t=PACK), src)
+            woven[keys[0]] = side
             return side, keys
 
-        y = [place([P, E * C], "y%d" % h, Z2 + h * E * C * 4) for h in range(HALVES)]
+        y = [place([P, E * C], "y%d" % h, ZB + h * E * C * 4) for h in range(HALVES)]
         slot_words = {}
         slot_scales = {}
+        closed = []
+        seen = {}
         banks = {}
 
+        made = []
+
         def share_bank(results):
-            bank = psum.tile([P, len(results) * C], F32, name="acc", tag="bank")
+            e, h = results[0]
+            number = LATE_BANKS[e - WHOLE] if h == 1 and e >= WHOLE else (len(made) + 5) % 8
+            made.append(number)
+            bank = in_bank(len(results) * C, "acc%d_%d" % (e, h), number)
             entry = [bank, results, len(results) * PASSES]
             for result in results:
                 banks[result] = entry
@@ -113,7 +126,10 @@ def tile_moe_pkd_lin_gelu_kernel(
             codes = coded.tile([P, len(keys) * P], U32, name="codes", align_bytes=64)
             scales = coded.tile([P, len(keys) * P], U8, name="scales", align_bytes=64)
             nc.vector.quantize_mx(out=codes[:].bitcast(FP8X4), scales=scales[:], in_=side[:])
+            seen[keys[0]] = codes
             for i, (e, o, h) in enumerate(keys):
+                if (e, h) not in banks:
+                    share_bank([(e, h)])
                 entry = banks[e, h]
                 bank, results, left = entry
                 at = results.index((e, h)) * C
@@ -129,13 +145,23 @@ def tile_moe_pkd_lin_gelu_kernel(
                 )
                 entry[2:3] = [left - 1]
                 if left == 1:
-                    for n, (done, half) in enumerate(results):
-                        nc.scalar.activation(
-                            y[half][:, done * C : (done + 1) * C],
-                            bank[:, n * C : (n + 1) * C],
-                            GELU,
-                            bias=bias[:, half, done : done + 1],
-                        )
+                    closed.append(entry)
+
+        def activate():
+            for bank, results, left in closed:
+                for n, (done, half) in enumerate(results):
+                    nc.scalar.activation(
+                        y[half][:, done * C : (done + 1) * C],
+                        bank[:, n * C : (n + 1) * C],
+                        GELU,
+                        bias=bias[:, half, done : done + 1],
+                    )
+            closed.clear()
+
+        def finish(units):
+            for unit in units:
+                multiply(unit)
+                activate()
 
         vector, scalar = nc.vector.tensor_copy, nc.scalar.copy
 
@@ -146,20 +172,19 @@ def tile_moe_pkd_lin_gelu_kernel(
         )
         spaced = gate.rearrange("r n t -> (r n t)").rearrange("(q s) -> q s", q=TOP * BLOCKS)
         nc.sync.dma_start(gate_rows[0 : TOP * BLOCKS, :], spaced[:, 0:P])
-        group = load_group(0, SPLIT * PASSES, Z1)
+        early = [(0, 4, load_whole(0, 4, ZA))]
         for q in range(4):
             nc.sync.dma_start(
                 token_scales[32 * q : 32 * q + 4 * PASSES, 0:T].bitcast(I32),
                 x_scales[:, 4 * q : 4 * q + 4, :].bitcast(I32),
             )
-        first = 9
-        chunk = load_whole(0, first, Z2)
+        early.append((4, 5, load_whole(4, 5, ZB)))
         nc.sync.dma_start(bias[:, :, 0:E], b.rearrange("(h p) e -> p h e", p=P))
-        second = load_whole(first, 9, Z0)
         back = []
         for r, pos in enumerate((pos1, pos2, pos3, pos4)):
             back.append(keep.tile([P, T // 16], U16, name="back%d" % r))
             nc.sync.dma_start(back[r][:], pos)
+        groups = [load_group(0, 0, 18, ZC), load_group(0, 18, 18, ZD)]
 
         for sort in range(PASSES + 1):
             for g in range(2):
@@ -174,69 +199,73 @@ def tile_moe_pkd_lin_gelu_kernel(
                     window = token_words[:, sort * T : sort * T + WINDOW].bitcast(U32)
                 nc.vector.tensor_copy(dst[:], window.indirect(cols))
 
-        units = []
-        for i in range(0, SPLIT * PASSES, 4):
-            n = min(4, SPLIT * PASSES - i)
-            units.append(round_and_weave(scalar, by_row(group[:, :, i : i + n, :]), half_keys(0, i, n), Z3 + i * KIB))
-        for i in range(0, first, 2):
-            n = min(2, first - i)
-            at = Z3 + (SPLIT * PASSES + 2 * i) * KIB
-            units.append(round_and_weave(scalar, by_pass(chunk[:, i : i + n, :, :]), whole_keys(i, n), at))
-
-        turned_gate = psum.tile([P, P], F32, name="turned_gate", tag="bank")
+        turned_gate = in_bank(P, "turned_gate", 7)
         nc.tensor.transpose(turned_gate[:], gate_rows[:], identity[:])
         gate_cols = keep.tile([P, TOP * BLOCKS], F32, name="gate_cols")
         nc.scalar.copy(gate_cols[:], turned_gate[:, 0 : TOP * BLOCKS])
         planes = keep.tile([P, TOP * T], F32, name="planes", align_bytes=ALIGN)
         for at in range(0, TOP * T, BANK):
-            spread = psum.tile([P, BANK], F32, name="spread", tag="bank")
+            spread = in_bank(BANK, "spread%d" % at, at // BANK)
             for j in range(0, BANK, P):
                 q = (at + j) // P
                 nc.tensor.transpose(spread[:, j : j + P], gate_cols[:, q : q + 1].to_broadcast([P, P]), identity[:])
             nc.scalar.copy(planes[:, at : at + BANK], spread[:])
 
-        for e in range(first // PASSES):
+        units = []
+        for first, count, chunk in early:
+            for i in range(0, count, 2):
+                n = min(2, count - i)
+                at = ZE + 2 * (first + i) * KIB
+                units.append(weave(scalar, by_pass(chunk[:, i : i + n, :, :]), whole_keys(first + i, n), at))
+        for e in range(3):
             share_bank([(e, h) for h in range(HALVES)])
-        share_bank([(e, 0) for e in range(WHOLE, E - 2)])
-        share_bank([(e, 0) for e in range(E - 2, E)])
         for unit in units:
             multiply(unit)
 
-        late = (
-            (9, Z0, (2, 2, 1), (2, 2)),
-            (9, Z1, (2, 2, 1), (2, 2)),
-            (6, Z3, (2, 1), (2, 1)),
-            (4, Z0, (2,), (2,)),
-            (3, Z0 + 16 * KIB, (2,), (1,)),
+        shares = (
+            ((scalar, 4), (scalar, 4), (scalar, 4), (vector, 4), (scalar, 2)),
+            ((vector, 4), (scalar, 4), (vector, 4), (vector, 2), (scalar, 4)),
         )
+        for g, group in enumerate(groups):
+            units = []
+            i = 0
+            for copy, n in shares[g]:
+                at = ZB + i * KIB if g == 0 and i < 8 else None
+                units.append(weave(copy, by_row(group[:, :, i : i + n, :]), half_keys(0, 18 * g + i, n), at))
+                i = i + n
+            multiply(units[0])
+            multiply(units[1])
+            activate()
+            finish(units[2:])
+
+        late = (
+            (6, ZA, (2, 1), (2, 1)),
+            (4, ZC, (2,), (2,)),
+            (3, ZC + 16 * KIB, (2,), (1,)),
+        )
+        first = 9
         for count, offset, mine, theirs in late:
-            chunk = second if first == 9 else load_whole(first, count, offset)
+            chunk = load_whole(first, count, offset)
             units = []
             i = 0
             for copy, sizes in ((vector, mine), (scalar, theirs)):
                 for n in sizes:
-                    units.append(round_and_weave(copy, by_pass(chunk[:, i : i + n, :, :]), whole_keys(first + i, n)))
+                    units.append(weave(copy, by_pass(chunk[:, i : i + n, :, :]), whole_keys(first + i, n)))
                     i = i + n
-            for g in range(first, first + count):
-                e, o = divmod(g, PASSES)
-                if o == 0:
-                    for h in range(HALVES):
-                        share_bank([(e, h)])
-            for unit in units:
-                multiply(unit)
+            finish(units)
             first = first + count
-        chunk = load_whole(first, 2, Z1)
+        chunk = load_whole(first, 2, ZC + 28 * KIB)
         units = []
         for i in range(2):
-            units.append(round_and_weave(vector, by_pass(chunk[:, i : i + 1, :, 0:P]), whole_keys(first + i, 1)[0:1]))
-        units.append(round_and_weave(scalar, by_pass(chunk[:, :, :, P:N]), whole_keys(first, 2)[1::2]))
-        for unit in units:
-            multiply(unit)
+            units.append(weave(vector, by_pass(chunk[:, i : i + 1, :, 0:P]), whole_keys(first + i, 1)[0:1]))
+        units.append(weave(scalar, by_pass(chunk[:, :, :, P:N]), whole_keys(first, 2)[1::2]))
+        finish(units)
 
         rest = half_keys(1, 0, SPLIT * PASSES)
-        group = load_group(1, GROUPED, Z1 + 8 * KIB)
-        singles = place([P, len(rest) - GROUPED, PACK, P], "singles", Z3)
-        for i, (e, o, h) in enumerate(rest[GROUPED:]):
+        starts = [sum(GROUPS[:g]) for g in range(len(GROUPS) + 1)]
+        groups = [load_group(1, starts[g], GROUPS[g], offset) for g, offset in enumerate((ZD, ZA, ZC))]
+        singles = place([P, len(rest) - starts[-1], PACK, P], "singles", ZC + 16 * KIB)
+        for i, (e, o, h) in enumerate(rest[starts[-1] :]):
             rows = w[e, o * K_PASS : (o + 1) * K_PASS, h * P : (h + 1) * P]
             nc.sync.dma_start(singles[:, i, :, :], rows.rearrange("(p j) n -> p j n", j=PACK))
 
@@ -246,80 +275,111 @@ def tile_moe_pkd_lin_gelu_kernel(
         def factor(r, cols):
             return planes[:, r * T + cols.start : r * T + cols.stop]
 
-        def add_turned(turned, part, cols, start, stop):
-            for c in range(cols.start // P, cols.stop // P):
-                nc.tensor.matmul(
-                    turned[c][:],
-                    lhsT=part[:, c * P : (c + 1) * P],
-                    rhs=identity[:],
-                    start=start,
-                    stop=stop,
-                    is_transpose=True,
-                )
-
-        def turn_back(turned, by_token, cols):
-            sums = psum.tile([P, cols.stop - cols.start], F32, name="sums", tag="bank")
-            for c in range(cols.start // P, cols.stop // P):
-                nc.scalar.copy(by_token[:, c, :], turned[c][:])
-                at = c * P - cols.start
-                nc.tensor.transpose(sums[:, at : at + P], by_token[:, c, :], identity[:])
-            return sums
-
         pieces = (slice(0, 3 * P), slice(3 * P, T))
         tokens = slice(0, T)
         wide = T * 4
-        turned = [psum.tile([P, P], F32, name="turned", tag="bank") for c in range(BLOCKS)]
-        plain = place([P, T], "plain0", Z0)
-        nc.scalar.activation(plain[:], y[0][:].indirect(picks(3, tokens)), COPY)
-        extra = place([P, T], "extra0", Z0 + 7 * wide)
-        nc.scalar.activation(extra[:, pieces[1]], y[0][:].indirect(picks(1, pieces[1])), COPY)
-        parts = {r: place([P, T], "part0_%d" % r, Z0 + (n + 1) * wide) for n, r in enumerate((0, 1, 3))}
-        parts[2] = parts[1]
-        for r, cols, values in ((0, tokens, None), (1, pieces[0], None), (3, tokens, plain), (2, pieces[1], None)):
-            values = y[0][:].indirect(picks(r, cols)) if values is None else values[:, cols]
+
+        def token_banks(name, first):
+            return [in_bank(cols.stop - cols.start, name + str(n), first + n) for n, cols in enumerate(pieces)]
+
+        def add_turned(turned, part, cols, start, stop):
+            for piece, bank in zip(pieces, turned):
+                for at in range(max(cols.start, piece.start), min(cols.stop, piece.stop), P):
+                    nc.tensor.matmul(
+                        bank[:, at - piece.start : at - piece.start + P],
+                        lhsT=part[:, at : at + P],
+                        rhs=identity[:],
+                        start=start and at == piece.start,
+                        stop=stop and at == min(cols.stop, piece.stop) - P,
+                        is_transpose=True,
+                    )
+
+        def turn_back(bank, by_token, cols, sums):
+            nc.scalar.copy(by_token[:, cols], bank[:])
+            for at in range(cols.start, cols.stop, P):
+                nc.tensor.transpose(sums[:, at - cols.start : at - cols.start + P], by_token[:, at : at + P], identity[:])
+        near, far = pieces
+        turned = token_banks("turned0_", 0)
+        plain = {r: place([P, T], "plain0_%d" % r, ZE + n * wide) for n, r in enumerate((1, 2, 3))}
+        parts = [place([P, T], "part0_%d" % r, ZE + (3 + r) * wide) for r in range(TOP)]
+        for r, cols in ((2, tokens), (3, tokens), (1, near)):
+            nc.scalar.activation(plain[r][:, cols], y[0][:].indirect(picks(r, cols)), COPY)
+        for r, cols, own in ((0, tokens, True), (2, tokens, False), (1, far, True), (3, tokens, False), (1, near, False)):
+            values = y[0][:].indirect(picks(r, cols)) if own else plain[r][:, cols]
             nc.vector.tensor_tensor(parts[r][:, cols], values, factor(r, cols), MULT)
-            add_turned(turned, parts[r], cols, r == 0, False)
+            for piece in pieces:
+                if cols.start <= piece.start < cols.stop:
+                    add_turned(turned, parts[r], piece, r == 0, (r, piece) in ((3, far), (1, near)))
 
-        share_bank([(e, 1) for e in range(WHOLE, E - 2)])
-        for e in range(E - 2, E):
-            share_bank([(e, 1)])
-        held = Z3 + 20 * KIB
-        units = []
-        for i, n, copy in ((0, 4, scalar), (4, 4, vector), (8, 1, scalar)):
-            units.append(round_and_weave(copy, by_row(group[:, :, i : i + n, :]), rest[i : i + n]))
-        for i, n, copy, offset in ((0, 2, scalar, None), (2, 2, vector, None), (4, 2, scalar, None), (8, 1, vector, held - KIB), (6, 2, scalar, held)):
-            keys = rest[GROUPED + i : GROUPED + i + n]
-            units.append(round_and_weave(copy, by_pass(singles[:, i : i + n, :, :]), keys, offset))
-        for n in range(len(units)):
-            multiply(units[n])
+        def grouped(copy, g, i, n, offset=None):
+            return weave(copy, by_row(groups[g][:, :, i : i + n, :]), rest[starts[g] + i : starts[g] + i + n], offset)
 
-        part = place([P, T], "part0_held", held - KIB)
-        for r, cols, values in ((2, pieces[0], y[0][:].indirect(picks(2, pieces[0]))), (1, pieces[1], extra[:, pieces[1]])):
-            nc.vector.tensor_tensor(part[:, cols], values, factor(r, cols), MULT)
-            add_turned(turned, part, cols, False, True)
+        def single(copy, i, n):
+            return weave(copy, by_pass(singles[:, i : i + n, :, :]), rest[starts[-1] + i : starts[-1] + i + n])
 
-        plain = place([P, T], "plain1", Z0 + 4 * wide)
-        for cols in pieces:
-            nc.scalar.activation(plain[:, cols], y[1][:].indirect(picks(2, cols)), COPY)
+        share_bank([(e, 1) for e in (10, 11, 12)])
+        share_bank([(e, 1) for e in (13, 14, 15)])
+        held = ZD + 24 * KIB
+        a = grouped(scalar, 0, 0, 2, held)
+        c = grouped(vector, 0, 2, 4)
+        d = grouped(scalar, 0, 8, 4)
+        multiply(a)
+        f = grouped(vector, 0, 6, 2)
+        by_token = place([P, T], "by_token0", held)
+        sums = token_banks("sums0_", 2)
+        for bank, cols, back_bank in zip(turned, pieces, sums):
+            turn_back(bank, by_token, cols, back_bank)
+        for unit in (c, f, d):
+            multiply(unit)
 
-        by_token = place([P, BLOCKS, P], "by_token0", Z0 + 5 * wide)
-        total = place([P, T], "total0", Z0 + 6 * wide)
-        sums = [turn_back(turned, by_token, cols) for cols in pieces]
+        a = grouped(scalar, 1, 4, 4)
+        c = grouped(vector, 1, 0, 4)
+        f = grouped(vector, 1, 8, 1)
+        activate()
+        for unit in (c, a, f):
+            multiply(unit)
+
+        a = grouped(scalar, 2, 4, 3)
+        c = grouped(vector, 2, 0, 4)
+        activate()
+        for unit in (c, a):
+            multiply(unit)
+        a = single(scalar, 0, 2)
+        c = single(vector, 2, 2)
+        d = single(scalar, 4, 1)
+        activate()
+        multiply(a)
+        f = single(vector, 5, 1)
+        multiply(c)
+        g = single(scalar, 6, 1)
+        activate()
+        multiply(d)
+        h = single(vector, 7, 1)
+        finish([f, g, h])
+
+        late_room = ZE
+        plain = {r: place([P, T], "plain1_%d" % r, late_room + n * wide) for n, r in enumerate((2, 3))}
+        parts = [place([P, T], "part1_%d" % r, late_room + (2 + r) * wide) for r in range(TOP)]
+        by_token = place([P, T], "by_token1", ZD + 27 * KIB)
+        total = place([P, T], "total1", ZD + 27 * KIB + wide)
+        fourth, fifth = slice(3 * P, 4 * P), slice(4 * P, T)
+        for r, cols in ((2, near), (3, near), (2, far), (3, fourth)):
+            nc.scalar.activation(plain[r][:, cols], y[1][:].indirect(picks(r, cols)), COPY)
+        first_total = place([P, T], "total0", ZA)
         for cols, bank in zip(pieces, sums):
-            nc.scalar.copy(total[:, cols], bank[:])
-        nc.sync.dma_start(out[0:P, :], total[:])
+            nc.scalar.copy(first_total[:, cols], bank[:])
+        nc.sync.dma_start(out[0:P, :], first_total[:])
 
-        turned = [psum.tile([P, P], F32, name="turned", tag="bank") for c in range(BLOCKS)]
-        parts = [place([P, T], "part1_%d" % r, Z1 + r * wide) for r in range(TOP)]
-        for r, cols in [(0, tokens)] + [(r, cols) for cols in pieces for r in (1, 2)]:
-            values = plain[:, cols] if r == 2 else y[1][:].indirect(picks(r, cols))
+        turned = token_banks("turned1_", 0)
+        order = ((0, near), (2, near), (0, far), (3, near), (3, fifth), (2, far), (3, fourth), (1, near), (1, far))
+        for r, cols in order:
+            values = plain[r][:, cols] if r in plain and cols != fifth else y[1][:].indirect(picks(r, cols))
             nc.vector.tensor_tensor(parts[r][:, cols], values, factor(r, cols), MULT)
-            add_turned(turned, parts[r], cols, r == 0, r == 2)
-        by_token = place([P, BLOCKS, P], "by_token1", Z1 + 4 * wide)
-        total = place([P, T], "total1", Z1 + 5 * wide)
-        sums = [turn_back(turned, by_token, cols) for cols in pieces]
-        for cols in pieces:
-            nc.vector.tensor_tensor(parts[3][:, cols], y[1][:].indirect(picks(3, cols)), factor(3, cols), MULT)
+            if r != 1:
+                add_turned(turned, parts[r], cols, r == 0, (r, cols) in ((3, near), (3, fourth)))
+        sums = token_banks("sums1_", 5)
+        for bank, cols, back_bank in zip(turned, pieces, sums):
+            turn_back(bank, by_token, cols, back_bank)
         for cols, bank in zip(pieces, sums):
-            nc.vector.tensor_tensor(total[:, cols], bank[:], parts[3][:, cols], ADD)
+            nc.vector.tensor_tensor(total[:, cols], bank[:], parts[1][:, cols], ADD)
             nc.sync.dma_start(out[P:N, cols], total[:, cols])

@@ -65,7 +65,7 @@ def tile_moe_pkd_lin_gelu_kernel(
         slot_list = keep.tile([P, E * C // 16], U16, name="slot_list")
 
         w_rows = w.rearrange("e k n -> (e k) n")
-        w_by_row = w.rearrange("e (o p j) n -> j p (e o) n", p=P, j=PACK)
+        w_by_row = w.rearrange("e (o r) n -> r (e o) n", r=K_PASS)
 
         def load_whole(first, count, offset):
             chunk = place([P, count, PACK, N], "chunk%d" % first, offset)
@@ -76,8 +76,7 @@ def tile_moe_pkd_lin_gelu_kernel(
         def load_group(h, first, count, offset):
             group = place([P, PACK, count, P], "group%d_%d" % (h, first), offset)
             at = WHOLE * PASSES + first
-            for j in range(PACK):
-                nc.sync.dma_start(group[:, j, :, :], w_by_row[j][:, at : at + count, h * P : (h + 1) * P])
+            nc.sync.dma_start(group[:].rearrange("p j o n -> p (j o) n"), w_by_row[:, at : at + count, h * P : (h + 1) * P])
             return group
 
         def whole_keys(first, count):

@@ -30,11 +30,11 @@ ALIGN = 256
 KIB = 1024
 SLOTS = E * C // 2
 WINDOW = 1728
-SPLIT = 12
+SPLIT = 11
 WHOLE = E - SPLIT
-GROUPS = (12, 9, 7)
-LATE_BANKS = (4, 5, 6, 6, 6, 7, 7, 7, 4, 5, 6, 7)
-ZA, ZB, ZC, ZD, ZE = 0, 24 * KIB, 44 * KIB, 80 * KIB, 116 * KIB
+LATE_BANKS = (4, 5, 5, 6, 7, 4, 5, 6, 6, 6, 7)
+ZA, ZB, ZC, ZD, ZE = 0, 36 * KIB, 56 * KIB, 92 * KIB, 128 * KIB
+
 
 def tile_moe_pkd_lin_gelu_kernel(
     tc, x_words, x_scales, w, b, gate, offs, pos1, pos2, pos3, pos4, out
@@ -76,7 +76,10 @@ def tile_moe_pkd_lin_gelu_kernel(
         def load_group(h, first, count, offset):
             group = place([P, PACK, count, P], "group%d_%d" % (h, first), offset)
             at = WHOLE * PASSES + first
-            nc.sync.dma_start(group[:].rearrange("p j o n -> p (j o) n"), w_by_row[:, at : at + count, h * P : (h + 1) * P])
+            src = w_by_row[:, at : at + count, h * P : (h + 1) * P]
+            if count == 1:
+                src = src.rearrange("(p j) o n -> p (j o) n", j=PACK)
+            nc.sync.dma_start(group[:].rearrange("p j o n -> p (j o) n"), src)
             return group
 
         def whole_keys(first, count):
@@ -89,7 +92,7 @@ def tile_moe_pkd_lin_gelu_kernel(
             return src.rearrange("p o t (c i) -> p o c t i", i=2)
 
         def by_row(src):
-            return src.rearrange("p t o (c i) -> p o c t i", i=2)
+            return src.rearrange("p t o (c i) -> p (o c) t i", i=2).unsqueeze(1)
 
         woven = {}
 
@@ -171,19 +174,19 @@ def tile_moe_pkd_lin_gelu_kernel(
         )
         spaced = gate.rearrange("r n t -> (r n t)").rearrange("(q s) -> q s", q=TOP * BLOCKS)
         nc.sync.dma_start(gate_rows[0 : TOP * BLOCKS, :], spaced[:, 0:P])
-        early = [(0, 4, load_whole(0, 4, ZA))]
+        early = [(0, 9, load_whole(0, 9, ZA))]
         for q in range(4):
             nc.sync.dma_start(
                 token_scales[32 * q : 32 * q + 4 * PASSES, 0:T].bitcast(I32),
                 x_scales[:, 4 * q : 4 * q + 4, :].bitcast(I32),
             )
-        early.append((4, 5, load_whole(4, 5, ZB)))
+        groups = [load_group(0, 0, 17, ZC)]
         nc.sync.dma_start(bias[:, :, 0:E], b.rearrange("(h p) e -> p h e", p=P))
         back = []
         for r, pos in enumerate((pos1, pos2, pos3, pos4)):
             back.append(keep.tile([P, T // 16], U16, name="back%d" % r))
             nc.sync.dma_start(back[r][:], pos)
-        groups = [load_group(0, 0, 18, ZC), load_group(0, 18, 18, ZD)]
+        groups.append(load_group(0, 17, 16, ZD))
 
         for sort in range(PASSES + 1):
             for g in range(2):
@@ -221,26 +224,29 @@ def tile_moe_pkd_lin_gelu_kernel(
         for unit in units:
             multiply(unit)
 
+        for first, last in ((9, 12), (12, 15), (15, 18), (18, 20)):
+            share_bank([(e, 0) for e in range(first, last)])
         shares = (
-            ((scalar, 4), (scalar, 4), (scalar, 4), (vector, 4), (scalar, 2)),
-            ((vector, 4), (scalar, 4), (vector, 4), (vector, 2), (scalar, 4)),
+            ((scalar, 4), (scalar, 4), (scalar, 3), (scalar, 3), (scalar, 3)),
+            ((vector, 4), (vector, 4), (scalar, 4), (vector, 4)),
         )
         for g, group in enumerate(groups):
             units = []
             i = 0
             for copy, n in shares[g]:
                 at = ZB + i * KIB if g == 0 and i < 8 else None
-                units.append(weave(copy, by_row(group[:, :, i : i + n, :]), half_keys(0, 18 * g + i, n), at))
+                units.append(weave(copy, by_row(group[:, :, i : i + n, :]), half_keys(0, 17 * g + i, n), at))
                 i = i + n
-            multiply(units[0])
-            multiply(units[1])
-            activate()
-            finish(units[2:])
+            if g == 0:
+                for unit in units:
+                    multiply(unit)
+        activate()
+        finish(units)
 
         late = (
-            (6, ZA, (2, 1), (2, 1)),
-            (4, ZC, (2,), (2,)),
-            (3, ZC + 16 * KIB, (2,), (1,)),
+            (7, ZA, (2, 2), (2, 1)),
+            (5, ZC, (2, 1), (2,)),
+            (3, ZD, (2,), (1,)),
         )
         first = 9
         for count, offset, mine, theirs in late:
@@ -253,20 +259,25 @@ def tile_moe_pkd_lin_gelu_kernel(
                     i = i + n
             finish(units)
             first = first + count
-        chunk = load_whole(first, 2, ZC + 28 * KIB)
-        units = []
-        for i in range(2):
-            units.append(weave(vector, by_pass(chunk[:, i : i + 1, :, 0:P]), whole_keys(first + i, 1)[0:1]))
-        units.append(weave(scalar, by_pass(chunk[:, :, :, P:N]), whole_keys(first, 2)[1::2]))
-        finish(units)
+        for count, offset in ((2, ZD + 12 * KIB), (1, ZA)):
+            chunk = load_whole(first, count, offset)
+            keys = whole_keys(first, count)
+            finish([weave(copy, by_pass(chunk[:, :, :, h * P : (h + 1) * P]), keys[h::HALVES]) for h, copy in enumerate((vector, scalar))])
+            first = first + count
 
         rest = half_keys(1, 0, SPLIT * PASSES)
-        starts = [sum(GROUPS[:g]) for g in range(len(GROUPS) + 1)]
-        groups = [load_group(1, starts[g], GROUPS[g], offset) for g, offset in enumerate((ZD, ZA, ZC))]
-        singles = place([P, len(rest) - starts[-1], PACK, P], "singles", ZC + 16 * KIB)
-        for i, (e, o, h) in enumerate(rest[starts[-1] :]):
-            rows = w[e, o * K_PASS : (o + 1) * K_PASS, h * P : (h + 1) * P]
-            nc.sync.dma_start(singles[:, i, :, :], rows.rearrange("(p j) n -> p j n", j=PACK))
+        sizes = (2, 5, 9, 6, 4, 3, 2, 1, 1)
+        starts = [sum(sizes[:g]) for g in range(len(sizes))]
+        places = [ZA + 4 * KIB + 2 * KIB * at for at in starts[:3]] + [ZC + 2 * KIB * (at - starts[3]) for at in starts[3:6]]
+        places = places + [ZD + 12 * KIB + 2 * KIB * (at - starts[6]) for at in starts[6:]]
+        groups = [load_group(1, at, n, offset) for at, n, offset in zip(starts, sizes, places)]
+
+        def grouped(copy, g, i, n):
+            return weave(copy, by_row(groups[g][:, :, i : i + n, :]), rest[starts[g] + i : starts[g] + i + n])
+
+        share_bank([(e, 1) for e in range(WHOLE + 1, WHOLE + 3)])
+        share_bank([(e, 1) for e in range(E - 4, E - 1)])
+        finish([grouped(scalar, 0, 0, 1), grouped(vector, 0, 1, 1)])
 
         def picks(r, cols):
             return back[r][:, cols.start // 16 : cols.stop // 16]
@@ -293,92 +304,85 @@ def tile_moe_pkd_lin_gelu_kernel(
                         is_transpose=True,
                     )
 
-        def turn_back(bank, by_token, cols, sums):
-            nc.scalar.copy(by_token[:, cols], bank[:])
+        def turn_back(bank, by_token, cols, sums, step):
             for at in range(cols.start, cols.stop, P):
+                if (at - cols.start) % step == 0:
+                    nc.scalar.copy(by_token[:, at : min(at + step, cols.stop)], bank[:, at - cols.start : min(at + step, cols.stop) - cols.start])
                 nc.tensor.transpose(sums[:, at - cols.start : at - cols.start + P], by_token[:, at : at + P], identity[:])
+
         near, far = pieces
         turned = token_banks("turned0_", 0)
-        plain = {r: place([P, T], "plain0_%d" % r, ZE + n * wide) for n, r in enumerate((1, 2, 3))}
-        parts = [place([P, T], "part0_%d" % r, ZE + (3 + r) * wide) for r in range(TOP)]
-        for r, cols in ((2, tokens), (3, tokens), (1, near)):
-            nc.scalar.activation(plain[r][:, cols], y[0][:].indirect(picks(r, cols)), COPY)
-        for r, cols, own in ((0, tokens, True), (2, tokens, False), (1, far, True), (3, tokens, False), (1, near, False)):
-            values = y[0][:].indirect(picks(r, cols)) if own else plain[r][:, cols]
+        plain = {r: place([P, T], "plain0_%d" % r, ZE + n * wide) for n, r in enumerate((2, 3))}
+        parts = [place([P, T], "part0_%d" % r, ZE + (2 + r) * wide) for r in range(TOP)]
+        for r in plain:
+            nc.scalar.activation(plain[r][:], y[0][:].indirect(picks(r, tokens)), COPY)
+        unit = grouped(scalar, 1, 0, 3)
+        for r, cols in ((0, tokens), (2, tokens), (1, near), (3, tokens), (1, far)):
+            values = plain[r][:, cols] if r in plain else y[0][:].indirect(picks(r, cols))
             nc.vector.tensor_tensor(parts[r][:, cols], values, factor(r, cols), MULT)
             for piece in pieces:
                 if cols.start <= piece.start < cols.stop:
-                    add_turned(turned, parts[r], piece, r == 0, (r, piece) in ((3, far), (1, near)))
-
-        def grouped(copy, g, i, n, offset=None):
-            return weave(copy, by_row(groups[g][:, :, i : i + n, :]), rest[starts[g] + i : starts[g] + i + n], offset)
-
-        def single(copy, i, n):
-            return weave(copy, by_pass(singles[:, i : i + n, :, :]), rest[starts[-1] + i : starts[-1] + i + n])
-
-        share_bank([(e, 1) for e in (10, 11, 12)])
-        share_bank([(e, 1) for e in (13, 14, 15)])
-        held = ZD + 24 * KIB
-        a = grouped(scalar, 0, 0, 2, held)
-        c = grouped(vector, 0, 2, 4)
-        d = grouped(scalar, 0, 8, 4)
-        multiply(a)
-        f = grouped(vector, 0, 6, 2)
-        by_token = place([P, T], "by_token0", held)
+                    add_turned(turned, parts[r], piece, r == 0, (r, piece) in ((3, near), (1, far)))
+        early_unit, unit = unit, grouped(vector, 1, 3, 2)
+        multiply(early_unit)
+        by_token = place([P, T], "by_token0", ZE + 6 * wide)
         sums = token_banks("sums0_", 2)
         for bank, cols, back_bank in zip(turned, pieces, sums):
-            turn_back(bank, by_token, cols, back_bank)
-        for unit in (c, f, d):
-            multiply(unit)
+            turn_back(bank, by_token, cols, back_bank, T)
+        finish([unit])
 
-        a = grouped(scalar, 1, 4, 4)
-        c = grouped(vector, 1, 0, 4)
-        f = grouped(vector, 1, 8, 1)
-        activate()
-        for unit in (c, a, f):
-            multiply(unit)
-
-        a = grouped(scalar, 2, 4, 3)
-        c = grouped(vector, 2, 0, 4)
-        activate()
-        for unit in (c, a):
-            multiply(unit)
-        a = single(scalar, 0, 2)
-        c = single(vector, 2, 2)
-        d = single(scalar, 4, 1)
-        activate()
-        multiply(a)
-        f = single(vector, 5, 1)
-        multiply(c)
-        g = single(scalar, 6, 1)
-        activate()
-        multiply(d)
-        h = single(vector, 7, 1)
-        finish([f, g, h])
-
-        late_room = ZE
-        plain = {r: place([P, T], "plain1_%d" % r, late_room + n * wide) for n, r in enumerate((2, 3))}
-        parts = [place([P, T], "part1_%d" % r, late_room + (2 + r) * wide) for r in range(TOP)]
-        by_token = place([P, T], "by_token1", ZD + 27 * KIB)
-        total = place([P, T], "total1", ZD + 27 * KIB + wide)
-        fourth, fifth = slice(3 * P, 4 * P), slice(4 * P, T)
-        for r, cols in ((2, near), (3, near), (2, far), (3, fourth)):
-            nc.scalar.activation(plain[r][:, cols], y[1][:].indirect(picks(r, cols)), COPY)
-        first_total = place([P, T], "total0", ZA)
+        shares = (((4, 1), (4,)), ((4,), (2,)), ((3,), (1,)), ((2,), (1,)), ((1,), (1,)))
+        for g, (mine, theirs) in enumerate(shares, 2):
+            units = []
+            i = 0
+            for copy, counts in ((vector, mine), (scalar, theirs)):
+                for n in counts:
+                    units.append(grouped(copy, g, i, n))
+                    i = i + n
+            activate()
+            for unit in units if g == 2 else units[::-1]:
+                multiply(unit)
+        units = [grouped(scalar, 7, 0, 1), grouped(vector, 8, 0, 1)]
+        first_total = place([P, T], "total0", places[7] - KIB // 2)
         for cols, bank in zip(pieces, sums):
             nc.scalar.copy(first_total[:, cols], bank[:])
         nc.sync.dma_start(out[0:P, :], first_total[:])
+        activate()
+        finish(units)
 
-        turned = token_banks("turned1_", 0)
+        late_room = ZE
+        plain = {r: place([P, T], "plain1_%d" % r, late_room + n * wide) for n, r in enumerate((1, 2, 3))}
+        parts = [place([P, T], "part1_%d" % r, late_room + (3 + r) * wide) for r in range(TOP)]
+        by_token = place([P, T], "by_token1", ZD)
+        total = place([P, T], "total1", ZD + wide)
+        fourth, fifth = slice(3 * P, 4 * P), slice(4 * P, T)
+        fetched = ((2, near), (3, near), (2, far), (3, fourth), (1, far))
+        for r, cols in fetched:
+            nc.scalar.activation(plain[r][:, cols], y[1][:].indirect(picks(r, cols)), COPY)
+
+        turned = [in_bank(P, "turned1_%d" % c, c) for c in range(BLOCKS)]
         order = ((0, near), (2, near), (0, far), (3, near), (3, fifth), (2, far), (3, fourth), (1, near), (1, far))
+        left = [TOP - 1] * BLOCKS
         for r, cols in order:
-            values = plain[r][:, cols] if r in plain and cols != fifth else y[1][:].indirect(picks(r, cols))
+            values = plain[r][:, cols] if (r, cols) in fetched else y[1][:].indirect(picks(r, cols))
             nc.vector.tensor_tensor(parts[r][:, cols], values, factor(r, cols), MULT)
-            if r != 1:
-                add_turned(turned, parts[r], cols, r == 0, (r, cols) in ((3, near), (3, fourth)))
+            for c in range(cols.start // P, cols.stop // P) if r != 1 else ():
+                nc.tensor.matmul(
+                    turned[c][:],
+                    lhsT=parts[r][:, c * P : (c + 1) * P],
+                    rhs=identity[:],
+                    start=left[c] == TOP - 1,
+                    stop=left[c] == 1,
+                    is_transpose=True,
+                )
+                left[c : c + 1] = [left[c] - 1]
         sums = token_banks("sums1_", 5)
-        for bank, cols, back_bank in zip(turned, pieces, sums):
-            turn_back(bank, by_token, cols, back_bank)
+        for c in (0, 1, 2, 4, 3):
+            cols = slice(c * P, (c + 1) * P)
+            n = 0 if c * P < far.start else 1
+            nc.scalar.copy(by_token[:, cols], turned[c][:])
+            at = c * P - pieces[n].start
+            nc.tensor.transpose(sums[n][:, at : at + P], by_token[:, cols], identity[:])
         for cols, bank in zip(pieces, sums):
             nc.vector.tensor_tensor(total[:, cols], bank[:], parts[1][:, cols], ADD)
             nc.sync.dma_start(out[P:N, cols], total[:, cols])

from contextlib import ExitStack

import concourse.mybir as mybir
from concourse.masks import make_identity

K, T, E, C, N = 1536, 640, 20, 128, 256
TOP = 4
FLOPS = 2 * E * C * K * N

F32 = mybir.dt.float32
BF16 = mybir.dt.bfloat16
I32 = mybir.dt.int32
U32 = mybir.dt.uint32
U16 = mybir.dt.uint16
U8 = mybir.dt.uint8
FP8X4 = mybir.dt.float8_e4m3fn_x4
GELU = mybir.ActivationFunctionType.Gelu_apprx_tanh
COPY = mybir.ActivationFunctionType.Copy
MULT = mybir.AluOpType.mult
ADD = mybir.AluOpType.add

P = 128
PACK = 4
K_PASS = P * PACK
PASSES = K // K_PASS
HALVES = N // P
BLOCKS = T // P
BANK = 512
ALIGN = 256
KIB = 1024
SLOTS = E * C // 2
WINDOW = 1728
SPLIT = 11
WHOLE = E - SPLIT
LATE_BANKS = (4, 5, 5, 6, 7, 4, 5, 6, 6, 6, 7)
ZA, ZB, ZC, ZD, ZE = 0, 36 * KIB, 56 * KIB, 92 * KIB, 128 * KIB


def tile_moe_pkd_lin_gelu_kernel(
    tc, x_words, x_scales, w, b, gate, offs, pos1, pos2, pos3, pos4, out
):
    nc = tc.nc
    with ExitStack() as ctx:
        keep = ctx.enter_context(tc.tile_pool(name="keep", bufs=1))
        room = ctx.enter_context(tc.tile_pool(name="room", bufs=1))
        sides = ctx.enter_context(tc.tile_pool(name="sides", bufs=6))
        coded = ctx.enter_context(tc.tile_pool(name="coded", bufs=4))
        psum = ctx.enter_context(tc.psum_pool(name="psum", bufs=1))

        def place(shape, name, offset):
            return room.tile(shape, F32, name=name, offset=offset, align_bytes=ALIGN)

        def in_bank(width, name, number):
            return psum.tile([P, width], F32, name=name, offset=number * BANK * 4)

        gate_rows = keep.tile([P, P], F32, name="gate_rows")
        nc.vector.memset(gate_rows[:], 0.0)
        token_scales = keep.tile([P, WINDOW], U8, name="token_scales")
        nc.gpsimd.memset(token_scales[:].bitcast(I32), 0)
        token_words = keep.tile([P, (PASSES - 1) * T + WINDOW], I32, name="token_words", align_bytes=ALIGN)
        nc.vector.memset(token_words[:, PASSES * T :], 0)
        bias = keep.tile([P, HALVES, 24], F32, name="bias")
        identity = keep.tile([P, P], F32, name="identity")
        make_identity(nc, identity[:])
        slot_list = keep.tile([P, E * C // 16], U16, name="slot_list")

        w_rows = w.rearrange("e k n -> (e k) n")
        w_by_row = w.rearrange("e (o r) n -> r (e o) n", r=K_PASS)

        def load_whole(first, count, offset):
            chunk = place([P, count, PACK, N], "chunk%d" % first, offset)
            src = w_rows[first * K_PASS : (first + count) * K_PASS, :].rearrange("(o p j) n -> p o (j n)", p=P, j=PACK)
            nc.sync.dma_start(chunk[:].rearrange("p o j n -> p o (j n)"), src)
            return chunk

        def load_group(h, first, count, offset):
            group = place([P, PACK, count, P], "group%d_%d" % (h, first), offset)
            at = WHOLE * PASSES + first
            src = w_by_row[:, at : at + count, h * P : (h + 1) * P]
            if count == 1:
                src = src.rearrange("(p j) o n -> p (j o) n", j=PACK)
            nc.sync.dma_start(group[:].rearrange("p j o n -> p (j o) n"), src)
            return group

        def whole_keys(first, count):
            return [divmod(g, PASSES) + (h,) for g in range(first, first + count) for h in range(HALVES)]

        def half_keys(h, first, count):
            return [divmod(WHOLE * PASSES + i, PASSES) + (h,) for i in range(first, first + count)]

        def by_pass(src):
            return src.rearrange("p o t (c i) -> p o c t i", i=2)

        def by_row(src):
            return src.rearrange("p t o (c i) -> p (o c) t i", i=2).unsqueeze(1)

        woven = {}

        def weave(copy, src, keys, offset=None):
            if offset is None:
                side = sides.tile([P, len(keys) * P * PACK], BF16, name="side", align_bytes=64)
            else:
                side = room.tile([P, len(keys) * P * PACK], BF16, name="side%d" % offset, offset=offset, align_bytes=ALIGN)
            copy(side[:].rearrange("p (o c i t) -> p o c t i", o=src.shape[1], i=2, t=PACK), src)
            woven[keys[0]] = side
            return side, keys

        y = [place([P, E * C], "y%d" % h, ZB + h * E * C * 4) for h in range(HALVES)]
        slot_words = {}
        slot_scales = {}
        closed = []
        seen = {}
        banks = {}

        made = []

        def share_bank(results):
            e, h = results[0]
            number = LATE_BANKS[e - WHOLE] if h == 1 and e >= WHOLE else (len(made) + 5) % 8
            made.append(number)
            bank = in_bank(len(results) * C, "acc%d_%d" % (e, h), number)
            entry = [bank, results, len(results) * PASSES]
            for result in results:
                banks[result] = entry

        def multiply(unit):
            side, keys = unit
            codes = coded.tile([P, len(keys) * P], U32, name="codes", align_bytes=64)
            scales = coded.tile([P, len(keys) * P], U8, name="scales", align_bytes=64)
            nc.vector.quantize_mx(out=codes[:].bitcast(FP8X4), scales=scales[:], in_=side[:])
            seen[keys[0]] = codes
            for i, (e, o, h) in enumerate(keys):
                if (e, h) not in banks:
                    share_bank([(e, h)])
                entry = banks[e, h]
                bank, results, left = entry
                at = results.index((e, h)) * C
                g, j = divmod(e * C, SLOTS)
                nc.tensor.matmul_mx(
                    out=bank[:, at : at + C],
                    lhsT=codes[:, i * P : (i + 1) * P].bitcast(FP8X4),
                    lhsT_scale=scales[:, i * P : (i + 1) * P],
                    rhs=slot_words[g, o][:, j : j + C].bitcast(FP8X4),
                    rhs_scale=slot_scales[g][4 * o : P, j : j + C],
                    start=left == len(results) * PASSES,
                    stop=left == 1,
                )
                entry[2:3] = [left - 1]
                if left == 1:
                    closed.append(entry)

        def activate():
            for bank, results, left in closed:
                for n, (done, half) in enumerate(results):
                    nc.scalar.activation(
                        y[half][:, done * C : (done + 1) * C],
                        bank[:, n * C : (n + 1) * C],
                        GELU,
                        bias=bias[:, half, done : done + 1],
                    )
            closed.clear()

        def finish(units):
            for unit in units:
                multiply(unit)
                activate()

        vector, scalar = nc.vector.tensor_copy, nc.scalar.copy

        nc.sync.dma_start(slot_list[:], offs)
        nc.sync.dma_start(
            token_words[:, 0 : PASSES * T].rearrange("p (o t) -> p o t", o=PASSES),
            x_words.rearrange("o p t r -> p o (t r)").bitcast(I32),
        )
        spaced = gate.rearrange("r n t -> (r n t)").rearrange("(q s) -> q s", q=TOP * BLOCKS)
        nc.sync.dma_start(gate_rows[0 : TOP * BLOCKS, :], spaced[:, 0:P])
        early = [(0, 9, load_whole(0, 9, ZA))]
        for q in range(4):
            nc.sync.dma_start(
                token_scales[32 * q : 32 * q + 4 * PASSES, 0:T].bitcast(I32),
                x_scales[:, 4 * q : 4 * q + 4, :].bitcast(I32),
            )
        groups = [load_group(0, 0, 17, ZC)]
        nc.sync.dma_start(bias[:, :, 0:E], b.rearrange("(h p) e -> p h e", p=P))
        back = []
        for r, pos in enumerate((pos1, pos2, pos3, pos4)):
            back.append(keep.tile([P, T // 16], U16, name="back%d" % r))
            nc.sync.dma_start(back[r][:], pos)
        groups.append(load_group(0, 17, 16, ZD))

        for sort in range(PASSES + 1):
            for g in range(2):
                cols = slot_list[:, g * SLOTS // 16 : (g + 1) * SLOTS // 16]
                if sort == PASSES:
                    dst = keep.tile([P, SLOTS], U8, name="slot_scales%d" % g, align_bytes=64)
                    slot_scales[g] = dst
                    window = token_scales[:]
                else:
                    dst = keep.tile([P, SLOTS], U32, name="slot_words%d_%d" % (g, sort), align_bytes=64)
                    slot_words[g, sort] = dst
                    window = token_words[:, sort * T : sort * T + WINDOW].bitcast(U32)
                nc.vector.tensor_copy(dst[:], window.indirect(cols))

        turned_gate = in_bank(P, "turned_gate", 7)
        nc.tensor.transpose(turned_gate[:], gate_rows[:], identity[:])
        gate_cols = keep.tile([P, TOP * BLOCKS], F32, name="gate_cols")
        nc.scalar.copy(gate_cols[:], turned_gate[:, 0 : TOP * BLOCKS])
        planes = keep.tile([P, TOP * T], F32, name="planes", align_bytes=ALIGN)
        for at in range(0, TOP * T, BANK):
            spread = in_bank(BANK, "spread%d" % at, at // BANK)
            for j in range(0, BANK, P):
                q = (at + j) // P
                nc.tensor.transpose(spread[:, j : j + P], gate_cols[:, q : q + 1].to_broadcast([P, P]), identity[:])
            nc.scalar.copy(planes[:, at : at + BANK], spread[:])

        units = []
        for first, count, chunk in early:
            for i in range(0, count, 2):
                n = min(2, count - i)
                at = ZE + 2 * (first + i) * KIB
                units.append(weave(scalar, by_pass(chunk[:, i : i + n, :, :]), whole_keys(first + i, n), at))
        for e in range(3):
            share_bank([(e, h) for h in range(HALVES)])
        for unit in units:
            multiply(unit)

        for first, last in ((9, 12), (12, 15), (15, 18), (18, 20)):
            share_bank([(e, 0) for e in range(first, last)])
        shares = (
            ((scalar, 4), (scalar, 4), (scalar, 3), (scalar, 3), (scalar, 3)),
            ((vector, 4), (vector, 4), (scalar, 4), (vector, 4)),
        )
        for g, group in enumerate(groups):
            units = []
            i = 0
            for copy, n in shares[g]:
                at = ZB + i * KIB if g == 0 and i < 8 else None
                units.append(weave(copy, by_row(group[:, :, i : i + n, :]), half_keys(0, 17 * g + i, n), at))
                i = i + n
            if g == 0:
                for unit in units:
                    multiply(unit)
        activate()
        finish(units)

        late = (
            (7, ZA, (2, 2), (2, 1)),
            (5, ZC, (2, 1), (2,)),
            (3, ZD, (2,), (1,)),
        )
        first = 9
        for count, offset, mine, theirs in late:
            chunk = load_whole(first, count, offset)
            units = []
            i = 0
            for copy, sizes in ((vector, mine), (scalar, theirs)):
                for n in sizes:
                    units.append(weave(copy, by_pass(chunk[:, i : i + n, :, :]), whole_keys(first + i, n)))
                    i = i + n
            finish(units)
            first = first + count
        for count, offset in ((2, ZD + 12 * KIB), (1, ZA)):
            chunk = load_whole(first, count, offset)
            keys = whole_keys(first, count)
            finish([weave(copy, by_pass(chunk[:, :, :, h * P : (h + 1) * P]), keys[h::HALVES]) for h, copy in enumerate((vector, scalar))])
            first = first + count

        rest = half_keys(1, 0, SPLIT * PASSES)
        sizes = (2, 5, 9, 6, 4, 3, 2, 1, 1)
        starts = [sum(sizes[:g]) for g in range(len(sizes))]
        places = [ZA + 4 * KIB + 2 * KIB * at for at in starts[:3]] + [ZC + 2 * KIB * (at - starts[3]) for at in starts[3:6]]
        places = places + [ZD + 12 * KIB + 2 * KIB * (at - starts[6]) for at in starts[6:]]
        groups = [load_group(1, at, n, offset) for at, n, offset in zip(starts, sizes, places)]

        def grouped(copy, g, i, n):
            return weave(copy, by_row(groups[g][:, :, i : i + n, :]), rest[starts[g] + i : starts[g] + i + n])

        share_bank([(e, 1) for e in range(WHOLE + 1, WHOLE + 3)])
        share_bank([(e, 1) for e in range(E - 4, E - 1)])
        finish([grouped(scalar, 0, 0, 1), grouped(vector, 0, 1, 1)])

        def picks(r, cols):
            return back[r][:, cols.start // 16 : cols.stop // 16]

        def factor(r, cols):
            return planes[:, r * T + cols.start : r * T + cols.stop]

        pieces = (slice(0, 3 * P), slice(3 * P, T))
        tokens = slice(0, T)
        wide = T * 4

        def token_banks(name, first):
            return [in_bank(cols.stop - cols.start, name + str(n), first + n) for n, cols in enumerate(pieces)]

        def add_turned(turned, part, cols, start, stop):
            for piece, bank in zip(pieces, turned):
                for at in range(max(cols.start, piece.start), min(cols.stop, piece.stop), P):
                    nc.tensor.matmul(
                        bank[:, at - piece.start : at - piece.start + P],
                        lhsT=part[:, at : at + P],
                        rhs=identity[:],
                        start=start and at == piece.start,
                        stop=stop and at == min(cols.stop, piece.stop) - P,
                        is_transpose=True,
                    )

        def turn_back(bank, by_token, cols, sums, step):
            for at in range(cols.start, cols.stop, P):
                if (at - cols.start) % step == 0:
                    nc.scalar.copy(by_token[:, at : min(at + step, cols.stop)], bank[:, at - cols.start : min(at + step, cols.stop) - cols.start])
                nc.tensor.transpose(sums[:, at - cols.start : at - cols.start + P], by_token[:, at : at + P], identity[:])

        near, far = pieces
        turned = token_banks("turned0_", 0)
        plain = {r: place([P, T], "plain0_%d" % r, ZE + n * wide) for n, r in enumerate((2, 3))}
        parts = [place([P, T], "part0_%d" % r, ZE + (2 + r) * wide) for r in range(TOP)]
        for r in plain:
            nc.scalar.activation(plain[r][:], y[0][:].indirect(picks(r, tokens)), COPY)
        unit = grouped(scalar, 1, 0, 3)
        for r, cols in ((0, tokens), (2, tokens), (1, near), (3, tokens), (1, far)):
            values = plain[r][:, cols] if r in plain else y[0][:].indirect(picks(r, cols))
            nc.vector.tensor_tensor(parts[r][:, cols], values, factor(r, cols), MULT)
            for piece in pieces:
                if cols.start <= piece.start < cols.stop:
                    add_turned(turned, parts[r], piece, r == 0, (r, piece) in ((3, near), (1, far)))
        early_unit, unit = unit, grouped(vector, 1, 3, 2)
        multiply(early_unit)
        by_token = place([P, T], "by_token0", ZE + 6 * wide)
        sums = token_banks("sums0_", 2)
        for bank, cols, back_bank in zip(turned, pieces, sums):
            turn_back(bank, by_token, cols, back_bank, T)
        finish([unit])

        shares = (((4, 1), (4,)), ((4,), (2,)), ((3,), (1,)), ((2,), (1,)), ((1,), (1,)))
        for g, (mine, theirs) in enumerate(shares, 2):
            units = []
            i = 0
            for copy, counts in ((vector, mine), (scalar, theirs)):
                for n in counts:
                    units.append(grouped(copy, g, i, n))
                    i = i + n
            activate()
            for unit in units if g == 2 else units[::-1]:
                multiply(unit)
        units = [grouped(scalar, 7, 0, 1), grouped(vector, 8, 0, 1)]
        first_total = place([P, T], "total0", places[7] - KIB // 2)
        for cols, bank in zip(pieces, sums):
            nc.scalar.copy(first_total[:, cols], bank[:])
        nc.sync.dma_start(out[0:P, :], first_total[:])
        activate()
        finish(units)

        late_room = ZE
        plain = {r: place([P, T], "plain1_%d" % r, late_room + n * wide) for n, r in enumerate((1, 2, 3))}
        parts = [place([P, T], "part1_%d" % r, late_room + (3 + r) * wide) for r in range(TOP)]
        by_token = place([P, T], "by_token1", ZD)
        total = place([P, T], "total1", ZD + wide)
        fourth, fifth = slice(3 * P, 4 * P), slice(4 * P, T)
        fetched = ((2, near), (3, near), (2, far), (3, fourth), (1, far))
        for r, cols in fetched:
            nc.scalar.activation(plain[r][:, cols], y[1][:].indirect(picks(r, cols)), COPY)

        turned = [in_bank(P, "turned1_%d" % c, c) for c in range(BLOCKS)]
        order = ((0, near), (2, near), (0, far), (3, near), (3, fifth), (2, far), (3, fourth), (1, near), (1, far))
        left = [TOP - 1] * BLOCKS
        for r, cols in order:
            values = plain[r][:, cols] if (r, cols) in fetched else y[1][:].indirect(picks(r, cols))
            nc.vector.tensor_tensor(parts[r][:, cols], values, factor(r, cols), MULT)
            for c in range(cols.start // P, cols.stop // P) if r != 1 else ():
                nc.tensor.matmul(
                    turned[c][:],
                    lhsT=parts[r][:, c * P : (c + 1) * P],
                    rhs=identity[:],
                    start=left[c] == TOP - 1,
                    stop=left[c] == 1,
                    is_transpose=True,
                )
                left[c : c + 1] = [left[c] - 1]
        sums = token_banks("sums1_", 5)
        for c in (0, 1, 2, 4, 3):
            cols = slice(c * P, (c + 1) * P)
            n = 0 if c * P < far.start else 1
            nc.scalar.copy(by_token[:, cols], turned[c][:])
            at = c * P - pieces[n].start
            nc.tensor.transpose(sums[n][:, at : at + P], by_token[:, cols], identity[:])
        for cols, bank in zip(pieces, sums):
            nc.vector.tensor_tensor(total[:, cols], bank[:], parts[1][:, cols], ADD)
            nc.sync.dma_start(out[P:N, cols], total[:, cols])
